import numpy as np
import ml_dtypes


def mxq(x, axis, fmt="e4m3"):
    dtype, down = {"e4m3": (ml_dtypes.float8_e4m3fn, 7), "e5m2": (ml_dtypes.float8_e5m2, 14)}[fmt]
    v = np.moveaxis(np.asarray(x, np.float32).astype(ml_dtypes.bfloat16).astype(np.float64), axis, -1)
    blocks = v.reshape(v.shape[:-1] + (-1, 32))
    amax = np.abs(blocks).max(-1, keepdims=True)
    byte = np.maximum(np.where(amax > 0, np.frexp(amax)[1] - 1 + 127, 0) - down, 1)
    scale = np.exp2(byte - 127.0)
    codes = (blocks / scale).astype(np.float32).astype(dtype).astype(np.float64)
    return np.moveaxis((codes * scale).reshape(v.shape), -1, axis)


WIDE = False


def mx_kscale(k):
    if not WIDE:
        return np.ones(k)
    levels = np.array([10, -10, 5, -5, 0])
    if k % 512:
        return np.exp2(np.random.permutation(np.resize(levels, k // 32))).repeat(32)
    a = np.empty((k // 512, 16))
    for p in range(k // 512):
        a[p, :8] = np.random.permutation(np.resize(levels, 8))
        for g in range(8):
            far = levels[np.abs(levels - a[p, g]) >= 10]
            a[p, g + 8] = far[np.random.randint(len(far))]
    return np.exp2(a.ravel()).repeat(32)


def f64(x):
    return np.asarray(x).astype(np.float64)


def striped(idx):
    return np.tile(idx.reshape(-1, 16).T, (8, 1)).astype(np.uint16)


def unstriped(offs):
    return offs[:16].T.reshape(-1).astype(np.int64)


E2M1 = np.array([0.0, 0.5, 1.0, 1.5, 2.0, 3.0, 4.0, 6.0, -0.0, -0.5, -1.0, -1.5, -2.0, -3.0, -4.0, -6.0])


def pack_weight(w, fmt):
    k, n = w.shape
    w = f64(np.asarray(w, np.float32).astype(ml_dtypes.bfloat16)).reshape(k // 32, 32, n)
    amax = np.abs(w).max(1)
    if fmt == "e4m3":
        byte = np.frexp(amax)[1] - 1 + 127 - 7
    else:
        mant, ex = np.frexp(amax / 6.0)
        byte = np.where(mant > 0.5, ex, ex - 1) + 127
    byte = np.clip(np.where(amax > 0, byte, 1), 1, 254)
    scaled = (w * np.exp2(127.0 - byte)[:, None, :]).reshape(k, n).astype(np.float32)
    by_word = np.ascontiguousarray(scaled.reshape(k // 512, 128, 4, n).transpose(0, 1, 3, 2))
    if fmt == "e4m3":
        words = by_word.astype(ml_dtypes.float8_e4m3fn).view(np.uint8)
    else:
        c = by_word.astype(ml_dtypes.float4_e2m1fn).view(np.uint8) & 0xF
        words = (c[..., 0::2] | (c[..., 1::2] << 4)).reshape(k // 512, 128, 2 * n)
    return np.ascontiguousarray(words), np.ascontiguousarray(byte.astype(np.uint8).reshape(k // 512, 16, n))


def unpack_weight(words, scales, fmt):
    g, _, n = scales.shape
    words = np.ascontiguousarray(words).reshape(g, 128, n, -1)
    if fmt == "e4m3":
        vals = words.view(ml_dtypes.float8_e4m3fn).astype(np.float64)
    else:
        nib = np.empty((g, 128, n, 4), np.uint8)
        nib[..., 0::2] = words & 0xF
        nib[..., 1::2] = words >> 4
        vals = E2M1[nib]
    vals = vals * np.repeat(np.exp2(scales.astype(np.float64) - 127.0), 8, axis=1)[..., None]
    return vals.transpose(0, 1, 3, 2).reshape(g * 512, n)


K, T, E, C, N = 512, 512, 4, 256, 512


def by_expert(wq, xq):
    return np.concatenate([wq[e].T @ xq[:, e * C:(e + 1) * C] for e in range(E)], axis=1)


def setup_inputs():
    n = np.random.standard_normal
    v = mx_kscale(N)
    first = np.random.permutation(np.repeat(np.arange(E), T // E))
    second = (first + 1 + np.random.permutation(np.repeat(np.arange(E - 1), -(-T // (E - 1)))[:T])) % E
    while np.bincount(second, minlength=E).max() != T // E:
        load = np.bincount(second, minlength=E); hi, lo = int(load.argmax()), int(load.argmin())
        t = np.flatnonzero((second == hi) & (first != lo))[0]; second[t] = lo
    slot_token = np.empty(E * C, np.int64); pos = np.empty((2, T), np.int64); fill = np.zeros(E, np.int64)
    place = np.stack([np.random.permutation(C) for _ in range(E)])
    for r, deal in enumerate((first, second)):
        for t in np.random.permutation(T):
            e = deal[t]; j = e * C + place[e, fill[e]]; fill[e] += 1; slot_token[j] = t; pos[r, t] = j
    g = np.random.uniform(0.2, 0.8, T)
    w_slot = np.empty(E * C); w_slot[pos[0]] = g; w_slot[pos[1]] = 1.0 - g
    dq = pack_weight(n((N, T)) * v[:, None], "e4m3")
    dk = pack_weight(n((N, T)) * v[:, None], "e4m3")
    dv = pack_weight(n((N, T)) * v[:, None], "e4m3")
    wk = [pack_weight(m, "e2m1") for m in n((E, N, K)) / np.sqrt(N) / v[None, :, None]]
    wv = [pack_weight(m, "e4m3") for m in n((E, N, K)) / np.sqrt(N) / v[None, :, None]]
    return {
        "dq_words": dq[0],
        "dq_scales": dq[1],
        "dk_words": dk[0],
        "dk_scales": dk[1],
        "dv_words": dv[0],
        "dv_scales": dv[1],
        "wq": (n((E, N, K)) / np.sqrt(N) / v[None, :, None]).astype(np.float32),
        "wk_words": np.stack([m[0] for m in wk]),
        "wk_scales": np.stack([m[1] for m in wk]),
        "wv_words": np.stack([m[0] for m in wv]),
        "wv_scales": np.stack([m[1] for m in wv]),
        "gate": (np.tile(w_slot, (128, 1))).astype(np.float32),
        "offs": striped(slot_token),
        "pos1": striped(pos[0]),
        "pos2": striped(pos[1]),
    }


def reference(dq_words, dq_scales, dk_words, dk_scales, dv_words, dv_scales, wq, wk_words, wk_scales, wv_words, wv_scales, gate, offs, pos1, pos2):
    wqq = mxq(f64(wq), 1, "e4m3")
    wk = np.stack([unpack_weight(wk_words[e], wk_scales[e], "e2m1") for e in range(E)])
    wv = np.stack([unpack_weight(wv_words[e], wv_scales[e], "e4m3") for e in range(E)])
    idx = unstriped(offs)
    gq, gk, gv = [unpack_weight(w, s, "e4m3")[:, idx] for w, s in ((dq_words, dq_scales), (dk_words, dk_scales), (dv_words, dv_scales))]
    dx = f64(gate[:1]) * (by_expert(wqq, gq) + by_expert(wk, gk) + by_expert(wv, gv))
    out = dx[:, unstriped(pos1)] + dx[:, unstriped(pos2)]
    return out

@@ -1,0 +1,248 @@
+from contextlib import ExitStack
+
+import concourse.mybir as mybir
+from concourse.masks import make_identity
+
+K, T, E, C, N = 512, 512, 4, 256, 512
+S = E * C
+FLOPS = 2 * 3 * N * K * S
+
+F32 = mybir.dt.float32
+BF16 = mybir.dt.bfloat16
+I32 = mybir.dt.int32
+U32 = mybir.dt.uint32
+U16 = mybir.dt.uint16
+U8 = mybir.dt.uint8
+FP8X4 = mybir.dt.float8_e4m3fn_x4
+FP4X4 = mybir.dt.float4_e2m1fn_x4
+COPY = mybir.ActivationFunctionType.Copy
+MULT = mybir.AluOpType.mult
+ADD = mybir.AluOpType.add
+
+P = 128
+CT = K // P
+LAST = E - 1
+HALF = K // 2
+SLOT_ROW = (8, 0, 4)
+WEIGHT_ROW = (0, 0, 4)
+
+
+def tile_moe_qkb_kernel(
+    tc, dq_words, dq_scales, dk_words, dk_scales, dv_words, dv_scales, wq,
+    wk_words, wk_scales, wv_words, wv_scales, gate, offs, pos1, pos2, out,
+):
+    nc = tc.nc
+    with ExitStack() as ctx:
+        keep = ctx.enter_context(tc.tile_pool(name="keep", bufs=1))
+        mm = ctx.enter_context(tc.psum_pool(name="mm", bufs=4))
+        tr = ctx.enter_context(tc.psum_pool(name="tr", bufs=3))
+
+        def sb(shape, dtype, name):
+            return keep.tile(shape, dtype, name=name, align_bytes=64)
+
+        offs_t = keep.tile([P, S // 16], U16, name="offs_t")
+        pos_t = [keep.tile([P, T // 16], U16, name="pos%d" % i) for i in range(2)]
+        names = ("q", "k", "v")
+        g_words_in = (dq_words, dk_words, dv_words)
+        g_scales_in = (dq_scales, dk_scales, dv_scales)
+        gw = [sb([P, T], U32, "gw_" + n) for n in names]
+        gs = [sb([P, T], U8, "gs_" + n) for n in names]
+        sw = [[sb([P, C], U32, "sw_%s%d" % (n, e)) for e in range(E)] for n in names]
+        ss = [[sb([P, C], U8, "ss_%s%d" % (n, e)) for e in range(E)] for n in names]
+        wks = sb([P, E, K], U8, "wks")
+        wvs = sb([P, E, K], U8, "wvs")
+        wkw = [sb([P, 2, 2 * K], U8, "wkw%d" % h) for h in range(2)]
+        wvw = [sb([P, K], U32, "wvw%d" % e) for e in range(E)]
+        raw = [sb([P, 4, K], F32, "raw%d" % e) for e in range(LAST)]
+        raw_last = [sb([P, 4, HALF], F32, "raw_last%d" % h) for h in range(2)]
+        grouped = [sb([P, K, 4], BF16, "grp%d" % e) for e in range(E)]
+        wqw = [sb([P, K], U32, "wqw%d" % e) for e in range(E)]
+        wqs = [sb([P, K], U8, "wqs%d" % e) for e in range(E)]
+        gate_rows = sb([P, P], F32, "gate_rows")
+        gate_col = sb([P, S // P], F32, "gate_col")
+        gate_last = sb([P, C], F32, "gate_last")
+        ident0 = sb([P, P], F32, "ident0")
+        ident = sb([P, P], F32, "ident")
+        by_slot = [sb([P, K], F32, "by_slot%d" % s) for s in range(2 * LAST)]
+        dx = [sb([P, S], F32, "dx%d" % ct) for ct in range(CT)]
+        got = [[sb([P, T], F32, "got%d_%d" % (ct, i)) for i in range(2)] for ct in range(CT)]
+        res = [sb([P, T], F32, "res%d" % ct) for ct in range(CT)]
+
+        for j in range(3):
+            nc.gpsimd.memset(gs[j][:].bitcast(I32), 0)
+        nc.vector.memset(wks[:].bitcast(I32), 0)
+        nc.vector.memset(wvs[:].bitcast(I32), 0)
+
+        def load_words(j):
+            nc.sync.dma_start(gw[j][:].bitcast(I32), g_words_in[j][0].rearrange("p t d -> p (t d)").bitcast(I32))
+
+        def load_scales(j, r):
+            rows = g_scales_in[j][0].rearrange("(q r) t -> r q t", r=4)
+            nc.sync.dma_start(gs[j][SLOT_ROW[j] + r:P:32, :].bitcast(I32), rows[r].bitcast(I32))
+
+        def load_weight_scales(j, queue):
+            plane, src = (wks, wk_scales) if j == 1 else (wvs, wv_scales)
+            rows = src.rearrange("e s (q r) c -> r q (e s) c", r=4)
+            for r in range(4):
+                queue.dma_start(plane[WEIGHT_ROW[j] + r:P:32, :, :].bitcast(I32), rows[r].bitcast(I32))
+
+        def wq_rows(e):
+            return wq[e].rearrange("(p j) c -> p j c", j=4)
+
+        def load_wk(h):
+            kw = wk_words.rearrange("e s p b -> p (e s) b")[:, 2 * h:2 * h + 2, :]
+            nc.sync.dma_start(wkw[h][:].bitcast(I32), kw.bitcast(I32))
+
+        def load_wv(e):
+            nc.sync.dma_start(wvw[e][:].bitcast(I32), wv_words[e, 0].rearrange("p c d -> p (c d)").bitcast(I32))
+
+        load_weight_scales(1, nc.gpsimd)
+        make_identity(nc, ident0[:])
+        nc.scalar.copy(ident[:], ident0[:])
+        nc.sync.dma_start(offs_t[:], offs)
+        load_words(0)
+        nc.sync.dma_start(raw[0][:], wq_rows(0))
+        load_words(1)
+        for r in range(4):
+            load_scales(0, r)
+        load_words(2)
+        for r in range(2):
+            load_scales(1, r)
+        nc.sync.dma_start(raw[1][:], wq_rows(1))
+        for r in range(2, 4):
+            load_scales(1, r)
+        for r in range(4):
+            load_scales(2, r)
+        nc.sync.dma_start(raw[2][:], wq_rows(2))
+        load_weight_scales(2, nc.sync)
+        load_wk(0)
+        load_wv(0)
+        nc.sync.dma_start(gate_rows[:], gate.rearrange("a (s p) -> (a s) p", p=P)[0:P, :])
+        load_wv(1)
+        nc.sync.dma_start(raw_last[0][:], wq_rows(LAST)[:, :, 0:HALF])
+        load_wk(1)
+        load_wv(2)
+        load_wv(3)
+        nc.sync.dma_start(gate_last[:], gate[:, LAST * C:S])
+        nc.sync.dma_start(pos_t[0][:], pos1)
+        nc.sync.dma_start(pos_t[1][:], pos2)
+        nc.sync.dma_start(raw_last[1][:], wq_rows(LAST)[:, :, HALF:K])
+
+        def gather_words(j, e):
+            nc.vector.tensor_copy(sw[j][e][:], gw[j][:].indirect(offs_t[:, e * C // 16:(e + 1) * C // 16]))
+
+        def gather_scales(j, e):
+            nc.vector.tensor_copy(ss[j][e][:], gs[j][:].indirect(offs_t[:, e * C // 16:(e + 1) * C // 16]))
+
+        def cast(e, src, c0, c1, s0):
+            w = c1 - c0
+            nc.scalar.copy(
+                grouped[e][:, c0:c1, :].rearrange("p (c i) j -> p c j i", i=4),
+                src[:, :, s0:s0 + w].rearrange("p j (c i) -> p c j i", i=4),
+            )
+
+        def quantize(e, c0, c1):
+            nc.vector.quantize_mx(
+                out=wqw[e][:, c0:c1].bitcast(FP8X4),
+                scales=wqs[e][:, c0:c1],
+                in_=grouped[e][:, c0:c1, :].rearrange("p c j -> p (c j)"),
+            )
+
+        def weights(j, e, c0, c1):
+            if j == 0:
+                return wqw[e][:, c0:c1].bitcast(FP8X4), wqs[e][:, c0:c1]
+            if j == 1:
+                return wkw[e // 2][:, e % 2, 2 * c0:2 * c1].bitcast(FP4X4), wks[:, e, c0:c1]
+            return wvw[e][:, c0:c1].bitcast(FP8X4), wvs[WEIGHT_ROW[2]:P, e, c0:c1]
+
+        def slots(j, e, u0, u1):
+            return sw[j][e][:, u0:u1].bitcast(FP8X4), ss[j][e][SLOT_ROW[j]:P, u0:u1]
+
+        def product_by_slot(e, h):
+            acc = mm.tile([P, K], F32, name="acc")
+            for n, j in enumerate((1, 2, 0)):
+                a, a_s = slots(j, e, h * P, (h + 1) * P)
+                b, b_s = weights(j, e, 0, K)
+                nc.tensor.matmul_mx(out=acc[:], lhsT=a, lhsT_scale=a_s, rhs=b, rhs_scale=b_s,
+                                    start=(n == 0), stop=(n == 2))
+            s = 2 * e + h
+            nc.scalar.activation(by_slot[s][:], acc[:], COPY, scale=gate_col[:, s:s + 1])
+
+        def turn(ct, s0, s1):
+            bank = tr.tile([P, K], F32, name="bank")
+            for s in range(s0, s1):
+                nc.tensor.transpose(bank[:, (s - s0) * P:(s - s0 + 1) * P], by_slot[s][:, ct * P:(ct + 1) * P], ident[:])
+            nc.scalar.copy(dx[ct][:, s0 * P:s1 * P], bank[:, 0:(s1 - s0) * P])
+
+        def product_by_feature(ct):
+            acc = mm.tile([P, K], F32, name="acc")
+            passes = ((0, 0, C), (1, 0, P), (1, P, C), (2, 0, C))
+            for n, (j, u0, u1) in enumerate(passes):
+                a, a_s = weights(j, LAST, ct * P, (ct + 1) * P)
+                b, b_s = slots(j, LAST, u0, u1)
+                nc.tensor.matmul_mx(out=acc[:, u0:u1], lhsT=a, lhsT_scale=a_s, rhs=b, rhs_scale=b_s,
+                                    start=(n == 0), stop=(n == len(passes) - 1))
+            return acc
+
+        def gate_last_expert(ct, acc):
+            nc.vector.tensor_tensor(dx[ct][:, LAST * C:S], acc[:, 0:C], gate_last[:], MULT)
+
+        def fetch(ct, i, t0, t1):
+            nc.vector.tensor_copy(got[ct][i][:, t0:t1], dx[ct][:].indirect(pos_t[i][:, t0 // 16:t1 // 16]))
+
+        def finish(ct, t0, t1, eng):
+            eng.tensor_tensor(res[ct][:, t0:t1], got[ct][0][:, t0:t1], got[ct][1][:, t0:t1], ADD)
+            nc.sync.dma_start(out[ct * P:(ct + 1) * P, t0:t1], res[ct][:, t0:t1])
+
+        gate_bank = tr.tile([P, K], F32, name="bank")
+        nc.tensor.transpose(gate_bank[:, 0:P], gate_rows[:], ident[:])
+        nc.scalar.copy(gate_col[:], gate_bank[:, 0:S // P])
+
+        for j in range(2):
+            for e in range(E):
+                gather_words(j, e)
+        for e in range(LAST):
+            cast(e, raw[e], 0, K, 0)
+        for e in range(LAST):
+            gather_words(2, e)
+            for j in range(3):
+                gather_scales(j, e)
+            quantize(e, 0, K)
+            for h in range(2):
+                product_by_slot(e, h)
+            if e == 0:
+                cast(LAST, raw_last[0], 0, HALF, 0)
+            if e == 1:
+                turn(0, 0, 4)
+        turn(0, 4, 6)
+        gather_scales(0, LAST)
+        gather_scales(1, LAST)
+        quantize(LAST, 0, HALF)
+        gather_words(2, LAST)
+        gather_scales(2, LAST)
+        accs = [product_by_feature(ct) for ct in range(2)]
+        turn(1, 0, 4)
+        turn(1, 4, 6)
+        cast(LAST, raw_last[1], HALF, K, 0)
+        gate_last_expert(0, accs[0])
+        gate_last_expert(1, accs[1])
+        fetch(0, 0, 0, T)
+        fetch(0, 1, 0, T)
+        quantize(LAST, HALF, K)
+        accs += [product_by_feature(ct) for ct in range(2, CT)]
+        for ct in range(2, CT):
+            turn(ct, 0, 4)
+            turn(ct, 4, 6)
+        finish(0, 0, T, nc.gpsimd)
+        for ct in range(1, CT - 1):
+            fetch(ct, 0, 0, T)
+            gate_last_expert(ct + 1, accs[ct + 1])
+            fetch(ct, 1, 0, T)
+            finish(ct, 0, T, nc.gpsimd)
+        ct = CT - 1
+        fetch(ct, 0, 0, T // 2)
+        fetch(ct, 1, 0, T // 2)
+        finish(ct, 0, T // 2, nc.gpsimd)
+        fetch(ct, 0, T // 2, T)
+        fetch(ct, 1, T // 2, T)
+        finish(ct, T // 2, T, nc.vector)

@@ -23,7 +23,7 @@ P = 128
 CT = K // P
 LAST = E - 1
 HALF = K // 2
-SLOT_ROW = (8, 0, 4)
+SLOT_ROW = (0, 0, 0)
 WEIGHT_ROW = (0, 0, 4)
 
 
@@ -34,7 +34,7 @@ def tile_moe_qkb_kernel(
     nc = tc.nc
     with ExitStack() as ctx:
         keep = ctx.enter_context(tc.tile_pool(name="keep", bufs=1))
-        mm = ctx.enter_context(tc.psum_pool(name="mm", bufs=4))
+        mm = ctx.enter_context(tc.psum_pool(name="mm", bufs=5))
         tr = ctx.enter_context(tc.psum_pool(name="tr", bufs=3))
 
         def sb(shape, dtype, name):
@@ -45,46 +45,48 @@ def tile_moe_qkb_kernel(
         names = ("q", "k", "v")
         g_words_in = (dq_words, dk_words, dv_words)
         g_scales_in = (dq_scales, dk_scales, dv_scales)
-        gw = [sb([P, T], U32, "gw_" + n) for n in names]
-        gs = [sb([P, T], U8, "gs_" + n) for n in names]
-        sw = [[sb([P, C], U32, "sw_%s%d" % (n, e)) for e in range(E)] for n in names]
-        ss = [[sb([P, C], U8, "ss_%s%d" % (n, e)) for e in range(E)] for n in names]
+        width = (2 * T, 2 * T, T)
+        gw = [sb([P, width[j]], U32, "gw_" + n) for j, n in enumerate(names)]
+        gs = [sb([P, width[j]], U8, "gs_" + n) for j, n in enumerate(names)]
+        runs = (((0, LAST), (LAST, E)), ((0, LAST), (LAST, E)), tuple((e, e + 1) for e in range(E)))
+        sw = [{r: sb([P, (r[1] - r[0]) * C], U32, "sw_%s%d" % (n, r[0])) for r in runs[j]} for j, n in enumerate(names)]
+        ss = [{r: sb([P, (r[1] - r[0]) * C], U8, "ss_%s%d" % (n, r[0])) for r in runs[j]} for j, n in enumerate(names)]
         wks = sb([P, E, K], U8, "wks")
         wvs = sb([P, E, K], U8, "wvs")
         wkw = [sb([P, 2, 2 * K], U8, "wkw%d" % h) for h in range(2)]
         wvw = [sb([P, K], U32, "wvw%d" % e) for e in range(E)]
-        raw = [sb([P, 4, K], F32, "raw%d" % e) for e in range(LAST)]
-        raw_last = [sb([P, 4, HALF], F32, "raw_last%d" % h) for h in range(2)]
+        raw = [sb([P, 4, K], F32, "raw%d" % e) for e in range(E)]
         grouped = [sb([P, K, 4], BF16, "grp%d" % e) for e in range(E)]
         wqw = [sb([P, K], U32, "wqw%d" % e) for e in range(E)]
         wqs = [sb([P, K], U8, "wqs%d" % e) for e in range(E)]
         gate_rows = sb([P, P], F32, "gate_rows")
         gate_col = sb([P, S // P], F32, "gate_col")
         gate_last = sb([P, C], F32, "gate_last")
-        ident0 = sb([P, P], F32, "ident0")
         ident = sb([P, P], F32, "ident")
         by_slot = [sb([P, K], F32, "by_slot%d" % s) for s in range(2 * LAST)]
         dx = [sb([P, S], F32, "dx%d" % ct) for ct in range(CT)]
         got = [[sb([P, T], F32, "got%d_%d" % (ct, i)) for i in range(2)] for ct in range(CT)]
         res = [sb([P, T], F32, "res%d" % ct) for ct in range(CT)]
 
-        for j in range(3):
-            nc.gpsimd.memset(gs[j][:].bitcast(I32), 0)
+        make_identity(nc, ident[:])
         nc.vector.memset(wks[:].bitcast(I32), 0)
         nc.vector.memset(wvs[:].bitcast(I32), 0)
+        for j in range(2):
+            nc.vector.memset(gw[j][:, T:2 * T].bitcast(I32), 0)
+            nc.vector.memset(gs[j][:, T:2 * T].bitcast(I32), 0)
 
         def load_words(j):
-            nc.sync.dma_start(gw[j][:].bitcast(I32), g_words_in[j][0].rearrange("p t d -> p (t d)").bitcast(I32))
+            nc.sync.dma_start(gw[j][:, 0:T].bitcast(I32), g_words_in[j][0].rearrange("p t d -> p (t d)").bitcast(I32))
 
-        def load_scales(j, r):
-            rows = g_scales_in[j][0].rearrange("(q r) t -> r q t", r=4)
-            nc.sync.dma_start(gs[j][SLOT_ROW[j] + r:P:32, :].bitcast(I32), rows[r].bitcast(I32))
+        def load_scales(j, q):
+            rows = g_scales_in[j][0][4 * q:4 * q + 4, :].bitcast(I32)
+            nc.sync.dma_start(gs[j][32 * q:32 * q + 32, 0:T].bitcast(I32), rows.unsqueeze(0).to_broadcast([8, 4, T // 4]))
 
-        def load_weight_scales(j, queue):
+        def load_weight_scales(j, r0, r1):
             plane, src = (wks, wk_scales) if j == 1 else (wvs, wv_scales)
             rows = src.rearrange("e s (q r) c -> r q (e s) c", r=4)
-            for r in range(4):
-                queue.dma_start(plane[WEIGHT_ROW[j] + r:P:32, :, :].bitcast(I32), rows[r].bitcast(I32))
+            for r in range(r0, r1):
+                nc.gpsimd.dma_start(plane[WEIGHT_ROW[j] + r:P:32, :, :].bitcast(I32), rows[r].bitcast(I32))
 
         def wq_rows(e):
             return wq[e].rearrange("(p j) c -> p j c", j=4)
@@ -96,43 +98,43 @@ def tile_moe_qkb_kernel(
         def load_wv(e):
             nc.sync.dma_start(wvw[e][:].bitcast(I32), wv_words[e, 0].rearrange("p c d -> p (c d)").bitcast(I32))
 
-        load_weight_scales(1, nc.gpsimd)
-        make_identity(nc, ident0[:])
-        nc.scalar.copy(ident[:], ident0[:])
-        nc.sync.dma_start(offs_t[:], offs)
+        load_weight_scales(1, 0, 4)
+        load_weight_scales(2, 0, 4)
         load_words(0)
-        nc.sync.dma_start(raw[0][:], wq_rows(0))
+        nc.sync.dma_start(offs_t[:], offs)
         load_words(1)
-        for r in range(4):
-            load_scales(0, r)
-        load_words(2)
-        for r in range(2):
-            load_scales(1, r)
+        nc.sync.dma_start(raw[0][:], wq_rows(0))
+        for q in range(4):
+            load_scales(0, q)
         nc.sync.dma_start(raw[1][:], wq_rows(1))
-        for r in range(2, 4):
-            load_scales(1, r)
-        for r in range(4):
-            load_scales(2, r)
+        nc.sync.dma_start(gate_rows[:], gate.rearrange("a (s p) -> (a s) p", p=P)[0:P, :])
+        for q in range(4):
+            load_scales(1, q)
+        load_words(2)
         nc.sync.dma_start(raw[2][:], wq_rows(2))
-        load_weight_scales(2, nc.sync)
+        for q in range(4):
+            load_scales(2, q)
+        nc.sync.dma_start(raw[3][:], wq_rows(3))
         load_wk(0)
         load_wv(0)
-        nc.sync.dma_start(gate_rows[:], gate.rearrange("a (s p) -> (a s) p", p=P)[0:P, :])
         load_wv(1)
-        nc.sync.dma_start(raw_last[0][:], wq_rows(LAST)[:, :, 0:HALF])
         load_wk(1)
         load_wv(2)
         load_wv(3)
         nc.sync.dma_start(gate_last[:], gate[:, LAST * C:S])
         nc.sync.dma_start(pos_t[0][:], pos1)
         nc.sync.dma_start(pos_t[1][:], pos2)
-        nc.sync.dma_start(raw_last[1][:], wq_rows(LAST)[:, :, HALF:K])
+
+        def run_of(j, e):
+            return [r for r in runs[j] if r[0] <= e < r[1]][0]
 
         def gather_words(j, e):
-            nc.vector.tensor_copy(sw[j][e][:], gw[j][:].indirect(offs_t[:, e * C // 16:(e + 1) * C // 16]))
+            r = run_of(j, e)
+            nc.vector.tensor_copy(sw[j][r][:], gw[j][:].indirect(offs_t[:, r[0] * C // 16:r[1] * C // 16]))
 
         def gather_scales(j, e):
-            nc.vector.tensor_copy(ss[j][e][:], gs[j][:].indirect(offs_t[:, e * C // 16:(e + 1) * C // 16]))
+            r = run_of(j, e)
+            nc.vector.tensor_copy(ss[j][r][:], gs[j][:].indirect(offs_t[:, r[0] * C // 16:r[1] * C // 16]))
 
         def cast(e, src, c0, c1, s0):
             w = c1 - c0
@@ -156,11 +158,13 @@ def tile_moe_qkb_kernel(
             return wvw[e][:, c0:c1].bitcast(FP8X4), wvs[WEIGHT_ROW[2]:P, e, c0:c1]
 
         def slots(j, e, u0, u1):
-            return sw[j][e][:, u0:u1].bitcast(FP8X4), ss[j][e][SLOT_ROW[j]:P, u0:u1]
+            r = run_of(j, e)
+            base = (e - r[0]) * C
+            return sw[j][r][:, base + u0:base + u1].bitcast(FP8X4), ss[j][r][SLOT_ROW[j]:P, base + u0:base + u1]
 
         def product_by_slot(e, h):
             acc = mm.tile([P, K], F32, name="acc")
-            for n, j in enumerate((1, 2, 0)):
+            for n, j in enumerate((1, 0, 2)):
                 a, a_s = slots(j, e, h * P, (h + 1) * P)
                 b, b_s = weights(j, e, 0, K)
                 nc.tensor.matmul_mx(out=acc[:], lhsT=a, lhsT_scale=a_s, rhs=b, rhs_scale=b_s,
@@ -194,55 +198,50 @@ def tile_moe_qkb_kernel(
             eng.tensor_tensor(res[ct][:, t0:t1], got[ct][0][:, t0:t1], got[ct][1][:, t0:t1], ADD)
             nc.sync.dma_start(out[ct * P:(ct + 1) * P, t0:t1], res[ct][:, t0:t1])
 
+        for j in range(2):
+            gather_words(j, 0)
+        for j in range(2):
+            gather_scales(j, 0)
+        for e in range(E):
+            cast(e, raw[e], 0, K, 0)
         gate_bank = tr.tile([P, K], F32, name="bank")
         nc.tensor.transpose(gate_bank[:, 0:P], gate_rows[:], ident[:])
         nc.scalar.copy(gate_col[:], gate_bank[:, 0:S // P])
 
-        for j in range(2):
-            for e in range(E):
-                gather_words(j, e)
         for e in range(LAST):
-            cast(e, raw[e], 0, K, 0)
-        for e in range(LAST):
-            gather_words(2, e)
-            for j in range(3):
-                gather_scales(j, e)
             quantize(e, 0, K)
+            gather_words(2, e)
+            gather_scales(2, e)
             for h in range(2):
                 product_by_slot(e, h)
-            if e == 0:
-                cast(LAST, raw_last[0], 0, HALF, 0)
             if e == 1:
                 turn(0, 0, 4)
         turn(0, 4, 6)
-        gather_scales(0, LAST)
-        gather_scales(1, LAST)
-        quantize(LAST, 0, HALF)
+        for j in range(2):
+            gather_words(j, LAST)
+            gather_scales(j, LAST)
+        quantize(LAST, 0, K)
         gather_words(2, LAST)
         gather_scales(2, LAST)
-        accs = [product_by_feature(ct) for ct in range(2)]
+        accs = [product_by_feature(ct) for ct in range(CT)]
         turn(1, 0, 4)
         turn(1, 4, 6)
-        cast(LAST, raw_last[1], HALF, K, 0)
         gate_last_expert(0, accs[0])
         gate_last_expert(1, accs[1])
         fetch(0, 0, 0, T)
         fetch(0, 1, 0, T)
-        quantize(LAST, HALF, K)
-        accs += [product_by_feature(ct) for ct in range(2, CT)]
         for ct in range(2, CT):
             turn(ct, 0, 4)
             turn(ct, 4, 6)
-        finish(0, 0, T, nc.gpsimd)
         for ct in range(1, CT - 1):
             fetch(ct, 0, 0, T)
+            finish(ct - 1, 0, T, nc.vector)
             gate_last_expert(ct + 1, accs[ct + 1])
             fetch(ct, 1, 0, T)
-            finish(ct, 0, T, nc.gpsimd)
         ct = CT - 1
-        fetch(ct, 0, 0, T // 2)
+        fetch(ct, 0, 0, T)
+        finish(ct - 1, 0, T, nc.vector)
         fetch(ct, 1, 0, T // 2)
-        finish(ct, 0, T // 2, nc.gpsimd)
-        fetch(ct, 0, T // 2, T)
         fetch(ct, 1, T // 2, T)
+        finish(ct, 0, T // 2, nc.vector)
         finish(ct, T // 2, T, nc.vector)

@@ -34,8 +34,8 @@ def tile_moe_qkb_kernel(
     nc = tc.nc
     with ExitStack() as ctx:
         keep = ctx.enter_context(tc.tile_pool(name="keep", bufs=1))
-        mm = ctx.enter_context(tc.psum_pool(name="mm", bufs=5))
-        tr = ctx.enter_context(tc.psum_pool(name="tr", bufs=3))
+        mm = ctx.enter_context(tc.psum_pool(name="mm", bufs=4))
+        tr = ctx.enter_context(tc.psum_pool(name="tr", bufs=4))
 
         def sb(shape, dtype, name):
             return keep.tile(shape, dtype, name=name, align_bytes=64)
@@ -60,7 +60,7 @@ def tile_moe_qkb_kernel(
         wqw = [sb([P, K], U32, "wqw%d" % e) for e in range(E)]
         wqs = [sb([P, K], U8, "wqs%d" % e) for e in range(E)]
         gate_rows = sb([P, P], F32, "gate_rows")
-        gate_col = sb([P, S // P], F32, "gate_col")
+        gate_col = sb([P, 2 * LAST], F32, "gate_col")
         gate_last = sb([P, C], F32, "gate_last")
         ident = sb([P, P], F32, "ident")
         by_slot = [sb([P, K], F32, "by_slot%d" % s) for s in range(2 * LAST)]
@@ -69,11 +69,6 @@ def tile_moe_qkb_kernel(
         res = [sb([P, T], F32, "res%d" % ct) for ct in range(CT)]
 
         make_identity(nc, ident[:])
-        nc.vector.memset(wks[:].bitcast(I32), 0)
-        nc.vector.memset(wvs[:].bitcast(I32), 0)
-        for j in range(2):
-            nc.vector.memset(gw[j][:, T:2 * T].bitcast(I32), 0)
-            nc.vector.memset(gs[j][:, T:2 * T].bitcast(I32), 0)
 
         def load_words(j):
             nc.sync.dma_start(gw[j][:, 0:T].bitcast(I32), g_words_in[j][0].rearrange("p t d -> p (t d)").bitcast(I32))
@@ -86,7 +81,7 @@ def tile_moe_qkb_kernel(
             plane, src = (wks, wk_scales) if j == 1 else (wvs, wv_scales)
             rows = src.rearrange("e s (q r) c -> r q (e s) c", r=4)
             for r in range(r0, r1):
-                nc.gpsimd.dma_start(plane[WEIGHT_ROW[j] + r:P:32, :, :].bitcast(I32), rows[r].bitcast(I32))
+                nc.sync.dma_start(plane[WEIGHT_ROW[j] + r:P:32, :, :].bitcast(I32), rows[r].bitcast(I32))
 
         def wq_rows(e):
             return wq[e].rearrange("(p j) c -> p j c", j=4)
@@ -98,8 +93,6 @@ def tile_moe_qkb_kernel(
         def load_wv(e):
             nc.sync.dma_start(wvw[e][:].bitcast(I32), wv_words[e, 0].rearrange("p c d -> p (c d)").bitcast(I32))
 
-        load_weight_scales(1, 0, 4)
-        load_weight_scales(2, 0, 4)
         load_words(0)
         nc.sync.dma_start(offs_t[:], offs)
         load_words(1)
@@ -114,9 +107,13 @@ def tile_moe_qkb_kernel(
         nc.sync.dma_start(raw[2][:], wq_rows(2))
         for q in range(4):
             load_scales(2, q)
+        load_weight_scales(1, 0, 2)
         nc.sync.dma_start(raw[3][:], wq_rows(3))
+        load_weight_scales(1, 2, 4)
+        load_weight_scales(2, 0, 2)
         load_wk(0)
         load_wv(0)
+        load_weight_scales(2, 2, 4)
         load_wv(1)
         load_wk(1)
         load_wv(2)
@@ -164,7 +161,7 @@ def tile_moe_qkb_kernel(
 
         def product_by_slot(e, h):
             acc = mm.tile([P, K], F32, name="acc")
-            for n, j in enumerate((1, 0, 2)):
+            for n, j in enumerate((0, 1, 2)):
                 a, a_s = slots(j, e, h * P, (h + 1) * P)
                 b, b_s = weights(j, e, 0, K)
                 nc.tensor.matmul_mx(out=acc[:], lhsT=a, lhsT_scale=a_s, rhs=b, rhs_scale=b_s,
@@ -206,7 +203,7 @@ def tile_moe_qkb_kernel(
             cast(e, raw[e], 0, K, 0)
         gate_bank = tr.tile([P, K], F32, name="bank")
         nc.tensor.transpose(gate_bank[:, 0:P], gate_rows[:], ident[:])
-        nc.scalar.copy(gate_col[:], gate_bank[:, 0:S // P])
+        nc.scalar.copy(gate_col[:], gate_bank[:, 0:2 * LAST])
 
         for e in range(LAST):
             quantize(e, 0, K)
@@ -223,25 +220,26 @@ def tile_moe_qkb_kernel(
         quantize(LAST, 0, K)
         gather_words(2, LAST)
         gather_scales(2, LAST)
-        accs = [product_by_feature(ct) for ct in range(CT)]
-        turn(1, 0, 4)
-        turn(1, 4, 6)
+        accs = [product_by_feature(ct) for ct in range(2)]
         gate_last_expert(0, accs[0])
         gate_last_expert(1, accs[1])
+        turn(1, 0, 2)
+        turn(1, 2, 6)
+        accs += [product_by_feature(ct) for ct in range(2, CT)]
         fetch(0, 0, 0, T)
         fetch(0, 1, 0, T)
         for ct in range(2, CT):
-            turn(ct, 0, 4)
-            turn(ct, 4, 6)
+            turn(ct, 0, 2)
+            turn(ct, 2, 6)
+        finish(0, 0, T, nc.gpsimd)
         for ct in range(1, CT - 1):
             fetch(ct, 0, 0, T)
-            finish(ct - 1, 0, T, nc.vector)
             gate_last_expert(ct + 1, accs[ct + 1])
             fetch(ct, 1, 0, T)
+            finish(ct, 0, T, nc.gpsimd)
         ct = CT - 1
         fetch(ct, 0, 0, T)
-        finish(ct - 1, 0, T, nc.vector)
         fetch(ct, 1, 0, T // 2)
+        finish(ct, 0, T // 2, nc.gpsimd)
         fetch(ct, 1, T // 2, T)
-        finish(ct, 0, T // 2, nc.vector)
         finish(ct, T // 2, T, nc.vector)

@@ -22,8 +22,7 @@ ADD = mybir.AluOpType.add
 P = 128
 CT = K // P
 LAST = E - 1
-HALF = K // 2
-SLOT_ROW = (0, 0, 0)
+KIB = 1024
 WEIGHT_ROW = (0, 0, 4)
 
 
@@ -34,6 +33,7 @@ def tile_moe_qkb_kernel(
     nc = tc.nc
     with ExitStack() as ctx:
         keep = ctx.enter_context(tc.tile_pool(name="keep", bufs=1))
+        reuse = ctx.enter_context(tc.tile_pool(name="reuse", bufs=1))
         mm = ctx.enter_context(tc.psum_pool(name="mm", bufs=4))
         tr = ctx.enter_context(tc.psum_pool(name="tr", bufs=4))
 
@@ -45,30 +45,46 @@ def tile_moe_qkb_kernel(
         names = ("q", "k", "v")
         g_words_in = (dq_words, dk_words, dv_words)
         g_scales_in = (dq_scales, dk_scales, dv_scales)
-        width = (2 * T, 2 * T, T)
+        width = (2 * T, 2 * T, 2 * T)
         gw = [sb([P, width[j]], U32, "gw_" + n) for j, n in enumerate(names)]
         gs = [sb([P, width[j]], U8, "gs_" + n) for j, n in enumerate(names)]
-        runs = (((0, LAST), (LAST, E)), ((0, LAST), (LAST, E)), tuple((e, e + 1) for e in range(E)))
-        sw = [{r: sb([P, (r[1] - r[0]) * C], U32, "sw_%s%d" % (n, r[0])) for r in runs[j]} for j, n in enumerate(names)]
-        ss = [{r: sb([P, (r[1] - r[0]) * C], U8, "ss_%s%d" % (n, r[0])) for r in runs[j]} for j, n in enumerate(names)]
+        word_runs = ((0, LAST), (LAST, E))
+        scale_runs = ((0, 2), (2, LAST), (LAST, E))
+
+        def at(offset, shape, dtype, name):
+            return reuse.tile(shape, dtype, name=name, align_bytes=64, offset=offset)
+
+        raw = [at(24 * KIB, [P, 4, K], F32, "raw0"), at(8 * KIB, [P, 4, K], F32, "raw1"), sb([P, 4, K], F32, "raw2"),
+               sb([P, 4, K], F32, "raw3")]
+        sw = [{word_runs[0]: sb([P, LAST * C], U32, "sw_" + n)} for n in names]
+        ss = [{scale_runs[0]: sb([P, 2 * C], U8, "ss_" + n)} for n in names]
+        for j in range(3):
+            ss[j][(2, LAST)] = at(21 * KIB + j * C, [P, C], U8, "ss_third_" + names[j])
+            sw[j][(LAST, E)] = at((12 + j) * KIB, [P, C], U32, "sw_last_" + names[j])
+            ss[j][(LAST, E)] = at(15 * KIB + j * C, [P, C], U8, "ss_last_" + names[j])
         wks = sb([P, E, K], U8, "wks")
         wvs = sb([P, E, K], U8, "wvs")
-        wkw = [sb([P, 2, 2 * K], U8, "wkw%d" % h) for h in range(2)]
-        wvw = [sb([P, K], U32, "wvw%d" % e) for e in range(E)]
-        raw = [sb([P, 4, K], F32, "raw%d" % e) for e in range(E)]
-        grouped = [sb([P, K, 4], BF16, "grp%d" % e) for e in range(E)]
-        wqw = [sb([P, K], U32, "wqw%d" % e) for e in range(E)]
-        wqs = [sb([P, K], U8, "wqs%d" % e) for e in range(E)]
+        wkw = [at(20 * KIB, [P, 2, 2 * K], U8, "wkw0"), sb([P, 2, 2 * K], U8, "wkw1")]
+        wvw = [at(32 * KIB, [P, K], U32, "wvw1") if e == 1 else sb([P, K], U32, "wvw%d" % e) for e in range(E)]
+        pieces = [(e, 0, K) for e in range(LAST)] + [(LAST, ct * P, (ct + 1) * P) for ct in range(CT)]
+        grouped = {pieces[0]: sb([P, K, 4], BF16, "grp0"), pieces[1]: at(24 * KIB, [P, K, 4], BF16, "grp1"),
+                   pieces[2]: at(12 * KIB, [P, K, 4], BF16, "grp2")}
+        for g, half_kib in zip(pieces[LAST:], (64, 3, 7, 40)):
+            grouped[g] = at(half_kib * KIB // 2, [P, P, 4], BF16, "grp_last%d" % g[1])
+        wqw = {g: sb([P, g[2] - g[1]], U32, "wqw%d_%d" % g[:2]) for g in pieces if g[0] != 2}
+        wqw[pieces[2]] = at(2 * KIB, [P, K], U32, "wqw2")
+        wqs = {g: sb([P, g[2] - g[1]], U8, "wqs%d_%d" % g[:2]) for g in pieces if g[0] != 2}
+        wqs[pieces[2]] = at(20 * KIB, [P, K], U8, "wqs2")
         gate_rows = sb([P, P], F32, "gate_rows")
-        gate_col = sb([P, 2 * LAST], F32, "gate_col")
+        gate_col = at(10 * KIB, [P, 2 * LAST], F32, "gate_col")
         gate_last = sb([P, C], F32, "gate_last")
         ident = sb([P, P], F32, "ident")
         by_slot = [sb([P, K], F32, "by_slot%d" % s) for s in range(2 * LAST)]
+        plain = {ct: sb([P, C], F32, "plain%d" % ct) for ct in range(1, CT)}
         dx = [sb([P, S], F32, "dx%d" % ct) for ct in range(CT)]
-        got = [[sb([P, T], F32, "got%d_%d" % (ct, i)) for i in range(2)] for ct in range(CT)]
+        got = [[at(0, [P, T], F32, "got0_0"), at(19 * KIB, [P, T], F32, "got0_1")]]
+        got += [[sb([P, T], F32, "got%d_%d" % (ct, i)) for i in range(2)] for ct in range(1, CT)]
         res = [sb([P, T], F32, "res%d" % ct) for ct in range(CT)]
-
-        make_identity(nc, ident[:])
 
         def load_words(j):
             nc.sync.dma_start(gw[j][:, 0:T].bitcast(I32), g_words_in[j][0].rearrange("p t d -> p (t d)").bitcast(I32))
@@ -81,7 +97,7 @@ def tile_moe_qkb_kernel(
             plane, src = (wks, wk_scales) if j == 1 else (wvs, wv_scales)
             rows = src.rearrange("e s (q r) c -> r q (e s) c", r=4)
             for r in range(r0, r1):
-                nc.sync.dma_start(plane[WEIGHT_ROW[j] + r:P:32, :, :].bitcast(I32), rows[r].bitcast(I32))
+                (nc.gpsimd if j == 1 or r < 2 else nc.sync).dma_start(plane[WEIGHT_ROW[j] + r:P:32, :, :].bitcast(I32), rows[r].bitcast(I32))
 
         def wq_rows(e):
             return wq[e].rearrange("(p j) c -> p j c", j=4)
@@ -93,81 +109,92 @@ def tile_moe_qkb_kernel(
         def load_wv(e):
             nc.sync.dma_start(wvw[e][:].bitcast(I32), wv_words[e, 0].rearrange("p c d -> p (c d)").bitcast(I32))
 
+        make_identity(nc, ident[:])
+        nc.gpsimd.dma_start(gate_rows[:], gate.rearrange("a (s p) -> (a s) p", p=P)[0:P, :])
+        load_weight_scales(1, 0, 4)
+        load_weight_scales(2, 0, 2)
         load_words(0)
         nc.sync.dma_start(offs_t[:], offs)
         load_words(1)
         nc.sync.dma_start(raw[0][:], wq_rows(0))
         for q in range(4):
             load_scales(0, q)
+        load_words(2)
         nc.sync.dma_start(raw[1][:], wq_rows(1))
-        nc.sync.dma_start(gate_rows[:], gate.rearrange("a (s p) -> (a s) p", p=P)[0:P, :])
         for q in range(4):
             load_scales(1, q)
-        load_words(2)
-        nc.sync.dma_start(raw[2][:], wq_rows(2))
-        for q in range(4):
+        for q in range(2):
             load_scales(2, q)
-        load_weight_scales(1, 0, 2)
-        nc.sync.dma_start(raw[3][:], wq_rows(3))
-        load_weight_scales(1, 2, 4)
-        load_weight_scales(2, 0, 2)
+        nc.sync.dma_start(raw[2][:], wq_rows(2))
+        for q in range(2, 4):
+            load_scales(2, q)
         load_wk(0)
+        load_weight_scales(2, 2, 3)
         load_wv(0)
-        load_weight_scales(2, 2, 4)
+        load_weight_scales(2, 3, 4)
         load_wv(1)
         load_wk(1)
         load_wv(2)
+        nc.sync.dma_start(raw[3][:], wq_rows(3))
         load_wv(3)
         nc.sync.dma_start(gate_last[:], gate[:, LAST * C:S])
         nc.sync.dma_start(pos_t[0][:], pos1)
         nc.sync.dma_start(pos_t[1][:], pos2)
 
-        def run_of(j, e):
-            return [r for r in runs[j] if r[0] <= e < r[1]][0]
+        def run_of(runs, e):
+            return [r for r in runs if r[0] <= e < r[1]][0]
 
         def gather_words(j, e):
-            r = run_of(j, e)
+            r = run_of(word_runs, e)
             nc.vector.tensor_copy(sw[j][r][:], gw[j][:].indirect(offs_t[:, r[0] * C // 16:r[1] * C // 16]))
 
         def gather_scales(j, e):
-            r = run_of(j, e)
+            r = run_of(scale_runs, e)
             nc.vector.tensor_copy(ss[j][r][:], gs[j][:].indirect(offs_t[:, r[0] * C // 16:r[1] * C // 16]))
 
-        def cast(e, src, c0, c1, s0):
-            w = c1 - c0
+        def cast(g):
             nc.scalar.copy(
-                grouped[e][:, c0:c1, :].rearrange("p (c i) j -> p c j i", i=4),
-                src[:, :, s0:s0 + w].rearrange("p j (c i) -> p c j i", i=4),
+                grouped[g][:].rearrange("p (c i) j -> p c j i", i=4),
+                raw[g[0]][:, :, g[1]:g[2]].rearrange("p j (c i) -> p c j i", i=4),
             )
 
-        def quantize(e, c0, c1):
+        def quantize(g):
             nc.vector.quantize_mx(
-                out=wqw[e][:, c0:c1].bitcast(FP8X4),
-                scales=wqs[e][:, c0:c1],
-                in_=grouped[e][:, c0:c1, :].rearrange("p c j -> p (c j)"),
+                out=wqw[g][:].bitcast(FP8X4),
+                scales=wqs[g][:],
+                in_=grouped[g][:].rearrange("p c j -> p (c j)"),
             )
 
         def weights(j, e, c0, c1):
             if j == 0:
-                return wqw[e][:, c0:c1].bitcast(FP8X4), wqs[e][:, c0:c1]
+                return wqw[(e, c0, c1)][:].bitcast(FP8X4), wqs[(e, c0, c1)][:]
             if j == 1:
                 return wkw[e // 2][:, e % 2, 2 * c0:2 * c1].bitcast(FP4X4), wks[:, e, c0:c1]
             return wvw[e][:, c0:c1].bitcast(FP8X4), wvs[WEIGHT_ROW[2]:P, e, c0:c1]
 
         def slots(j, e, u0, u1):
-            r = run_of(j, e)
-            base = (e - r[0]) * C
-            return sw[j][r][:, base + u0:base + u1].bitcast(FP8X4), ss[j][r][SLOT_ROW[j]:P, base + u0:base + u1]
+            rw, rs = run_of(word_runs, e), run_of(scale_runs, e)
+            bw, bs = (e - rw[0]) * C, (e - rs[0]) * C
+            return sw[j][rw][:, bw + u0:bw + u1].bitcast(FP8X4), ss[j][rs][:, bs + u0:bs + u1]
 
         def product_by_slot(e, h):
             acc = mm.tile([P, K], F32, name="acc")
-            for n, j in enumerate((0, 1, 2)):
+            for n, j in enumerate((1, 2, 0) if e == 2 else (0, 1, 2)):
                 a, a_s = slots(j, e, h * P, (h + 1) * P)
                 b, b_s = weights(j, e, 0, K)
                 nc.tensor.matmul_mx(out=acc[:], lhsT=a, lhsT_scale=a_s, rhs=b, rhs_scale=b_s,
                                     start=(n == 0), stop=(n == 2))
             s = 2 * e + h
             nc.scalar.activation(by_slot[s][:], acc[:], COPY, scale=gate_col[:, s:s + 1])
+
+        def turn_half(ct, h):
+            bank = tr.tile([P, K], F32, name="bank")
+            for e in range(LAST):
+                nc.tensor.transpose(bank[:, e * P:(e + 1) * P], by_slot[2 * e + h][:, ct * P:(ct + 1) * P], ident[:])
+            nc.scalar.copy(
+                dx[ct][:].rearrange("p (e h u) -> p h e u", h=2, u=P)[:, h, 0:LAST, :],
+                bank[:, 0:LAST * P].rearrange("p (e u) -> p e u", u=P),
+            )
 
         def turn(ct, s0, s1):
             bank = tr.tile([P, K], F32, name="bank")
@@ -188,6 +215,10 @@ def tile_moe_qkb_kernel(
         def gate_last_expert(ct, acc):
             nc.vector.tensor_tensor(dx[ct][:, LAST * C:S], acc[:, 0:C], gate_last[:], MULT)
 
+        def gate_last_expert_aside(ct, acc):
+            nc.scalar.copy(plain[ct][:], acc[:, 0:C])
+            nc.gpsimd.tensor_tensor(dx[ct][:, LAST * C:S], plain[ct][:], gate_last[:], MULT)
+
         def fetch(ct, i, t0, t1):
             nc.vector.tensor_copy(got[ct][i][:, t0:t1], dx[ct][:].indirect(pos_t[i][:, t0 // 16:t1 // 16]))
 
@@ -195,46 +226,42 @@ def tile_moe_qkb_kernel(
             eng.tensor_tensor(res[ct][:, t0:t1], got[ct][0][:, t0:t1], got[ct][1][:, t0:t1], ADD)
             nc.sync.dma_start(out[ct * P:(ct + 1) * P, t0:t1], res[ct][:, t0:t1])
 
-        for j in range(2):
+        for j in range(3):
             gather_words(j, 0)
-        for j in range(2):
-            gather_scales(j, 0)
-        for e in range(E):
-            cast(e, raw[e], 0, K, 0)
+        for g in pieces[:LAST]:
+            cast(g)
         gate_bank = tr.tile([P, K], F32, name="bank")
         nc.tensor.transpose(gate_bank[:, 0:P], gate_rows[:], ident[:])
         nc.scalar.copy(gate_col[:], gate_bank[:, 0:2 * LAST])
 
-        for e in range(LAST):
-            quantize(e, 0, K)
-            gather_words(2, e)
-            gather_scales(2, e)
+        gather_scales(0, 0)
+        quantize(pieces[0])
+        gather_scales(1, 0)
+        quantize(pieces[1])
+        gather_scales(2, 0)
+        for e in range(2):
             for h in range(2):
                 product_by_slot(e, h)
-            if e == 1:
-                turn(0, 0, 4)
+        for j in (1, 2, 0):
+            gather_scales(j, 2)
+        quantize(pieces[2])
+        for h in range(2):
+            product_by_slot(2, h)
+        turn(0, 0, 4)
         turn(0, 4, 6)
-        for j in range(2):
+        for j in range(3):
             gather_words(j, LAST)
             gather_scales(j, LAST)
-        quantize(LAST, 0, K)
-        gather_words(2, LAST)
-        gather_scales(2, LAST)
-        accs = [product_by_feature(ct) for ct in range(2)]
-        gate_last_expert(0, accs[0])
-        gate_last_expert(1, accs[1])
-        turn(1, 0, 2)
-        turn(1, 2, 6)
-        accs += [product_by_feature(ct) for ct in range(2, CT)]
-        fetch(0, 0, 0, T)
-        fetch(0, 1, 0, T)
-        for ct in range(2, CT):
-            turn(ct, 0, 2)
-            turn(ct, 2, 6)
-        finish(0, 0, T, nc.gpsimd)
-        for ct in range(1, CT - 1):
+        for g in pieces[LAST:]:
+            cast(g)
+            quantize(g)
+        gate_last_expert(0, product_by_feature(0))
+        for ct in range(1, CT):
+            gate_last_expert_aside(ct, product_by_feature(ct))
+            for h in range(2):
+                turn_half(ct, h)
+        for ct in range(CT - 1):
             fetch(ct, 0, 0, T)
-            gate_last_expert(ct + 1, accs[ct + 1])
             fetch(ct, 1, 0, T)
             finish(ct, 0, T, nc.gpsimd)
         ct = CT - 1

@@ -80,11 +80,9 @@ def tile_moe_qkb_kernel(
         gate_last = sb([P, C], F32, "gate_last")
         ident = sb([P, P], F32, "ident")
         by_slot = [sb([P, K], F32, "by_slot%d" % s) for s in range(2 * LAST)]
-        plain = {ct: sb([P, C], F32, "plain%d" % ct) for ct in range(1, CT)}
         dx = [sb([P, S], F32, "dx%d" % ct) for ct in range(CT)]
-        got = [[at(0, [P, T], F32, "got0_0"), at(19 * KIB, [P, T], F32, "got0_1")]]
-        got += [[sb([P, T], F32, "got%d_%d" % (ct, i)) for i in range(2)] for ct in range(1, CT)]
-        res = [sb([P, T], F32, "res%d" % ct) for ct in range(CT)]
+        first = [at(0, [P, T], F32, "first0")] + [sb([P, T], F32, "first%d" % ct) for ct in range(1, CT)]
+        res = [at(19 * KIB, [P, T], F32, "res0")] + [sb([P, T], F32, "res%d" % ct) for ct in range(1, CT)]
 
         def load_words(j):
             nc.sync.dma_start(gw[j][:, 0:T].bitcast(I32), g_words_in[j][0].rearrange("p t d -> p (t d)").bitcast(I32))
@@ -215,15 +213,12 @@ def tile_moe_qkb_kernel(
         def gate_last_expert(ct, acc):
             nc.vector.tensor_tensor(dx[ct][:, LAST * C:S], acc[:, 0:C], gate_last[:], MULT)
 
-        def gate_last_expert_aside(ct, acc):
-            nc.scalar.copy(plain[ct][:], acc[:, 0:C])
-            nc.gpsimd.tensor_tensor(dx[ct][:, LAST * C:S], plain[ct][:], gate_last[:], MULT)
+        def fetch(ct):
+            nc.vector.tensor_copy(first[ct][:], dx[ct][:].indirect(pos_t[0][:]))
 
-        def fetch(ct, i, t0, t1):
-            nc.vector.tensor_copy(got[ct][i][:, t0:t1], dx[ct][:].indirect(pos_t[i][:, t0 // 16:t1 // 16]))
-
-        def finish(ct, t0, t1, eng):
-            eng.tensor_tensor(res[ct][:, t0:t1], got[ct][0][:, t0:t1], got[ct][1][:, t0:t1], ADD)
+        def fetch_add(ct, t0, t1):
+            nc.vector.tensor_tensor(res[ct][:, t0:t1], dx[ct][:].indirect(pos_t[1][:, t0 // 16:t1 // 16]),
+                                    first[ct][:, t0:t1], ADD)
             nc.sync.dma_start(out[ct * P:(ct + 1) * P, t0:t1], res[ct][:, t0:t1])
 
         for j in range(3):
@@ -257,16 +252,12 @@ def tile_moe_qkb_kernel(
             quantize(g)
         gate_last_expert(0, product_by_feature(0))
         for ct in range(1, CT):
-            gate_last_expert_aside(ct, product_by_feature(ct))
+            gate_last_expert(ct, product_by_feature(ct))
             for h in range(2):
                 turn_half(ct, h)
         for ct in range(CT - 1):
-            fetch(ct, 0, 0, T)
-            fetch(ct, 1, 0, T)
-            finish(ct, 0, T, nc.gpsimd)
-        ct = CT - 1
-        fetch(ct, 0, 0, T)
-        fetch(ct, 1, 0, T // 2)
-        finish(ct, 0, T // 2, nc.gpsimd)
-        fetch(ct, 1, T // 2, T)
-        finish(ct, T // 2, T, nc.vector)
+            fetch(ct)
+            fetch_add(ct, 0, T)
+        fetch(CT - 1)
+        fetch_add(CT - 1, 0, T // 2)
+        fetch_add(CT - 1, T // 2, T)

@@ -95,7 +95,7 @@ def tile_moe_qkb_kernel(
             plane, src = (wks, wk_scales) if j == 1 else (wvs, wv_scales)
             rows = src.rearrange("e s (q r) c -> r q (e s) c", r=4)
             for r in range(r0, r1):
-                (nc.gpsimd if j == 1 or r < 2 else nc.sync).dma_start(plane[WEIGHT_ROW[j] + r:P:32, :, :].bitcast(I32), rows[r].bitcast(I32))
+                nc.sync.dma_start(plane[WEIGHT_ROW[j] + r:P:32, :, :].bitcast(I32), rows[r].bitcast(I32))
 
         def wq_rows(e):
             return wq[e].rearrange("(p j) c -> p j c", j=4)
@@ -108,9 +108,6 @@ def tile_moe_qkb_kernel(
             nc.sync.dma_start(wvw[e][:].bitcast(I32), wv_words[e, 0].rearrange("p c d -> p (c d)").bitcast(I32))
 
         make_identity(nc, ident[:])
-        nc.gpsimd.dma_start(gate_rows[:], gate.rearrange("a (s p) -> (a s) p", p=P)[0:P, :])
-        load_weight_scales(1, 0, 4)
-        load_weight_scales(2, 0, 2)
         load_words(0)
         nc.sync.dma_start(offs_t[:], offs)
         load_words(1)
@@ -121,15 +118,15 @@ def tile_moe_qkb_kernel(
         nc.sync.dma_start(raw[1][:], wq_rows(1))
         for q in range(4):
             load_scales(1, q)
-        for q in range(2):
-            load_scales(2, q)
+        nc.sync.dma_start(gate_rows[:], gate.rearrange("a (s p) -> (a s) p", p=P)[0:P, :])
+        load_scales(2, 0)
         nc.sync.dma_start(raw[2][:], wq_rows(2))
-        for q in range(2, 4):
+        for q in range(1, 4):
             load_scales(2, q)
+        load_weight_scales(1, 0, 4)
         load_wk(0)
-        load_weight_scales(2, 2, 3)
         load_wv(0)
-        load_weight_scales(2, 3, 4)
+        load_weight_scales(2, 0, 4)
         load_wv(1)
         load_wk(1)
         load_wv(2)

@@ -49,17 +49,17 @@ def tile_moe_qkb_kernel(
         gw = [sb([P, width[j]], U32, "gw_" + n) for j, n in enumerate(names)]
         gs = [sb([P, width[j]], U8, "gs_" + n) for j, n in enumerate(names)]
         word_runs = ((0, LAST), (LAST, E))
-        scale_runs = ((0, 2), (2, LAST), (LAST, E))
+        scale_runs = (word_runs, word_runs, ((0, 2), (2, LAST), (LAST, E)))
 
         def at(offset, shape, dtype, name):
             return reuse.tile(shape, dtype, name=name, align_bytes=64, offset=offset)
 
-        raw = [at(24 * KIB, [P, 4, K], F32, "raw0"), at(8 * KIB, [P, 4, K], F32, "raw1"), sb([P, 4, K], F32, "raw2"),
-               sb([P, 4, K], F32, "raw3")]
+        raw = [at(24 * KIB, [P, 4, K], F32, "raw0"), at(8 * KIB, [P, 4, K], F32, "raw1"), sb([P, 4, K], F32, "raw2")]
+        raw_last = [sb([P, 4, P], F32, "raw_last_head"), sb([P, 4, K - P], F32, "raw_last_rest")]
         sw = [{word_runs[0]: sb([P, LAST * C], U32, "sw_" + n)} for n in names]
-        ss = [{scale_runs[0]: sb([P, 2 * C], U8, "ss_" + n)} for n in names]
+        ss = [{r: sb([P, (r[1] - r[0]) * C], U8, "ss_%s%d" % (n, r[0])) for r in scale_runs[j][:-1]}
+              for j, n in enumerate(names)]
         for j in range(3):
-            ss[j][(2, LAST)] = at(21 * KIB + j * C, [P, C], U8, "ss_third_" + names[j])
             sw[j][(LAST, E)] = at((12 + j) * KIB, [P, C], U32, "sw_last_" + names[j])
             ss[j][(LAST, E)] = at(15 * KIB + j * C, [P, C], U8, "ss_last_" + names[j])
         wks = sb([P, E, K], U8, "wks")
@@ -69,20 +69,21 @@ def tile_moe_qkb_kernel(
         pieces = [(e, 0, K) for e in range(LAST)] + [(LAST, ct * P, (ct + 1) * P) for ct in range(CT)]
         grouped = {pieces[0]: sb([P, K, 4], BF16, "grp0"), pieces[1]: at(24 * KIB, [P, K, 4], BF16, "grp1"),
                    pieces[2]: at(12 * KIB, [P, K, 4], BF16, "grp2")}
-        for g, half_kib in zip(pieces[LAST:], (64, 3, 7, 40)):
-            grouped[g] = at(half_kib * KIB // 2, [P, P, 4], BF16, "grp_last%d" % g[1])
+        for g, kib in zip(pieces[LAST:], (32, 44, 45, 46)):
+            grouped[g] = at(kib * KIB, [P, P, 4], BF16, "grp_last%d" % g[1])
         wqw = {g: sb([P, g[2] - g[1]], U32, "wqw%d_%d" % g[:2]) for g in pieces if g[0] != 2}
         wqw[pieces[2]] = at(2 * KIB, [P, K], U32, "wqw2")
-        wqs = {g: sb([P, g[2] - g[1]], U8, "wqs%d_%d" % g[:2]) for g in pieces if g[0] != 2}
+        wqs = {g: sb([P, g[2] - g[1]], U8, "wqs%d_%d" % g[:2]) for g in pieces if g not in pieces[2:4]}
         wqs[pieces[2]] = at(20 * KIB, [P, K], U8, "wqs2")
+        wqs[pieces[LAST]] = at(5 * KIB // 2, [P, P], U8, "wqs_last0")
         gate_rows = sb([P, P], F32, "gate_rows")
-        gate_col = at(10 * KIB, [P, 2 * LAST], F32, "gate_col")
-        gate_last = sb([P, C], F32, "gate_last")
+        gate_col = at(10 * KIB, [P, 2 * E], F32, "gate_col")
+        gate_tail = {e: sb([P, C], F32, "gate_tail%d" % e) for e in (2, LAST)}
         ident = sb([P, P], F32, "ident")
-        by_slot = [sb([P, K], F32, "by_slot%d" % s) for s in range(2 * LAST)]
+        by_slot = [sb([P, K], F32, "by_slot%d" % s) for s in range(2 * E)]
         dx = [sb([P, S], F32, "dx%d" % ct) for ct in range(CT)]
-        first = [at(0, [P, T], F32, "first0")] + [sb([P, T], F32, "first%d" % ct) for ct in range(1, CT)]
-        res = [at(19 * KIB, [P, T], F32, "res0")] + [sb([P, T], F32, "res%d" % ct) for ct in range(1, CT)]
+        first = [at(46 * KIB, [P, T], F32, "first0")] + [sb([P, T], F32, "first%d" % ct) for ct in range(1, CT)]
+        res = [sb([P, T], F32, "res%d" % ct) for ct in range(CT)]
 
         def load_words(j):
             nc.sync.dma_start(gw[j][:, 0:T].bitcast(I32), g_words_in[j][0].rearrange("p t d -> p (t d)").bitcast(I32))
@@ -95,7 +96,7 @@ def tile_moe_qkb_kernel(
             plane, src = (wks, wk_scales) if j == 1 else (wvs, wv_scales)
             rows = src.rearrange("e s (q r) c -> r q (e s) c", r=4)
             for r in range(r0, r1):
-                nc.sync.dma_start(plane[WEIGHT_ROW[j] + r:P:32, :, :].bitcast(I32), rows[r].bitcast(I32))
+                (nc.gpsimd if j == 1 else nc.sync).dma_start(plane[WEIGHT_ROW[j] + r:P:32, :, :].bitcast(I32), rows[r].bitcast(I32))
 
         def wq_rows(e):
             return wq[e].rearrange("(p j) c -> p j c", j=4)
@@ -107,6 +108,8 @@ def tile_moe_qkb_kernel(
         def load_wv(e):
             nc.sync.dma_start(wvw[e][:].bitcast(I32), wv_words[e, 0].rearrange("p c d -> p (c d)").bitcast(I32))
 
+        nc.gpsimd.dma_start(gate_rows[:], gate.rearrange("a (s p) -> (a s) p", p=P)[0:P, :])
+        load_weight_scales(1, 0, 4)
         make_identity(nc, ident[:])
         load_words(0)
         nc.sync.dma_start(offs_t[:], offs)
@@ -118,22 +121,25 @@ def tile_moe_qkb_kernel(
         nc.sync.dma_start(raw[1][:], wq_rows(1))
         for q in range(4):
             load_scales(1, q)
-        nc.sync.dma_start(gate_rows[:], gate.rearrange("a (s p) -> (a s) p", p=P)[0:P, :])
-        load_scales(2, 0)
-        nc.sync.dma_start(raw[2][:], wq_rows(2))
-        for q in range(1, 4):
+        for q in range(2):
             load_scales(2, q)
-        load_weight_scales(1, 0, 4)
+        nc.sync.dma_start(raw[2][:], wq_rows(2))
+        for q in range(2, 4):
+            load_scales(2, q)
         load_wk(0)
+        load_weight_scales(2, 0, 1)
         load_wv(0)
-        load_weight_scales(2, 0, 4)
+        load_weight_scales(2, 1, 2)
         load_wv(1)
+        load_weight_scales(2, 2, 4)
         load_wk(1)
         load_wv(2)
-        nc.sync.dma_start(raw[3][:], wq_rows(3))
+        nc.sync.dma_start(gate_tail[2][:], gate[:, 2 * C:LAST * C])
+        nc.sync.dma_start(raw_last[0][:], wq_rows(LAST)[:, :, 0:P])
         load_wv(3)
-        nc.sync.dma_start(gate_last[:], gate[:, LAST * C:S])
+        nc.sync.dma_start(gate_tail[LAST][:], gate[:, LAST * C:S])
         nc.sync.dma_start(pos_t[0][:], pos1)
+        nc.sync.dma_start(raw_last[1][:], wq_rows(LAST)[:, :, P:K])
         nc.sync.dma_start(pos_t[1][:], pos2)
 
         def run_of(runs, e):
@@ -144,13 +150,21 @@ def tile_moe_qkb_kernel(
             nc.vector.tensor_copy(sw[j][r][:], gw[j][:].indirect(offs_t[:, r[0] * C // 16:r[1] * C // 16]))
 
         def gather_scales(j, e):
-            r = run_of(scale_runs, e)
+            r = run_of(scale_runs[j], e)
             nc.vector.tensor_copy(ss[j][r][:], gs[j][:].indirect(offs_t[:, r[0] * C // 16:r[1] * C // 16]))
 
         def cast(g):
+            if g[0] < LAST:
+                rows = raw[g[0]][:]
+            elif g[1] == 0:
+                rows = raw_last[0][:]
+            else:
+                rows = raw_last[1][:, :, g[1] - P:g[2] - P]
+                nc.gpsimd.tensor_copy(grouped[g][:], rows.rearrange("p j c -> p c j"))
+                return
             nc.scalar.copy(
                 grouped[g][:].rearrange("p (c i) j -> p c j i", i=4),
-                raw[g[0]][:, :, g[1]:g[2]].rearrange("p j (c i) -> p c j i", i=4),
+                rows.rearrange("p j (c i) -> p c j i", i=4),
             )
 
         def quantize(g):
@@ -162,33 +176,36 @@ def tile_moe_qkb_kernel(
 
         def weights(j, e, c0, c1):
             if j == 0:
-                return wqw[(e, c0, c1)][:].bitcast(FP8X4), wqs[(e, c0, c1)][:]
+                g = [g for g in pieces if g[0] == e and g[1] <= c0 < g[2]][0]
+                return wqw[g][:, c0 - g[1]:c1 - g[1]].bitcast(FP8X4), wqs[g][:, c0 - g[1]:c1 - g[1]]
             if j == 1:
                 return wkw[e // 2][:, e % 2, 2 * c0:2 * c1].bitcast(FP4X4), wks[:, e, c0:c1]
             return wvw[e][:, c0:c1].bitcast(FP8X4), wvs[WEIGHT_ROW[2]:P, e, c0:c1]
 
         def slots(j, e, u0, u1):
-            rw, rs = run_of(word_runs, e), run_of(scale_runs, e)
+            rw, rs = run_of(word_runs, e), run_of(scale_runs[j], e)
             bw, bs = (e - rw[0]) * C, (e - rs[0]) * C
             return sw[j][rw][:, bw + u0:bw + u1].bitcast(FP8X4), ss[j][rs][:, bs + u0:bs + u1]
 
-        def product_by_slot(e, h):
+        def product_by_slot(e, h, passes):
             acc = mm.tile([P, K], F32, name="acc")
-            for n, j in enumerate((1, 2, 0) if e == 2 else (0, 1, 2)):
+            for n, (j, c0, c1) in enumerate(passes):
                 a, a_s = slots(j, e, h * P, (h + 1) * P)
-                b, b_s = weights(j, e, 0, K)
-                nc.tensor.matmul_mx(out=acc[:], lhsT=a, lhsT_scale=a_s, rhs=b, rhs_scale=b_s,
-                                    start=(n == 0), stop=(n == 2))
-            s = 2 * e + h
-            nc.scalar.activation(by_slot[s][:], acc[:], COPY, scale=gate_col[:, s:s + 1])
+                b, b_s = weights(j, e, c0, c1)
+                nc.tensor.matmul_mx(out=acc[:, c0:c1], lhsT=a, lhsT_scale=a_s, rhs=b, rhs_scale=b_s,
+                                    start=(n == 0), stop=(n == len(passes) - 1))
+            return acc
 
-        def turn_half(ct, h):
+        def gate_by_slot(s, acc, c0, c1):
+            nc.scalar.activation(by_slot[s][:, c0:c1], acc[:, c0:c1], COPY, scale=gate_col[:, s:s + 1])
+
+        def turn_half(ct, h, experts):
             bank = tr.tile([P, K], F32, name="bank")
-            for e in range(LAST):
+            for e in range(experts):
                 nc.tensor.transpose(bank[:, e * P:(e + 1) * P], by_slot[2 * e + h][:, ct * P:(ct + 1) * P], ident[:])
             nc.scalar.copy(
-                dx[ct][:].rearrange("p (e h u) -> p h e u", h=2, u=P)[:, h, 0:LAST, :],
-                bank[:, 0:LAST * P].rearrange("p (e u) -> p e u", u=P),
+                dx[ct][:].rearrange("p (e h u) -> p h e u", h=2, u=P)[:, h, 0:experts, :],
+                bank[:, 0:experts * P].rearrange("p (e u) -> p e u", u=P),
             )
 
         def turn(ct, s0, s1):
@@ -197,18 +214,16 @@ def tile_moe_qkb_kernel(
                 nc.tensor.transpose(bank[:, (s - s0) * P:(s - s0 + 1) * P], by_slot[s][:, ct * P:(ct + 1) * P], ident[:])
             nc.scalar.copy(dx[ct][:, s0 * P:s1 * P], bank[:, 0:(s1 - s0) * P])
 
-        def product_by_feature(ct):
-            acc = mm.tile([P, K], F32, name="acc")
+        def product_by_feature(e, ct, acc):
             passes = ((0, 0, C), (1, 0, P), (1, P, C), (2, 0, C))
             for n, (j, u0, u1) in enumerate(passes):
-                a, a_s = weights(j, LAST, ct * P, (ct + 1) * P)
-                b, b_s = slots(j, LAST, u0, u1)
+                a, a_s = weights(j, e, ct * P, (ct + 1) * P)
+                b, b_s = slots(j, e, u0, u1)
                 nc.tensor.matmul_mx(out=acc[:, u0:u1], lhsT=a, lhsT_scale=a_s, rhs=b, rhs_scale=b_s,
                                     start=(n == 0), stop=(n == len(passes) - 1))
-            return acc
 
-        def gate_last_expert(ct, acc):
-            nc.vector.tensor_tensor(dx[ct][:, LAST * C:S], acc[:, 0:C], gate_last[:], MULT)
+        def gate_by_feature(e, ct, acc):
+            nc.vector.tensor_tensor(dx[ct][:, e * C:(e + 1) * C], acc, gate_tail[e][:], MULT)
 
         def fetch(ct):
             nc.vector.tensor_copy(first[ct][:], dx[ct][:].indirect(pos_t[0][:]))
@@ -224,35 +239,49 @@ def tile_moe_qkb_kernel(
             cast(g)
         gate_bank = tr.tile([P, K], F32, name="bank")
         nc.tensor.transpose(gate_bank[:, 0:P], gate_rows[:], ident[:])
-        nc.scalar.copy(gate_col[:], gate_bank[:, 0:2 * LAST])
+        nc.scalar.copy(gate_col[:], gate_bank[:, 0:2 * E])
 
         gather_scales(0, 0)
         quantize(pieces[0])
         gather_scales(1, 0)
         quantize(pieces[1])
         gather_scales(2, 0)
-        for e in range(2):
-            for h in range(2):
-                product_by_slot(e, h)
-        for j in (1, 2, 0):
-            gather_scales(j, 2)
+        for s in range(4):
+            gate_by_slot(s, product_by_slot(s // 2, s % 2, ((0, 0, K), (1, 0, K), (2, 0, K))), 0, K)
+        gather_scales(2, 2)
         quantize(pieces[2])
-        for h in range(2):
-            product_by_slot(2, h)
         turn(0, 0, 4)
-        turn(0, 4, 6)
+        cast(pieces[LAST])
+        third = mm.tile([P, K], F32, name="acc")
+        product_by_feature(2, 0, third[:, 0:C])
+        gate_by_feature(2, 0, third[:, 0:C])
+        wide = ((P, 3 * P), (3 * P, K))
+        narrow = tuple((ct * P, (ct + 1) * P) for ct in range(1, CT))
+        for s in range(4, 6):
+            acc = product_by_slot(2, s % 2, [(j,) + c for j, cuts in ((2, wide), (1, narrow), (0, wide)) for c in cuts])
+            gate_by_slot(s, acc, P, K)
         for j in range(3):
             gather_words(j, LAST)
             gather_scales(j, LAST)
-        for g in pieces[LAST:]:
+        quantize(pieces[LAST])
+        lone = mm.tile([P, K], F32, name="acc")
+        product_by_feature(LAST, 0, lone[:, 0:C])
+        gate_by_feature(LAST, 0, lone[:, 0:C])
+        for g in pieces[LAST + 1:]:
             cast(g)
             quantize(g)
-        gate_last_expert(0, product_by_feature(0))
-        for ct in range(1, CT):
-            gate_last_expert(ct, product_by_feature(ct))
+        fetch(0)
+        for h in range(2):
+            turn_half(1, h, LAST)
+        for s in range(6, 8):
+            acc = product_by_slot(LAST, s % 2, [(j,) + c for j, cuts in ((2, wide), (1, narrow), (0, narrow)) for c in cuts])
+            gate_by_slot(s, acc, P, K)
+        turn(1, 6, 8)
+        for ct in range(2, CT):
             for h in range(2):
-                turn_half(ct, h)
-        for ct in range(CT - 1):
+                turn_half(ct, h, E)
+        fetch_add(0, 0, T)
+        for ct in range(1, CT - 1):
             fetch(ct)
             fetch_add(ct, 0, T)
         fetch(CT - 1)

@@ -78,7 +78,7 @@ def tile_moe_qkb_kernel(
         wqs[pieces[LAST]] = at(5 * KIB // 2, [P, P], U8, "wqs_last0")
         gate_rows = sb([P, P], F32, "gate_rows")
         gate_col = at(10 * KIB, [P, 2 * E], F32, "gate_col")
-        gate_tail = {e: sb([P, C], F32, "gate_tail%d" % e) for e in (2, LAST)}
+        gate_tail = sb([P, 2 * C], F32, "gate_tail")
         ident = sb([P, P], F32, "ident")
         by_slot = [sb([P, K], F32, "by_slot%d" % s) for s in range(2 * E)]
         dx = [sb([P, S], F32, "dx%d" % ct) for ct in range(CT)]
@@ -90,7 +90,7 @@ def tile_moe_qkb_kernel(
 
         def load_scales(j, q):
             rows = g_scales_in[j][0][4 * q:4 * q + 4, :].bitcast(I32)
-            nc.sync.dma_start(gs[j][32 * q:32 * q + 32, 0:T].bitcast(I32), rows.unsqueeze(0).to_broadcast([8, 4, T // 4]))
+            nc.sync.dma_start(gs[j][32 * q:32 * q + 4, 0:T].bitcast(I32), rows)
 
         def load_weight_scales(j, r0, r1):
             plane, src = (wks, wk_scales) if j == 1 else (wvs, wv_scales)
@@ -108,6 +108,8 @@ def tile_moe_qkb_kernel(
         def load_wv(e):
             nc.sync.dma_start(wvw[e][:].bitcast(I32), wv_words[e, 0].rearrange("p c d -> p (c d)").bitcast(I32))
 
+        for j in range(3):
+            nc.vector.memset(gs[j][:, 0:T].bitcast(I32), 0)
         nc.gpsimd.dma_start(gate_rows[:], gate.rearrange("a (s p) -> (a s) p", p=P)[0:P, :])
         load_weight_scales(1, 0, 4)
         make_identity(nc, ident[:])
@@ -115,9 +117,9 @@ def tile_moe_qkb_kernel(
         nc.sync.dma_start(offs_t[:], offs)
         load_words(1)
         nc.sync.dma_start(raw[0][:], wq_rows(0))
+        load_words(2)
         for q in range(4):
             load_scales(0, q)
-        load_words(2)
         nc.sync.dma_start(raw[1][:], wq_rows(1))
         for q in range(4):
             load_scales(1, q)
@@ -134,10 +136,9 @@ def tile_moe_qkb_kernel(
         load_weight_scales(2, 2, 4)
         load_wk(1)
         load_wv(2)
-        nc.sync.dma_start(gate_tail[2][:], gate[:, 2 * C:LAST * C])
         nc.sync.dma_start(raw_last[0][:], wq_rows(LAST)[:, :, 0:P])
         load_wv(3)
-        nc.sync.dma_start(gate_tail[LAST][:], gate[:, LAST * C:S])
+        nc.sync.dma_start(gate_tail[:], gate[:, 2 * C:S])
         nc.sync.dma_start(pos_t[0][:], pos1)
         nc.sync.dma_start(raw_last[1][:], wq_rows(LAST)[:, :, P:K])
         nc.sync.dma_start(pos_t[1][:], pos2)
@@ -222,9 +223,6 @@ def tile_moe_qkb_kernel(
                 nc.tensor.matmul_mx(out=acc[:, u0:u1], lhsT=a, lhsT_scale=a_s, rhs=b, rhs_scale=b_s,
                                     start=(n == 0), stop=(n == len(passes) - 1))
 
-        def gate_by_feature(e, ct, acc):
-            nc.vector.tensor_tensor(dx[ct][:, e * C:(e + 1) * C], acc, gate_tail[e][:], MULT)
-
         def fetch(ct):
             nc.vector.tensor_copy(first[ct][:], dx[ct][:].indirect(pos_t[0][:]))
 
@@ -252,9 +250,8 @@ def tile_moe_qkb_kernel(
         quantize(pieces[2])
         turn(0, 0, 4)
         cast(pieces[LAST])
-        third = mm.tile([P, K], F32, name="acc")
-        product_by_feature(2, 0, third[:, 0:C])
-        gate_by_feature(2, 0, third[:, 0:C])
+        tail = tr.tile([P, K], F32, name="bank")
+        product_by_feature(2, 0, tail[:, 0:C])
         wide = ((P, 3 * P), (3 * P, K))
         narrow = tuple((ct * P, (ct + 1) * P) for ct in range(1, CT))
         for s in range(4, 6):
@@ -264,12 +261,11 @@ def tile_moe_qkb_kernel(
             gather_words(j, LAST)
             gather_scales(j, LAST)
         quantize(pieces[LAST])
-        lone = mm.tile([P, K], F32, name="acc")
-        product_by_feature(LAST, 0, lone[:, 0:C])
-        gate_by_feature(LAST, 0, lone[:, 0:C])
+        product_by_feature(LAST, 0, tail[:, C:2 * C])
         for g in pieces[LAST + 1:]:
             cast(g)
             quantize(g)
+        nc.vector.tensor_tensor(dx[0][:, 2 * C:S], tail[:], gate_tail[:], MULT)
         fetch(0)
         for h in range(2):
             turn_half(1, h, LAST)

@@ -21,9 +21,12 @@ ADD = mybir.AluOpType.add
 
 P = 128
 CT = K // P
-LAST = E - 1
+QP, KP, VP = 0, 1, 2
+THIRD, LAST = E - 2, E - 1
 KIB = 1024
-WEIGHT_ROW = (0, 0, 4)
+WINDOW = 2 * T
+WV_ROW = 4
+BANKS = 4
 
 
 def tile_moe_qkb_kernel(
@@ -34,194 +37,184 @@ def tile_moe_qkb_kernel(
     with ExitStack() as ctx:
         keep = ctx.enter_context(tc.tile_pool(name="keep", bufs=1))
         reuse = ctx.enter_context(tc.tile_pool(name="reuse", bufs=1))
-        mm = ctx.enter_context(tc.psum_pool(name="mm", bufs=4))
-        tr = ctx.enter_context(tc.psum_pool(name="tr", bufs=4))
+        mm = ctx.enter_context(tc.psum_pool(name="mm", bufs=BANKS))
+        tr = ctx.enter_context(tc.psum_pool(name="tr", bufs=BANKS))
 
         def sb(shape, dtype, name):
             return keep.tile(shape, dtype, name=name, align_bytes=64)
 
-        offs_t = keep.tile([P, S // 16], U16, name="offs_t")
-        pos_t = [keep.tile([P, T // 16], U16, name="pos%d" % i) for i in range(2)]
-        names = ("q", "k", "v")
-        g_words_in = (dq_words, dk_words, dv_words)
-        g_scales_in = (dq_scales, dk_scales, dv_scales)
-        width = (2 * T, 2 * T, 2 * T)
-        gw = [sb([P, width[j]], U32, "gw_" + n) for j, n in enumerate(names)]
-        gs = [sb([P, width[j]], U8, "gs_" + n) for j, n in enumerate(names)]
-        word_runs = ((0, LAST), (LAST, E))
-        scale_runs = (word_runs, word_runs, ((0, 2), (2, LAST), (LAST, E)))
-
         def at(offset, shape, dtype, name):
             return reuse.tile(shape, dtype, name=name, align_bytes=64, offset=offset)
 
-        raw = [at(24 * KIB, [P, 4, K], F32, "raw0"), at(8 * KIB, [P, 4, K], F32, "raw1"), sb([P, 4, K], F32, "raw2")]
-        raw_last = [sb([P, 4, P], F32, "raw_last_head"), sb([P, 4, K - P], F32, "raw_last_rest")]
-        sw = [{word_runs[0]: sb([P, LAST * C], U32, "sw_" + n)} for n in names]
-        ss = [{r: sb([P, (r[1] - r[0]) * C], U8, "ss_%s%d" % (n, r[0])) for r in scale_runs[j][:-1]}
-              for j, n in enumerate(names)]
-        for j in range(3):
-            sw[j][(LAST, E)] = at((12 + j) * KIB, [P, C], U32, "sw_last_" + names[j])
-            ss[j][(LAST, E)] = at(15 * KIB + j * C, [P, C], U8, "ss_last_" + names[j])
-        wks = sb([P, E, K], U8, "wks")
-        wvs = sb([P, E, K], U8, "wvs")
-        wkw = [at(20 * KIB, [P, 2, 2 * K], U8, "wkw0"), sb([P, 2, 2 * K], U8, "wkw1")]
-        wvw = [at(32 * KIB, [P, K], U32, "wvw1") if e == 1 else sb([P, K], U32, "wvw%d" % e) for e in range(E)]
+        WQ2, ROUND3, WK01, RAW1, RAW0 = 0, 2 * KIB, 4 * KIB, 8 * KIB, 16 * KIB
+        ROUND2 = RAW1 + 4 * KIB
+
+        offs_t = keep.tile([P, S // 16], U16, name="offs_t")
+        pos_t = [keep.tile([P, T // 16], U16, name="pos%d" % i) for i in range(2)]
+        names = ("q", "k", "v")
+        grad_words_in = (dq_words, dk_words, dv_words)
+        grad_scales_in = (dq_scales, dk_scales, dv_scales)
+        grad_words = [sb([P, WINDOW], U32, "grad_words_" + n) for n in names]
+        grad_scales = [sb([P, WINDOW], U8, "grad_scales_" + n) for n in names]
+
+        word_runs = ((0, LAST), (LAST, E))
+        scale_runs = (word_runs, word_runs, ((0, THIRD), (THIRD, LAST), (LAST, E)))
+        raw = [at(RAW0, [P, 4, K], F32, "raw0"), at(RAW1, [P, 4, K], F32, "raw1")]
+        raw += [sb([P, 4, K], F32, "raw%d" % e) for e in (THIRD, LAST)]
+        slot_words = [{word_runs[0]: sb([P, LAST * C], U32, "slot_words_" + n)} for n in names]
+        slot_scales = [{r: sb([P, (r[1] - r[0]) * C], U8, "slot_scales_%s%d" % (n, r[0])) for r in scale_runs[j][:-1]}
+                       for j, n in enumerate(names)]
+        for j, n in enumerate(names):
+            slot_words[j][(LAST, E)] = at(ROUND2 + j * 4 * C, [P, C], U32, "slot_words_last_" + n)
+            slot_scales[j][(LAST, E)] = at(ROUND2 + 3 * 4 * C + j * C, [P, C], U8, "slot_scales_last_" + n)
+        wk_plane = sb([P, E, K], U8, "wk_plane")
+        wv_plane = sb([P, E, K], U8, "wv_plane")
+        wk_pairs = [at(WK01, [P, 2, 2 * K], U8, "wk_pair0"), sb([P, 2, 2 * K], U8, "wk_pair1")]
+        wv_codes = [sb([P, K], U32, "wv_codes%d" % e) for e in range(E)]
+
         pieces = [(e, 0, K) for e in range(LAST)] + [(LAST, ct * P, (ct + 1) * P) for ct in range(CT)]
-        grouped = {pieces[0]: sb([P, K, 4], BF16, "grp0"), pieces[1]: at(24 * KIB, [P, K, 4], BF16, "grp1"),
-                   pieces[2]: at(12 * KIB, [P, K, 4], BF16, "grp2")}
-        for g, kib in zip(pieces[LAST:], (32, 44, 45, 46)):
-            grouped[g] = at(kib * KIB, [P, P, 4], BF16, "grp_last%d" % g[1])
-        wqw = {g: sb([P, g[2] - g[1]], U32, "wqw%d_%d" % g[:2]) for g in pieces if g[0] != 2}
-        wqw[pieces[2]] = at(2 * KIB, [P, K], U32, "wqw2")
-        wqs = {g: sb([P, g[2] - g[1]], U8, "wqs%d_%d" % g[:2]) for g in pieces if g not in pieces[2:4]}
-        wqs[pieces[2]] = at(20 * KIB, [P, K], U8, "wqs2")
-        wqs[pieces[LAST]] = at(5 * KIB // 2, [P, P], U8, "wqs_last0")
+        rounded = {pieces[0]: sb([P, K, 4], BF16, "rounded0"), pieces[1]: at(RAW0, [P, K, 4], BF16, "rounded1"),
+                   pieces[THIRD]: at(ROUND2, [P, K, 4], BF16, "rounded2")}
+        for g in pieces[LAST:-1]:
+            rounded[g] = sb([P, P, 4], BF16, "rounded_last%d" % g[1])
+        rounded[pieces[-1]] = at(ROUND3, [P, P, 4], BF16, "rounded_end")
+        wq_codes = {g: sb([P, g[2] - g[1]], U32, "wq_codes%d_%d" % g[:2]) for g in pieces if g[0] != THIRD}
+        wq_codes[pieces[THIRD]] = at(WQ2, [P, K], U32, "wq_codes2")
+        wq_plane = {g: sb([P, g[2] - g[1]], U8, "wq_plane%d_%d" % g[:2]) for g in pieces if g not in pieces[THIRD:E]}
+        wq_plane[pieces[THIRD]] = at(WK01, [P, K], U8, "wq_plane2")
+        wq_plane[pieces[LAST]] = at(WQ2, [P, P], U8, "wq_plane_last0")
         gate_rows = sb([P, P], F32, "gate_rows")
-        gate_col = at(10 * KIB, [P, 2 * E], F32, "gate_col")
+        gate_col = at(RAW1, [P, 2 * LAST], F32, "gate_col")
         gate_tail = sb([P, 2 * C], F32, "gate_tail")
         ident = sb([P, P], F32, "ident")
-        by_slot = [sb([P, K], F32, "by_slot%d" % s) for s in range(2 * E)]
+        by_slot = [sb([P, K], F32, "by_slot%d" % s) for s in range(2 * LAST)]
         dx = [sb([P, S], F32, "dx%d" % ct) for ct in range(CT)]
-        first = [at(46 * KIB, [P, T], F32, "first0")] + [sb([P, T], F32, "first%d" % ct) for ct in range(1, CT)]
+        first = [at(ROUND3, [P, T], F32, "first0")] + [sb([P, T], F32, "first%d" % ct) for ct in range(1, CT)]
         res = [sb([P, T], F32, "res%d" % ct) for ct in range(CT)]
 
-        def load_words(j):
-            nc.sync.dma_start(gw[j][:, 0:T].bitcast(I32), g_words_in[j][0].rearrange("p t d -> p (t d)").bitcast(I32))
+        def load_grad_words(j):
+            words = grad_words_in[j][0].rearrange("p t d -> p (t d)").bitcast(I32)
+            nc.sync.dma_start(grad_words[j][:, 0:T].bitcast(I32), words)
 
-        def load_scales(j, q):
-            rows = g_scales_in[j][0][4 * q:4 * q + 4, :].bitcast(I32)
-            nc.sync.dma_start(gs[j][32 * q:32 * q + 4, 0:T].bitcast(I32), rows)
+        def load_grad_scales(j, q0, q1):
+            for q in range(q0, q1):
+                rows = grad_scales_in[j][0][4 * q:4 * q + 4, :].bitcast(I32)
+                nc.sync.dma_start(grad_scales[j][32 * q:32 * q + 4, 0:T].bitcast(I32), rows)
 
-        def load_weight_scales(j, r0, r1):
-            plane, src = (wks, wk_scales) if j == 1 else (wvs, wv_scales)
-            rows = src.rearrange("e s (q r) c -> r q (e s) c", r=4)
+        def load_plane(queue, plane, first_row, scales, r0, r1):
+            rows = scales.rearrange("e s (q r) c -> r q (e s) c", r=4)
             for r in range(r0, r1):
-                (nc.gpsimd if j == 1 else nc.sync).dma_start(plane[WEIGHT_ROW[j] + r:P:32, :, :].bitcast(I32), rows[r].bitcast(I32))
+                queue.dma_start(plane[first_row + r:P:32, :, :].bitcast(I32), rows[r].bitcast(I32))
 
-        def wq_rows(e):
-            return wq[e].rearrange("(p j) c -> p j c", j=4)
+        def load_wq(e):
+            nc.sync.dma_start(raw[e][:], wq[e].rearrange("(p j) c -> p j c", j=4))
 
-        def load_wk(h):
-            kw = wk_words.rearrange("e s p b -> p (e s) b")[:, 2 * h:2 * h + 2, :]
-            nc.sync.dma_start(wkw[h][:].bitcast(I32), kw.bitcast(I32))
+        def load_wk(pair):
+            words = wk_words.rearrange("e s p b -> p (e s) b")[:, 2 * pair:2 * pair + 2, :]
+            nc.sync.dma_start(wk_pairs[pair][:].bitcast(I32), words.bitcast(I32))
 
         def load_wv(e):
-            nc.sync.dma_start(wvw[e][:].bitcast(I32), wv_words[e, 0].rearrange("p c d -> p (c d)").bitcast(I32))
+            nc.sync.dma_start(wv_codes[e][:].bitcast(I32), wv_words[e, 0].rearrange("p c d -> p (c d)").bitcast(I32))
 
         for j in range(3):
-            nc.vector.memset(gs[j][:, 0:T].bitcast(I32), 0)
+            nc.vector.memset(grad_scales[j][:, 0:T].bitcast(I32), 0)
         nc.gpsimd.dma_start(gate_rows[:], gate.rearrange("a (s p) -> (a s) p", p=P)[0:P, :])
-        load_weight_scales(1, 0, 4)
+        load_plane(nc.gpsimd, wk_plane, 0, wk_scales, 0, 4)
         make_identity(nc, ident[:])
-        load_words(0)
+        load_grad_words(QP)
         nc.sync.dma_start(offs_t[:], offs)
-        load_words(1)
-        nc.sync.dma_start(raw[0][:], wq_rows(0))
-        load_words(2)
-        for q in range(4):
-            load_scales(0, q)
-        nc.sync.dma_start(raw[1][:], wq_rows(1))
-        for q in range(4):
-            load_scales(1, q)
-        for q in range(2):
-            load_scales(2, q)
-        nc.sync.dma_start(raw[2][:], wq_rows(2))
-        for q in range(2, 4):
-            load_scales(2, q)
+        load_grad_words(KP)
+        load_wq(0)
+        load_grad_words(VP)
+        load_grad_scales(QP, 0, 4)
+        load_wq(1)
+        load_grad_scales(KP, 0, 4)
+        load_grad_scales(VP, 0, 2)
+        load_wq(THIRD)
+        load_grad_scales(VP, 2, 4)
         load_wk(0)
-        load_weight_scales(2, 0, 1)
+        load_plane(nc.sync, wv_plane, WV_ROW, wv_scales, 0, 1)
         load_wv(0)
-        load_weight_scales(2, 1, 2)
+        load_plane(nc.sync, wv_plane, WV_ROW, wv_scales, 1, 2)
         load_wv(1)
-        load_weight_scales(2, 2, 4)
+        load_plane(nc.sync, wv_plane, WV_ROW, wv_scales, 2, 4)
         load_wk(1)
-        load_wv(2)
-        nc.sync.dma_start(raw_last[0][:], wq_rows(LAST)[:, :, 0:P])
-        load_wv(3)
-        nc.sync.dma_start(gate_tail[:], gate[:, 2 * C:S])
+        load_wv(THIRD)
+        load_wq(LAST)
+        load_wv(LAST)
+        nc.sync.dma_start(gate_tail[:], gate[:, THIRD * C:S])
         nc.sync.dma_start(pos_t[0][:], pos1)
-        nc.sync.dma_start(raw_last[1][:], wq_rows(LAST)[:, :, P:K])
         nc.sync.dma_start(pos_t[1][:], pos2)
 
         def run_of(runs, e):
             return [r for r in runs if r[0] <= e < r[1]][0]
 
+        def offsets_of(run):
+            return offs_t[:, run[0] * C // 16:run[1] * C // 16]
+
         def gather_words(j, e):
-            r = run_of(word_runs, e)
-            nc.vector.tensor_copy(sw[j][r][:], gw[j][:].indirect(offs_t[:, r[0] * C // 16:r[1] * C // 16]))
+            run = run_of(word_runs, e)
+            nc.vector.tensor_copy(slot_words[j][run][:], grad_words[j][:].indirect(offsets_of(run)))
 
         def gather_scales(j, e):
-            r = run_of(scale_runs[j], e)
-            nc.vector.tensor_copy(ss[j][r][:], gs[j][:].indirect(offs_t[:, r[0] * C // 16:r[1] * C // 16]))
+            run = run_of(scale_runs[j], e)
+            nc.vector.tensor_copy(slot_scales[j][run][:], grad_scales[j][:].indirect(offsets_of(run)))
 
         def cast(g):
-            if g[0] < LAST:
-                rows = raw[g[0]][:]
-            elif g[1] == 0:
-                rows = raw_last[0][:]
+            rows = raw[g[0]][:, :, g[1]:g[2]]
+            if g in pieces[-2:]:
+                nc.gpsimd.tensor_copy(rounded[g][:], rows.rearrange("p j c -> p c j"))
             else:
-                rows = raw_last[1][:, :, g[1] - P:g[2] - P]
-                nc.gpsimd.tensor_copy(grouped[g][:], rows.rearrange("p j c -> p c j"))
-                return
-            nc.scalar.copy(
-                grouped[g][:].rearrange("p (c i) j -> p c j i", i=4),
-                rows.rearrange("p j (c i) -> p c j i", i=4),
-            )
+                nc.scalar.copy(rounded[g][:].rearrange("p (c i) j -> p c j i", i=4),
+                               rows.rearrange("p j (c i) -> p c j i", i=4))
 
         def quantize(g):
-            nc.vector.quantize_mx(
-                out=wqw[g][:].bitcast(FP8X4),
-                scales=wqs[g][:],
-                in_=grouped[g][:].rearrange("p c j -> p (c j)"),
-            )
+            nc.vector.quantize_mx(out=wq_codes[g][:].bitcast(FP8X4), scales=wq_plane[g][:],
+                                  in_=rounded[g][:].rearrange("p c j -> p (c j)"))
 
         def weights(j, e, c0, c1):
-            if j == 0:
-                g = [g for g in pieces if g[0] == e and g[1] <= c0 < g[2]][0]
-                return wqw[g][:, c0 - g[1]:c1 - g[1]].bitcast(FP8X4), wqs[g][:, c0 - g[1]:c1 - g[1]]
-            if j == 1:
-                return wkw[e // 2][:, e % 2, 2 * c0:2 * c1].bitcast(FP4X4), wks[:, e, c0:c1]
-            return wvw[e][:, c0:c1].bitcast(FP8X4), wvs[WEIGHT_ROW[2]:P, e, c0:c1]
+            if j == QP:
+                g = [piece for piece in pieces if piece[0] == e and piece[1] <= c0 < piece[2]][0]
+                return wq_codes[g][:, c0 - g[1]:c1 - g[1]].bitcast(FP8X4), wq_plane[g][:, c0 - g[1]:c1 - g[1]]
+            if j == KP:
+                return wk_pairs[e // 2][:, e % 2, 2 * c0:2 * c1].bitcast(FP4X4), wk_plane[:, e, c0:c1]
+            return wv_codes[e][:, c0:c1].bitcast(FP8X4), wv_plane[WV_ROW:P, e, c0:c1]
 
         def slots(j, e, u0, u1):
-            rw, rs = run_of(word_runs, e), run_of(scale_runs[j], e)
-            bw, bs = (e - rw[0]) * C, (e - rs[0]) * C
-            return sw[j][rw][:, bw + u0:bw + u1].bitcast(FP8X4), ss[j][rs][:, bs + u0:bs + u1]
+            word_run, scale_run = run_of(word_runs, e), run_of(scale_runs[j], e)
+            w0, s0 = (e - word_run[0]) * C, (e - scale_run[0]) * C
+            return (slot_words[j][word_run][:, w0 + u0:w0 + u1].bitcast(FP8X4),
+                    slot_scales[j][scale_run][:, s0 + u0:s0 + u1])
 
-        def product_by_slot(e, h, passes):
+        def product_by_slot(s, passes):
+            e, h = divmod(s, 2)
             acc = mm.tile([P, K], F32, name="acc")
             for n, (j, c0, c1) in enumerate(passes):
                 a, a_s = slots(j, e, h * P, (h + 1) * P)
                 b, b_s = weights(j, e, c0, c1)
                 nc.tensor.matmul_mx(out=acc[:, c0:c1], lhsT=a, lhsT_scale=a_s, rhs=b, rhs_scale=b_s,
                                     start=(n == 0), stop=(n == len(passes) - 1))
-            return acc
-
-        def gate_by_slot(s, acc, c0, c1):
-            nc.scalar.activation(by_slot[s][:, c0:c1], acc[:, c0:c1], COPY, scale=gate_col[:, s:s + 1])
-
-        def turn_half(ct, h, experts):
-            bank = tr.tile([P, K], F32, name="bank")
-            for e in range(experts):
-                nc.tensor.transpose(bank[:, e * P:(e + 1) * P], by_slot[2 * e + h][:, ct * P:(ct + 1) * P], ident[:])
-            nc.scalar.copy(
-                dx[ct][:].rearrange("p (e h u) -> p h e u", h=2, u=P)[:, h, 0:experts, :],
-                bank[:, 0:experts * P].rearrange("p (e u) -> p e u", u=P),
-            )
-
-        def turn(ct, s0, s1):
-            bank = tr.tile([P, K], F32, name="bank")
-            for s in range(s0, s1):
-                nc.tensor.transpose(bank[:, (s - s0) * P:(s - s0 + 1) * P], by_slot[s][:, ct * P:(ct + 1) * P], ident[:])
-            nc.scalar.copy(dx[ct][:, s0 * P:s1 * P], bank[:, 0:(s1 - s0) * P])
+            c0 = passes[0][1]
+            nc.scalar.activation(by_slot[s][:, c0:K], acc[:, c0:K], COPY, scale=gate_col[:, s:s + 1])
 
         def product_by_feature(e, ct, acc):
-            passes = ((0, 0, C), (1, 0, P), (1, P, C), (2, 0, C))
+            passes = ((QP, 0, C), (KP, 0, P), (KP, P, C), (VP, 0, C))
             for n, (j, u0, u1) in enumerate(passes):
                 a, a_s = weights(j, e, ct * P, (ct + 1) * P)
                 b, b_s = slots(j, e, u0, u1)
                 nc.tensor.matmul_mx(out=acc[:, u0:u1], lhsT=a, lhsT_scale=a_s, rhs=b, rhs_scale=b_s,
                                     start=(n == 0), stop=(n == len(passes) - 1))
+
+        def transposed(ct, slot_tiles):
+            bank = tr.tile([P, K], F32, name="bank")
+            for i, s in enumerate(slot_tiles):
+                nc.tensor.transpose(bank[:, i * P:(i + 1) * P], by_slot[s][:, ct * P:(ct + 1) * P], ident[:])
+            return bank
+
+        def turn_half(ct, h):
+            bank = transposed(ct, range(h, 2 * LAST, 2))
+            nc.scalar.copy(dx[ct][:].rearrange("p (e h u) -> p h e u", h=2, u=P)[:, h, 0:LAST, :],
+                           bank[:, 0:LAST * P].rearrange("p (e u) -> p e u", u=P))
 
         def fetch(ct):
             nc.vector.tensor_copy(first[ct][:], dx[ct][:].indirect(pos_t[0][:]))
@@ -231,51 +224,52 @@ def tile_moe_qkb_kernel(
                                     first[ct][:, t0:t1], ADD)
             nc.sync.dma_start(out[ct * P:(ct + 1) * P, t0:t1], res[ct][:, t0:t1])
 
-        for j in range(3):
+        for j in (QP, KP, VP):
             gather_words(j, 0)
         for g in pieces[:LAST]:
             cast(g)
         gate_bank = tr.tile([P, K], F32, name="bank")
         nc.tensor.transpose(gate_bank[:, 0:P], gate_rows[:], ident[:])
-        nc.scalar.copy(gate_col[:], gate_bank[:, 0:2 * E])
-
-        gather_scales(0, 0)
+        nc.scalar.copy(gate_col[:], gate_bank[:, 0:2 * LAST])
+        gather_scales(QP, 0)
         quantize(pieces[0])
-        gather_scales(1, 0)
+        gather_scales(KP, 0)
         quantize(pieces[1])
-        gather_scales(2, 0)
-        for s in range(4):
-            gate_by_slot(s, product_by_slot(s // 2, s % 2, ((0, 0, K), (1, 0, K), (2, 0, K))), 0, K)
-        gather_scales(2, 2)
-        quantize(pieces[2])
-        turn(0, 0, 4)
-        cast(pieces[LAST])
+        gather_scales(VP, 0)
+        for s in range(2 * THIRD):
+            product_by_slot(s, [(j, 0, K) for j in (QP, KP, VP)])
+
+        gather_scales(VP, THIRD)
+        quantize(pieces[THIRD])
+        nc.scalar.copy(dx[0][:, 0:THIRD * C], transposed(0, range(2 * THIRD))[:])
+        for g in pieces[LAST:]:
+            cast(g)
         tail = tr.tile([P, K], F32, name="bank")
-        product_by_feature(2, 0, tail[:, 0:C])
+        product_by_feature(THIRD, 0, tail[:, 0:C])
         wide = ((P, 3 * P), (3 * P, K))
         narrow = tuple((ct * P, (ct + 1) * P) for ct in range(1, CT))
-        for s in range(4, 6):
-            acc = product_by_slot(2, s % 2, [(j,) + c for j, cuts in ((2, wide), (1, narrow), (0, wide)) for c in cuts])
-            gate_by_slot(s, acc, P, K)
-        for j in range(3):
+        for s in range(2 * THIRD, 2 * LAST):
+            product_by_slot(s, [(j,) + cut for j, cuts in ((VP, wide), (KP, narrow), (QP, wide)) for cut in cuts])
+
+        for j in (QP, KP, VP):
             gather_words(j, LAST)
             gather_scales(j, LAST)
         quantize(pieces[LAST])
         product_by_feature(LAST, 0, tail[:, C:2 * C])
         for g in pieces[LAST + 1:]:
-            cast(g)
             quantize(g)
-        nc.vector.tensor_tensor(dx[0][:, 2 * C:S], tail[:], gate_tail[:], MULT)
+        nc.vector.tensor_tensor(dx[0][:, THIRD * C:S], tail[:], gate_tail[:], MULT)
         fetch(0)
-        for h in range(2):
-            turn_half(1, h, LAST)
-        for s in range(6, 8):
-            acc = product_by_slot(LAST, s % 2, [(j,) + c for j, cuts in ((2, wide), (1, narrow), (0, narrow)) for c in cuts])
-            gate_by_slot(s, acc, P, K)
-        turn(1, 6, 8)
-        for ct in range(2, CT):
+        pair = mm.tile([P, K], F32, name="acc")
+        lone = mm.tile([P, K], F32, name="acc")
+        sums = {1: pair[:, 0:C], 2: pair[:, C:2 * C], 3: lone[:, 0:C]}
+        for ct in range(1, CT):
+            product_by_feature(LAST, ct, sums[ct])
+        for ct in range(1, CT):
+            nc.vector.tensor_tensor(dx[ct][:, LAST * C:S], sums[ct], gate_tail[:, C:2 * C], MULT)
             for h in range(2):
-                turn_half(ct, h, E)
+                turn_half(ct, h)
+
         fetch_add(0, 0, T)
         for ct in range(1, CT - 1):
             fetch(ct)

@@ -146,6 +146,8 @@ def tile_moe_qkb_kernel(
         nc.sync.dma_start(pos_t[0][:], pos1)
         nc.sync.dma_start(pos_t[1][:], pos2)
 
+        halves = ((0, T // 2), (T // 2, T))
+
         def run_of(runs, e):
             return [r for r in runs if r[0] <= e < r[1]][0]
 
@@ -217,11 +219,14 @@ def tile_moe_qkb_kernel(
                            bank[:, 0:LAST * P].rearrange("p (e u) -> p e u", u=P))
 
         def fetch(ct):
-            nc.vector.tensor_copy(first[ct][:], dx[ct][:].indirect(pos_t[0][:]))
+            for t0, t1 in halves:
+                nc.vector.tensor_copy(first[ct][:, t0:t1], dx[ct][:].indirect(pos_t[0][:, t0 // 16:t1 // 16]))
 
         def fetch_add(ct, t0, t1):
             nc.vector.tensor_tensor(res[ct][:, t0:t1], dx[ct][:].indirect(pos_t[1][:, t0 // 16:t1 // 16]),
                                     first[ct][:, t0:t1], ADD)
+
+        def store(ct, t0, t1):
             nc.sync.dma_start(out[ct * P:(ct + 1) * P, t0:t1], res[ct][:, t0:t1])
 
         for j in (QP, KP, VP):
@@ -270,10 +275,12 @@ def tile_moe_qkb_kernel(
             for h in range(2):
                 turn_half(ct, h)
 
-        fetch_add(0, 0, T)
-        for ct in range(1, CT - 1):
-            fetch(ct)
-            fetch_add(ct, 0, T)
-        fetch(CT - 1)
-        fetch_add(CT - 1, 0, T // 2)
-        fetch_add(CT - 1, T // 2, T)
+        for ct in range(CT):
+            if ct > 0:
+                fetch(ct)
+            for t0, t1 in halves:
+                fetch_add(ct, t0, t1)
+                if ct == CT - 1:
+                    store(ct, t0, t1)
+            if ct < CT - 1:
+                store(ct, 0, T)

@@ -22,11 +22,10 @@ ADD = mybir.AluOpType.add
 P = 128
 CT = K // P
 QP, KP, VP = 0, 1, 2
-THIRD, LAST = E - 2, E - 1
+EARLY, LATE = (0, 1), (2, 3)
+H = S // 2
 KIB = 1024
-WINDOW = 2 * T
 WV_ROW = 4
-BANKS = 4
 
 
 def tile_moe_qkb_kernel(
@@ -37,8 +36,10 @@ def tile_moe_qkb_kernel(
     with ExitStack() as ctx:
         keep = ctx.enter_context(tc.tile_pool(name="keep", bufs=1))
         reuse = ctx.enter_context(tc.tile_pool(name="reuse", bufs=1))
-        mm = ctx.enter_context(tc.psum_pool(name="mm", bufs=BANKS))
-        tr = ctx.enter_context(tc.psum_pool(name="tr", bufs=BANKS))
+        psum = ctx.enter_context(tc.psum_pool(name="psum", bufs=1))
+
+        def bank(n):
+            return psum.tile([P, K], F32, name="bank%d" % n)
 
         def sb(shape, dtype, name):
             return keep.tile(shape, dtype, name=name, align_bytes=64)
@@ -46,51 +47,45 @@ def tile_moe_qkb_kernel(
         def at(offset, shape, dtype, name):
             return reuse.tile(shape, dtype, name=name, align_bytes=64, offset=offset)
 
-        WQ2, ROUND3, WK01, RAW1, RAW0 = 0, 2 * KIB, 4 * KIB, 8 * KIB, 16 * KIB
-        ROUND2 = RAW1 + 4 * KIB
+        RAW = [8 * KIB * e for e in range(E)]
+        GATE0 = RAW[1] + 2 * KIB
+        REST3 = 32 * KIB
 
         offs_t = keep.tile([P, S // 16], U16, name="offs_t")
         pos_t = [keep.tile([P, T // 16], U16, name="pos%d" % i) for i in range(2)]
         names = ("q", "k", "v")
         grad_words_in = (dq_words, dk_words, dv_words)
         grad_scales_in = (dq_scales, dk_scales, dv_scales)
-        grad_words = [sb([P, WINDOW], U32, "grad_words_" + n) for n in names]
-        grad_scales = [sb([P, WINDOW], U8, "grad_scales_" + n) for n in names]
-
-        word_runs = ((0, LAST), (LAST, E))
-        scale_runs = (word_runs, word_runs, ((0, THIRD), (THIRD, LAST), (LAST, E)))
-        raw = [at(RAW0, [P, 4, K], F32, "raw0"), at(RAW1, [P, 4, K], F32, "raw1")]
-        raw += [sb([P, 4, K], F32, "raw%d" % e) for e in (THIRD, LAST)]
-        slot_words = [{word_runs[0]: sb([P, LAST * C], U32, "slot_words_" + n)} for n in names]
-        slot_scales = [{r: sb([P, (r[1] - r[0]) * C], U8, "slot_scales_%s%d" % (n, r[0])) for r in scale_runs[j][:-1]}
-                       for j, n in enumerate(names)]
-        for j, n in enumerate(names):
-            slot_words[j][(LAST, E)] = at(ROUND2 + j * 4 * C, [P, C], U32, "slot_words_last_" + n)
-            slot_scales[j][(LAST, E)] = at(ROUND2 + 3 * 4 * C + j * C, [P, C], U8, "slot_scales_last_" + n)
+        grad_words = [sb([P, 3 * T], U32, "grad_words_" + n) for n in names]
+        grad_scales = [sb([P, 2 * T], U8, "grad_scales_" + n) for n in names]
+        raw = [at(RAW[e], [P, 4, K], F32, "raw%d" % e) for e in range(E)]
+        rounded = [sb([P, K, 4], BF16, "rounded%d" % e) for e in EARLY]
+        rounded_late = sb([P, CT, 2, P, 4], BF16, "rounded_late")
+        slot_words = [sb([P, S], U32, "slot_words_" + n) for n in names]
+        slot_scales = [
+            [sb([P, H], U8, "slot_scales_q0"), at(RAW[2], [P, H], U8, "slot_scales_q1")],
+            [at(RAW[1] + 4 * KIB, [P, H], U8, "slot_scales_k0"), at(RAW[2] + H, [P, H], U8, "slot_scales_k1")],
+            [at(RAW[1] + KIB, [P, H], U8, "slot_scales_v0"), at(GATE0, [P, H], U8, "slot_scales_v1")],
+        ]
         wk_plane = sb([P, E, K], U8, "wk_plane")
         wv_plane = sb([P, E, K], U8, "wv_plane")
-        wk_pairs = [at(WK01, [P, 2, 2 * K], U8, "wk_pair0"), sb([P, 2, 2 * K], U8, "wk_pair1")]
+        wk_pairs = [sb([P, 2, 2 * K], U8, "wk_pair%d" % i) for i in range(2)]
         wv_codes = [sb([P, K], U32, "wv_codes%d" % e) for e in range(E)]
-
-        pieces = [(e, 0, K) for e in range(LAST)] + [(LAST, ct * P, (ct + 1) * P) for ct in range(CT)]
-        rounded = {pieces[0]: sb([P, K, 4], BF16, "rounded0"), pieces[1]: at(RAW0, [P, K, 4], BF16, "rounded1"),
-                   pieces[THIRD]: at(ROUND2, [P, K, 4], BF16, "rounded2")}
-        for g in pieces[LAST:-1]:
-            rounded[g] = sb([P, P, 4], BF16, "rounded_last%d" % g[1])
-        rounded[pieces[-1]] = at(ROUND3, [P, P, 4], BF16, "rounded_end")
-        wq_codes = {g: sb([P, g[2] - g[1]], U32, "wq_codes%d_%d" % g[:2]) for g in pieces if g[0] != THIRD}
-        wq_codes[pieces[THIRD]] = at(WQ2, [P, K], U32, "wq_codes2")
-        wq_plane = {g: sb([P, g[2] - g[1]], U8, "wq_plane%d_%d" % g[:2]) for g in pieces if g not in pieces[THIRD:E]}
-        wq_plane[pieces[THIRD]] = at(WK01, [P, K], U8, "wq_plane2")
-        wq_plane[pieces[LAST]] = at(WQ2, [P, P], U8, "wq_plane_last0")
+        wq_codes = [sb([P, K], U32, "wq_codes%d" % e) for e in EARLY]
+        wq_plane = [sb([P, K], U8, "wq_plane%d" % e) for e in EARLY]
+        late_codes = [sb([P, 2 * P], U32, "late_codes%d" % ct) for ct in range(CT)]
+        late_plane = [at(GATE0 + H + ct * 2 * P, [P, 2 * P], U8, "late_plane%d" % ct) for ct in range(CT)]
         gate_rows = sb([P, P], F32, "gate_rows")
-        gate_col = at(RAW1, [P, 2 * LAST], F32, "gate_col")
-        gate_tail = sb([P, 2 * C], F32, "gate_tail")
+        gate_col = at(RAW[1], [P, 2 * E], F32, "gate_col")
+        gate_first = at(GATE0, [P, 3 * P], F32, "gate_first")
+        gate_tail = sb([P, H], F32, "gate_tail")
         ident = sb([P, P], F32, "ident")
-        by_slot = [sb([P, K], F32, "by_slot%d" % s) for s in range(2 * LAST)]
+        head = sb([P, 4, P], F32, "head")
+        rest = [sb([P, K - P], F32, "rest%d" % s) for s in range(3)] + [at(REST3, [P, K - P], F32, "rest3")]
+        late = {ct: sb([P, 4, P], F32, "late%d" % ct) for ct in range(1, CT)}
         dx = [sb([P, S], F32, "dx%d" % ct) for ct in range(CT)]
-        first = [at(ROUND3, [P, T], F32, "first0")] + [sb([P, T], F32, "first%d" % ct) for ct in range(1, CT)]
-        res = [sb([P, T], F32, "res%d" % ct) for ct in range(CT)]
+        first = [sb([P, T], F32, "first%d" % ct) for ct in range(CT)]
+        res = [at(REST3, [P, T], F32, "res1") if ct == 1 else sb([P, T], F32, "res%d" % ct) for ct in range(CT)]
 
         def load_grad_words(j):
             words = grad_words_in[j][0].rearrange("p t d -> p (t d)").bitcast(I32)
@@ -118,169 +113,175 @@ def tile_moe_qkb_kernel(
 
         for j in range(3):
             nc.vector.memset(grad_scales[j][:, 0:T].bitcast(I32), 0)
-        nc.gpsimd.dma_start(gate_rows[:], gate.rearrange("a (s p) -> (a s) p", p=P)[0:P, :])
-        load_plane(nc.gpsimd, wk_plane, 0, wk_scales, 0, 4)
         make_identity(nc, ident[:])
+        load_plane(nc.gpsimd, wk_plane, 0, wk_scales, 0, 4)
         load_grad_words(QP)
         nc.sync.dma_start(offs_t[:], offs)
         load_grad_words(KP)
         load_wq(0)
         load_grad_words(VP)
+        nc.sync.dma_start(gate_rows[:], gate.rearrange("a (s p) -> (a s) p", p=P)[0:P, :])
         load_grad_scales(QP, 0, 4)
         load_wq(1)
         load_grad_scales(KP, 0, 4)
         load_grad_scales(VP, 0, 2)
-        load_wq(THIRD)
+        load_wq(2)
         load_grad_scales(VP, 2, 4)
+        load_plane(nc.sync, wv_plane, WV_ROW, wv_scales, 0, 2)
         load_wk(0)
-        load_plane(nc.sync, wv_plane, WV_ROW, wv_scales, 0, 1)
-        load_wv(0)
-        load_plane(nc.sync, wv_plane, WV_ROW, wv_scales, 1, 2)
-        load_wv(1)
+        load_wq(3)
         load_plane(nc.sync, wv_plane, WV_ROW, wv_scales, 2, 4)
+        load_wv(0)
+        load_wv(1)
         load_wk(1)
-        load_wv(THIRD)
-        load_wq(LAST)
-        load_wv(LAST)
-        nc.sync.dma_start(gate_tail[:], gate[:, THIRD * C:S])
+        load_wv(2)
+        load_wv(3)
+        nc.sync.dma_start(gate_tail[:], gate[:, H:S])
         nc.sync.dma_start(pos_t[0][:], pos1)
         nc.sync.dma_start(pos_t[1][:], pos2)
 
-        halves = ((0, T // 2), (T // 2, T))
+        def gather_words(j):
+            nc.vector.tensor_copy(slot_words[j][:], grad_words[j][:].indirect(offs_t[:]))
 
-        def run_of(runs, e):
-            return [r for r in runs if r[0] <= e < r[1]][0]
+        def gather_scales(j, half):
+            offsets = offs_t[:, half * H // 16:(half + 1) * H // 16]
+            nc.vector.tensor_copy(slot_scales[j][half][:], grad_scales[j][:].indirect(offsets))
 
-        def offsets_of(run):
-            return offs_t[:, run[0] * C // 16:run[1] * C // 16]
-
-        def gather_words(j, e):
-            run = run_of(word_runs, e)
-            nc.vector.tensor_copy(slot_words[j][run][:], grad_words[j][:].indirect(offsets_of(run)))
-
-        def gather_scales(j, e):
-            run = run_of(scale_runs[j], e)
-            nc.vector.tensor_copy(slot_scales[j][run][:], grad_scales[j][:].indirect(offsets_of(run)))
-
-        def cast(g):
-            rows = raw[g[0]][:, :, g[1]:g[2]]
-            if g in pieces[-2:]:
-                nc.gpsimd.tensor_copy(rounded[g][:], rows.rearrange("p j c -> p c j"))
+        def cast(e):
+            if e in EARLY:
+                dst = rounded[e][:].rearrange("p (t c i) j -> p t c j i", t=CT, i=4)
             else:
-                nc.scalar.copy(rounded[g][:].rearrange("p (c i) j -> p c j i", i=4),
-                               rows.rearrange("p j (c i) -> p c j i", i=4))
+                dst = rounded_late[:, :, e - 2, :, :].rearrange("p t (c i) j -> p t c j i", i=4)
+            nc.scalar.copy(dst, raw[e][:].rearrange("p j (t c i) -> p t c j i", t=CT, i=4))
 
-        def quantize(g):
-            nc.vector.quantize_mx(out=wq_codes[g][:].bitcast(FP8X4), scales=wq_plane[g][:],
-                                  in_=rounded[g][:].rearrange("p c j -> p (c j)"))
+        def quantize(codes, plane, values):
+            nc.vector.quantize_mx(out=codes[:].bitcast(FP8X4), scales=plane[:], in_=values)
+
+        def quantize_early(e):
+            quantize(wq_codes[e], wq_plane[e], rounded[e][:].rearrange("p c j -> p (c j)"))
+
+        def quantize_late(ct):
+            quantize(late_codes[ct], late_plane[ct], rounded_late[:, ct, :, :, :].rearrange("p e c j -> p (e c j)"))
 
         def weights(j, e, c0, c1):
+            if j == QP and e in EARLY:
+                return wq_codes[e][:, c0:c1].bitcast(FP8X4), wq_plane[e][:, c0:c1]
             if j == QP:
-                g = [piece for piece in pieces if piece[0] == e and piece[1] <= c0 < piece[2]][0]
-                return wq_codes[g][:, c0 - g[1]:c1 - g[1]].bitcast(FP8X4), wq_plane[g][:, c0 - g[1]:c1 - g[1]]
+                ct, cols = c0 // P, slice((e - 2) * P, (e - 1) * P)
+                return late_codes[ct][:, cols].bitcast(FP8X4), late_plane[ct][:, cols]
             if j == KP:
                 return wk_pairs[e // 2][:, e % 2, 2 * c0:2 * c1].bitcast(FP4X4), wk_plane[:, e, c0:c1]
             return wv_codes[e][:, c0:c1].bitcast(FP8X4), wv_plane[WV_ROW:P, e, c0:c1]
 
-        def slots(j, e, u0, u1):
-            word_run, scale_run = run_of(word_runs, e), run_of(scale_runs[j], e)
-            w0, s0 = (e - word_run[0]) * C, (e - scale_run[0]) * C
-            return (slot_words[j][word_run][:, w0 + u0:w0 + u1].bitcast(FP8X4),
-                    slot_scales[j][scale_run][:, s0 + u0:s0 + u1])
+        def slots(j, u0, u1):
+            half = u0 // H
+            return slot_words[j][:, u0:u1].bitcast(FP8X4), slot_scales[j][half][:, u0 - half * H:u1 - half * H]
 
-        def product_by_slot(s, passes):
-            e, h = divmod(s, 2)
-            acc = mm.tile([P, K], F32, name="acc")
-            for n, (j, c0, c1) in enumerate(passes):
-                a, a_s = slots(j, e, h * P, (h + 1) * P)
-                b, b_s = weights(j, e, c0, c1)
-                nc.tensor.matmul_mx(out=acc[:, c0:c1], lhsT=a, lhsT_scale=a_s, rhs=b, rhs_scale=b_s,
-                                    start=(n == 0), stop=(n == len(passes) - 1))
-            c0 = passes[0][1]
-            nc.scalar.activation(by_slot[s][:, c0:K], acc[:, c0:K], COPY, scale=gate_col[:, s:s + 1])
+        def mx(acc, stationary, moving, start, stop):
+            nc.tensor.matmul_mx(out=acc, lhsT=stationary[0], lhsT_scale=stationary[1], rhs=moving[0],
+                                rhs_scale=moving[1], start=start, stop=stop)
 
-        def product_by_feature(e, ct, acc):
-            passes = ((QP, 0, C), (KP, 0, P), (KP, P, C), (VP, 0, C))
-            for n, (j, u0, u1) in enumerate(passes):
-                a, a_s = weights(j, e, ct * P, (ct + 1) * P)
-                b, b_s = slots(j, e, u0, u1)
-                nc.tensor.matmul_mx(out=acc[:, u0:u1], lhsT=a, lhsT_scale=a_s, rhs=b, rhs_scale=b_s,
-                                    start=(n == 0), stop=(n == len(passes) - 1))
+        def gated_copy(dst, src, gates, s):
+            nc.scalar.activation(dst, src, COPY, scale=gates[:, s:s + 1])
 
-        def transposed(ct, slot_tiles):
-            bank = tr.tile([P, K], F32, name="bank")
-            for i, s in enumerate(slot_tiles):
-                nc.tensor.transpose(bank[:, i * P:(i + 1) * P], by_slot[s][:, ct * P:(ct + 1) * P], ident[:])
-            return bank
+        def turn(ct, half, blocks, n):
+            turned = bank(n)
+            for i, block in enumerate(blocks):
+                nc.tensor.transpose(turned[:, i * P:(i + 1) * P], block, ident[:])
+            nc.scalar.copy(dx[ct][:, half * H:(half + 1) * H], turned[:])
 
-        def turn_half(ct, h):
-            bank = transposed(ct, range(h, 2 * LAST, 2))
-            nc.scalar.copy(dx[ct][:].rearrange("p (e h u) -> p h e u", h=2, u=P)[:, h, 0:LAST, :],
-                           bank[:, 0:LAST * P].rearrange("p (e u) -> p e u", u=P))
+        def turn_early(ct, n):
+            turn(ct, 0, [rest[s][:, (ct - 1) * P:ct * P] for s in range(4)], n)
 
-        def fetch(ct):
-            for t0, t1 in halves:
-                nc.vector.tensor_copy(first[ct][:, t0:t1], dx[ct][:].indirect(pos_t[0][:, t0 // 16:t1 // 16]))
+        def late_passes(acc, ct, j, start, stop):
+            for i in range(4):
+                s = 4 + i
+                mx(acc[:, i * P:(i + 1) * P], slots(j, s * P, (s + 1) * P), weights(j, s // 2, ct * P, (ct + 1) * P),
+                   start and i == 0, stop and i == 3)
+
+        def late_copies(acc, ct):
+            for i in range(4):
+                gated_copy(late[ct][:, i, :], acc[:, i * P:(i + 1) * P], gate_col, 4 + i)
+
+        def tail_passes(acc, j, start, stop):
+            width = P if j == KP else C
+            cuts = list(range(H, S, width))
+            for u0 in cuts:
+                mx(acc[:, u0 - H:u0 - H + width], weights(j, u0 // C, 0, P), slots(j, u0, u0 + width),
+                   start and u0 == cuts[0], stop and u0 == cuts[-1])
+
+        def fetch(ct, t0, t1):
+            nc.vector.tensor_copy(first[ct][:, t0:t1], dx[ct][:].indirect(pos_t[0][:, t0 // 16:t1 // 16]))
 
         def fetch_add(ct, t0, t1):
             nc.vector.tensor_tensor(res[ct][:, t0:t1], dx[ct][:].indirect(pos_t[1][:, t0 // 16:t1 // 16]),
                                     first[ct][:, t0:t1], ADD)
-
-        def store(ct, t0, t1):
             nc.sync.dma_start(out[ct * P:(ct + 1) * P, t0:t1], res[ct][:, t0:t1])
 
         for j in (QP, KP, VP):
-            gather_words(j, 0)
-        for g in pieces[:LAST]:
-            cast(g)
-        gate_bank = tr.tile([P, K], F32, name="bank")
+            gather_words(j)
+        cast(0)
+        cast(1)
+        gate_bank = bank(4)
         nc.tensor.transpose(gate_bank[:, 0:P], gate_rows[:], ident[:])
-        nc.scalar.copy(gate_col[:], gate_bank[:, 0:2 * LAST])
+        nc.scalar.copy(gate_col[:], gate_bank[:, 0:2 * E])
+        nc.scalar.copy(gate_first[:, 0:4], gate_bank[:, 0:4])
+        cast(2)
+        cast(3)
         gather_scales(QP, 0)
-        quantize(pieces[0])
+        quantize_early(0)
+        quantize_early(1)
         gather_scales(KP, 0)
-        quantize(pieces[1])
         gather_scales(VP, 0)
-        for s in range(2 * THIRD):
-            product_by_slot(s, [(j, 0, K) for j in (QP, KP, VP)])
-
-        gather_scales(VP, THIRD)
-        quantize(pieces[THIRD])
-        nc.scalar.copy(dx[0][:, 0:THIRD * C], transposed(0, range(2 * THIRD))[:])
-        for g in pieces[LAST:]:
-            cast(g)
-        tail = tr.tile([P, K], F32, name="bank")
-        product_by_feature(THIRD, 0, tail[:, 0:C])
-        wide = ((P, 3 * P), (3 * P, K))
-        narrow = tuple((ct * P, (ct + 1) * P) for ct in range(1, CT))
-        for s in range(2 * THIRD, 2 * LAST):
-            product_by_slot(s, [(j,) + cut for j, cuts in ((VP, wide), (KP, narrow), (QP, wide)) for cut in cuts])
-
+        sums = [bank(s) for s in range(4)]
         for j in (QP, KP, VP):
-            gather_words(j, LAST)
-            gather_scales(j, LAST)
-        quantize(pieces[LAST])
-        product_by_feature(LAST, 0, tail[:, C:2 * C])
-        for g in pieces[LAST + 1:]:
-            quantize(g)
-        nc.vector.tensor_tensor(dx[0][:, THIRD * C:S], tail[:], gate_tail[:], MULT)
-        fetch(0)
-        pair = mm.tile([P, K], F32, name="acc")
-        lone = mm.tile([P, K], F32, name="acc")
-        sums = {1: pair[:, 0:C], 2: pair[:, C:2 * C], 3: lone[:, 0:C]}
-        for ct in range(1, CT):
-            product_by_feature(LAST, ct, sums[ct])
-        for ct in range(1, CT):
-            nc.vector.tensor_tensor(dx[ct][:, LAST * C:S], sums[ct], gate_tail[:, C:2 * C], MULT)
-            for h in range(2):
-                turn_half(ct, h)
+            for s in range(4):
+                mx(sums[s][:], slots(j, s * P, (s + 1) * P), weights(j, s // 2, 0, K), j == QP, j == VP)
+        for s in range(4):
+            gated_copy(head[:, s, :], sums[s][:, 0:P], gate_first, s)
+        turn(0, 0, [head[:, s, :] for s in range(4)], 4)
+        for s in range(4):
+            gated_copy(rest[s][:], sums[s][:, P:K], gate_col, s)
+        turn_early(1, 1)
 
-        for ct in range(CT):
-            if ct > 0:
-                fetch(ct)
-            for t0, t1 in halves:
-                fetch_add(ct, t0, t1)
-                if ct == CT - 1:
-                    store(ct, t0, t1)
-            if ct < CT - 1:
-                store(ct, 0, T)
+        gather_scales(KP, 1)
+        gather_scales(QP, 1)
+        quantize_late(0)
+        gather_scales(VP, 1)
+        quantize_late(1)
+        quantize_late(2)
+        tail = bank(5)
+        late_sums = {1: bank(6), 2: bank(7)}
+        tail_passes(tail, KP, True, False)
+        tail_passes(tail, QP, False, False)
+        late_passes(late_sums[1], 1, KP, True, False)
+        late_passes(late_sums[2], 2, KP, True, False)
+        tail_passes(tail, VP, False, True)
+        nc.vector.tensor_tensor(dx[0][:, H:S], tail[:], gate_tail[:], MULT)
+        quantize_late(3)
+        for ct in (1, 2):
+            late_passes(late_sums[ct], ct, VP, False, False)
+            late_passes(late_sums[ct], ct, QP, False, True)
+        late_copies(late_sums[1], 1)
+        turn(1, 1, [late[1][:, i, :] for i in range(4)], 4)
+        turn_early(2, 2)
+        late_copies(late_sums[2], 2)
+        turn(2, 1, [late[2][:, i, :] for i in range(4)], 5)
+        late_sums[3] = bank(0)
+        for j in (KP, VP, QP):
+            late_passes(late_sums[3], 3, j, j == KP, j == QP)
+        late_copies(late_sums[3], 3)
+        turn_early(3, 5)
+        turn(3, 1, [late[3][:, i, :] for i in range(4)], 3)
+
+        fetch(0, 0, T)
+        fetch_add(0, 0, T)
+        fetch(1, 0, T)
+        fetch(2, 0, T)
+        fetch_add(1, 0, T)
+        fetch_add(2, 0, T)
+        parts = ((0, 3 * T // 4), (3 * T // 4, T))
+        for t0, t1 in parts:
+            fetch(3, t0, t1)
+        for t0, t1 in parts:
+            fetch_add(3, t0, t1)

@@ -60,7 +60,7 @@ def tile_moe_qkb_kernel(
         grad_scales = [sb([P, 2 * T], U8, "grad_scales_" + n) for n in names]
         raw = [at(RAW[e], [P, 4, K], F32, "raw%d" % e) for e in range(E)]
         rounded = [sb([P, K, 4], BF16, "rounded%d" % e) for e in EARLY]
-        rounded_late = sb([P, CT, 2, P, 4], BF16, "rounded_late")
+        rounded_late = [sb([P, 2, 2, P, 4], BF16, "rounded_late%d" % h) for h in range(2)]
         slot_words = [sb([P, S], U32, "slot_words_" + n) for n in names]
         slot_scales = [
             [sb([P, H], U8, "slot_scales_q0"), at(RAW[2], [P, H], U8, "slot_scales_q1")],
@@ -74,7 +74,8 @@ def tile_moe_qkb_kernel(
         wq_codes = [sb([P, K], U32, "wq_codes%d" % e) for e in EARLY]
         wq_plane = [sb([P, K], U8, "wq_plane%d" % e) for e in EARLY]
         late_codes = [sb([P, 2 * P], U32, "late_codes%d" % ct) for ct in range(CT)]
-        late_plane = [at(GATE0 + H + ct * 2 * P, [P, 2 * P], U8, "late_plane%d" % ct) for ct in range(CT)]
+        late_plane = [sb([P, 2 * P], U8, "late_plane0")]
+        late_plane.extend([at(GATE0 + H + ct * 2 * P, [P, 2 * P], U8, "late_plane%d" % ct) for ct in range(1, CT)])
         gate_rows = sb([P, P], F32, "gate_rows")
         gate_col = at(RAW[1], [P, 2 * E], F32, "gate_col")
         gate_first = at(GATE0, [P, 3 * P], F32, "gate_first")
@@ -128,9 +129,9 @@ def tile_moe_qkb_kernel(
         load_wq(2)
         load_grad_scales(VP, 2, 4)
         load_plane(nc.sync, wv_plane, WV_ROW, wv_scales, 0, 2)
-        load_wk(0)
         load_wq(3)
         load_plane(nc.sync, wv_plane, WV_ROW, wv_scales, 2, 4)
+        load_wk(0)
         load_wv(0)
         load_wv(1)
         load_wk(1)
@@ -148,11 +149,16 @@ def tile_moe_qkb_kernel(
             nc.vector.tensor_copy(slot_scales[j][half][:], grad_scales[j][:].indirect(offsets))
 
         def cast(e):
-            if e in EARLY:
-                dst = rounded[e][:].rearrange("p (t c i) j -> p t c j i", t=CT, i=4)
+            nc.scalar.copy(rounded[e][:].rearrange("p (c i) j -> p c j i", i=4),
+                           raw[e][:].rearrange("p j (c i) -> p c j i", i=4))
+
+        def cast_late(e, h):
+            dst, src = rounded_late[h][:, :, e - 2, :, :], raw[e][:, :, 2 * h * P:2 * (h + 1) * P]
+            if (e, h) == (3, 1):
+                nc.gpsimd.tensor_scalar(dst, src.rearrange("p j (t c) -> p t c j", t=2), 1.0, 0.0, MULT, ADD)
             else:
-                dst = rounded_late[:, :, e - 2, :, :].rearrange("p t (c i) j -> p t c j i", i=4)
-            nc.scalar.copy(dst, raw[e][:].rearrange("p j (t c i) -> p t c j i", t=CT, i=4))
+                nc.scalar.copy(dst.rearrange("p t (c i) j -> p t c j i", i=4),
+                               src.rearrange("p j (t c i) -> p t c j i", t=2, i=4))
 
         def quantize(codes, plane, values):
             nc.vector.quantize_mx(out=codes[:].bitcast(FP8X4), scales=plane[:], in_=values)
@@ -161,7 +167,7 @@ def tile_moe_qkb_kernel(
             quantize(wq_codes[e], wq_plane[e], rounded[e][:].rearrange("p c j -> p (c j)"))
 
         def quantize_late(ct):
-            quantize(late_codes[ct], late_plane[ct], rounded_late[:, ct, :, :, :].rearrange("p e c j -> p (e c j)"))
+            quantize(late_codes[ct], late_plane[ct], rounded_late[ct // 2][:, ct % 2, :, :, :].rearrange("p e c j -> p (e c j)"))
 
         def weights(j, e, c0, c1):
             if j == QP and e in EARLY:
@@ -225,9 +231,10 @@ def tile_moe_qkb_kernel(
         gate_bank = bank(4)
         nc.tensor.transpose(gate_bank[:, 0:P], gate_rows[:], ident[:])
         nc.scalar.copy(gate_col[:], gate_bank[:, 0:2 * E])
-        nc.scalar.copy(gate_first[:, 0:4], gate_bank[:, 0:4])
-        cast(2)
-        cast(3)
+        nc.scalar.copy(gate_first[:, 0:2], gate_bank[:, 0:2])
+        for e in LATE:
+            for h in range(2):
+                cast_late(e, h)
         gather_scales(QP, 0)
         quantize_early(0)
         quantize_early(1)
@@ -238,7 +245,7 @@ def tile_moe_qkb_kernel(
             for s in range(4):
                 mx(sums[s][:], slots(j, s * P, (s + 1) * P), weights(j, s // 2, 0, K), j == QP, j == VP)
         for s in range(4):
-            gated_copy(head[:, s, :], sums[s][:, 0:P], gate_first, s)
+            gated_copy(head[:, s, :], sums[s][:, 0:P], gate_first if s < 2 else gate_col, s)
         turn(0, 0, [head[:, s, :] for s in range(4)], 4)
         for s in range(4):
             gated_copy(rest[s][:], sums[s][:, P:K], gate_col, s)

@@ -50,6 +50,7 @@ def tile_moe_qkb_kernel(
         RAW = [8 * KIB * e for e in range(E)]
         GATE0 = RAW[1] + 2 * KIB
         REST3 = 32 * KIB
+        END2 = 34 * KIB
 
         offs_t = keep.tile([P, S // 16], U16, name="offs_t")
         pos_t = [keep.tile([P, T // 16], U16, name="pos%d" % i) for i in range(2)]
@@ -60,7 +61,9 @@ def tile_moe_qkb_kernel(
         grad_scales = [sb([P, 2 * T], U8, "grad_scales_" + n) for n in names]
         raw = [at(RAW[e], [P, 4, K], F32, "raw%d" % e) for e in range(E)]
         rounded = [sb([P, K, 4], BF16, "rounded%d" % e) for e in EARLY]
-        rounded_late = [sb([P, 2, 2, P, 4], BF16, "rounded_late%d" % h) for h in range(2)]
+        rounded_late = sb([P, 2, 2, P, 4], BF16, "rounded_late")
+        rounded_mid = sb([P, 2, P, 4], BF16, "rounded_mid")
+        rounded_end = {2: at(END2, [P, P, 4], BF16, "rounded_end2"), 3: sb([P, P, 4], BF16, "rounded_end3")}
         slot_words = [sb([P, S], U32, "slot_words_" + n) for n in names]
         slot_scales = [
             [sb([P, H], U8, "slot_scales_q0"), at(RAW[2], [P, H], U8, "slot_scales_q1")],
@@ -73,9 +76,11 @@ def tile_moe_qkb_kernel(
         wv_codes = [sb([P, K], U32, "wv_codes%d" % e) for e in range(E)]
         wq_codes = [sb([P, K], U32, "wq_codes%d" % e) for e in EARLY]
         wq_plane = [sb([P, K], U8, "wq_plane%d" % e) for e in EARLY]
-        late_codes = [sb([P, 2 * P], U32, "late_codes%d" % ct) for ct in range(CT)]
+        late_codes = [sb([P, 2 * P], U32, "late_codes%d" % ct) for ct in range(CT - 1)]
+        end_codes = {e: sb([P, P], U32, "end_codes%d" % e) for e in LATE}
+        end_plane = {2: at(GATE0 + H + 3 * 2 * P, [P, P], U8, "end_plane2"), 3: at(END2, [P, P], U8, "end_plane3")}
         late_plane = [sb([P, 2 * P], U8, "late_plane0")]
-        late_plane.extend([at(GATE0 + H + ct * 2 * P, [P, 2 * P], U8, "late_plane%d" % ct) for ct in range(1, CT)])
+        late_plane.extend([at(GATE0 + H + ct * 2 * P, [P, 2 * P], U8, "late_plane%d" % ct) for ct in range(1, CT - 1)])
         gate_rows = sb([P, P], F32, "gate_rows")
         gate_col = at(RAW[1], [P, 2 * E], F32, "gate_col")
         gate_first = at(GATE0, [P, 3 * P], F32, "gate_first")
@@ -92,10 +97,10 @@ def tile_moe_qkb_kernel(
             words = grad_words_in[j][0].rearrange("p t d -> p (t d)").bitcast(I32)
             nc.sync.dma_start(grad_words[j][:, 0:T].bitcast(I32), words)
 
-        def load_grad_scales(j, q0, q1):
+        def load_grad_scales(j, q0, q1, queue=nc.sync):
             for q in range(q0, q1):
                 rows = grad_scales_in[j][0][4 * q:4 * q + 4, :].bitcast(I32)
-                nc.sync.dma_start(grad_scales[j][32 * q:32 * q + 4, 0:T].bitcast(I32), rows)
+                queue.dma_start(grad_scales[j][32 * q:32 * q + 4, 0:T].bitcast(I32), rows)
 
         def load_plane(queue, plane, first_row, scales, r0, r1):
             rows = scales.rearrange("e s (q r) c -> r q (e s) c", r=4)
@@ -115,7 +120,8 @@ def tile_moe_qkb_kernel(
         for j in range(3):
             nc.vector.memset(grad_scales[j][:, 0:T].bitcast(I32), 0)
         make_identity(nc, ident[:])
-        load_plane(nc.gpsimd, wk_plane, 0, wk_scales, 0, 4)
+        load_grad_scales(VP, 2, 4, nc.gpsimd)
+        load_plane(nc.gpsimd, wk_plane, 0, wk_scales, 0, 2)
         load_grad_words(QP)
         nc.sync.dma_start(offs_t[:], offs)
         load_grad_words(KP)
@@ -127,7 +133,7 @@ def tile_moe_qkb_kernel(
         load_grad_scales(KP, 0, 4)
         load_grad_scales(VP, 0, 2)
         load_wq(2)
-        load_grad_scales(VP, 2, 4)
+        load_plane(nc.sync, wk_plane, 0, wk_scales, 2, 4)
         load_plane(nc.sync, wv_plane, WV_ROW, wv_scales, 0, 2)
         load_wq(3)
         load_plane(nc.sync, wv_plane, WV_ROW, wv_scales, 2, 4)
@@ -152,13 +158,16 @@ def tile_moe_qkb_kernel(
             nc.scalar.copy(rounded[e][:].rearrange("p (c i) j -> p c j i", i=4),
                            raw[e][:].rearrange("p j (c i) -> p c j i", i=4))
 
-        def cast_late(e, h):
-            dst, src = rounded_late[h][:, :, e - 2, :, :], raw[e][:, :, 2 * h * P:2 * (h + 1) * P]
-            if (e, h) == (3, 1):
-                nc.gpsimd.tensor_scalar(dst, src.rearrange("p j (t c) -> p t c j", t=2), 1.0, 0.0, MULT, ADD)
-            else:
-                nc.scalar.copy(dst.rearrange("p t (c i) j -> p t c j i", i=4),
-                               src.rearrange("p j (t c i) -> p t c j i", t=2, i=4))
+        def cast_late(e):
+            nc.scalar.copy(rounded_late[:, :, e - 2, :, :].rearrange("p t (c i) j -> p t c j i", i=4),
+                           raw[e][:, :, 0:2 * P].rearrange("p j (t c i) -> p t c j i", t=2, i=4))
+            for ct, dst in ((2, rounded_mid[:, e - 2, :, :]), (3, rounded_end[e][:])):
+                src = raw[e][:, :, ct * P:(ct + 1) * P]
+                if e == E - 1:
+                    nc.gpsimd.tensor_scalar(dst, src.rearrange("p j c -> p c j"), 1.0, 0.0, MULT, ADD)
+                else:
+                    nc.scalar.copy(dst.rearrange("p (c i) j -> p c j i", i=4),
+                                   src.rearrange("p j (c i) -> p c j i", i=4))
 
         def quantize(codes, plane, values):
             nc.vector.quantize_mx(out=codes[:].bitcast(FP8X4), scales=plane[:], in_=values)
@@ -167,11 +176,17 @@ def tile_moe_qkb_kernel(
             quantize(wq_codes[e], wq_plane[e], rounded[e][:].rearrange("p c j -> p (c j)"))
 
         def quantize_late(ct):
-            quantize(late_codes[ct], late_plane[ct], rounded_late[ct // 2][:, ct % 2, :, :, :].rearrange("p e c j -> p (e c j)"))
+            values = rounded_mid[:] if ct == 2 else rounded_late[:, ct, :, :, :]
+            quantize(late_codes[ct], late_plane[ct], values.rearrange("p e c j -> p (e c j)"))
+
+        def quantize_end(e):
+            quantize(end_codes[e], end_plane[e], rounded_end[e][:].rearrange("p c j -> p (c j)"))
 
         def weights(j, e, c0, c1):
             if j == QP and e in EARLY:
                 return wq_codes[e][:, c0:c1].bitcast(FP8X4), wq_plane[e][:, c0:c1]
+            if j == QP and c0 == K - P:
+                return end_codes[e][:].bitcast(FP8X4), end_plane[e][:]
             if j == QP:
                 ct, cols = c0 // P, slice((e - 2) * P, (e - 1) * P)
                 return late_codes[ct][:, cols].bitcast(FP8X4), late_plane[ct][:, cols]
@@ -233,8 +248,7 @@ def tile_moe_qkb_kernel(
         nc.scalar.copy(gate_col[:], gate_bank[:, 0:2 * E])
         nc.scalar.copy(gate_first[:, 0:2], gate_bank[:, 0:2])
         for e in LATE:
-            for h in range(2):
-                cast_late(e, h)
+            cast_late(e)
         gather_scales(QP, 0)
         quantize_early(0)
         quantize_early(1)
@@ -249,7 +263,6 @@ def tile_moe_qkb_kernel(
         turn(0, 0, [head[:, s, :] for s in range(4)], 4)
         for s in range(4):
             gated_copy(rest[s][:], sums[s][:, P:K], gate_col, s)
-        turn_early(1, 1)
 
         gather_scales(KP, 1)
         gather_scales(QP, 1)
@@ -265,23 +278,25 @@ def tile_moe_qkb_kernel(
         late_passes(late_sums[2], 2, KP, True, False)
         tail_passes(tail, VP, False, True)
         nc.vector.tensor_tensor(dx[0][:, H:S], tail[:], gate_tail[:], MULT)
-        quantize_late(3)
+        quantize_end(2)
+        fetch(0, 0, T)
+        quantize_end(3)
         for ct in (1, 2):
             late_passes(late_sums[ct], ct, VP, False, False)
             late_passes(late_sums[ct], ct, QP, False, True)
         late_copies(late_sums[1], 1)
+        turn_early(1, 5)
         turn(1, 1, [late[1][:, i, :] for i in range(4)], 4)
-        turn_early(2, 2)
+        turn_early(2, 6)
         late_copies(late_sums[2], 2)
-        turn(2, 1, [late[2][:, i, :] for i in range(4)], 5)
+        turn(2, 1, [late[2][:, i, :] for i in range(4)], 1)
         late_sums[3] = bank(0)
         for j in (KP, VP, QP):
             late_passes(late_sums[3], 3, j, j == KP, j == QP)
         late_copies(late_sums[3], 3)
-        turn_early(3, 5)
+        turn_early(3, 1)
         turn(3, 1, [late[3][:, i, :] for i in range(4)], 3)
 
-        fetch(0, 0, T)
         fetch_add(0, 0, T)
         fetch(1, 0, T)
         fetch(2, 0, T)

@@ -25,7 +25,6 @@ QP, KP, VP = 0, 1, 2
 EARLY, LATE = (0, 1), (2, 3)
 H = S // 2
 KIB = 1024
-WV_ROW = 4
 
 
 def tile_moe_qkb_kernel(
@@ -71,7 +70,7 @@ def tile_moe_qkb_kernel(
             [at(RAW[1] + KIB, [P, H], U8, "slot_scales_v0"), at(GATE0, [P, H], U8, "slot_scales_v1")],
         ]
         wk_plane = sb([P, E, K], U8, "wk_plane")
-        wv_plane = sb([P, E, K], U8, "wv_plane")
+        wv_plane = sb([P, K], U8, "wv_plane")
         wk_pairs = [sb([P, 2, 2 * K], U8, "wk_pair%d" % i) for i in range(2)]
         wv_codes = [sb([P, K], U32, "wv_codes%d" % e) for e in range(E)]
         wq_codes = [sb([P, K], U32, "wq_codes%d" % e) for e in EARLY]
@@ -97,15 +96,20 @@ def tile_moe_qkb_kernel(
             words = grad_words_in[j][0].rearrange("p t d -> p (t d)").bitcast(I32)
             nc.sync.dma_start(grad_words[j][:, 0:T].bitcast(I32), words)
 
-        def load_grad_scales(j, q0, q1, queue=nc.sync):
+        def load_grad_scales(j, q0, q1):
             for q in range(q0, q1):
                 rows = grad_scales_in[j][0][4 * q:4 * q + 4, :].bitcast(I32)
-                queue.dma_start(grad_scales[j][32 * q:32 * q + 4, 0:T].bitcast(I32), rows)
+                nc.sync.dma_start(grad_scales[j][32 * q:32 * q + 4, 0:T].bitcast(I32), rows)
 
-        def load_plane(queue, plane, first_row, scales, r0, r1):
-            rows = scales.rearrange("e s (q r) c -> r q (e s) c", r=4)
-            for r in range(r0, r1):
-                queue.dma_start(plane[first_row + r:P:32, :, :].bitcast(I32), rows[r].bitcast(I32))
+        def load_wk_plane():
+            rows = wk_scales.rearrange("e s (q r) c -> r q (e s) c", r=4)
+            for r in range(4):
+                nc.gpsimd.dma_start(wk_plane[r:P:32, :, :].bitcast(I32), rows[r].bitcast(I32))
+
+        def load_wv_plane(q0, q1):
+            rows = wv_scales.rearrange("e s (q r) c -> q (e s) r c", r=4)
+            for q in range(q0, q1):
+                nc.sync.dma_start(wv_plane[32 * q:32 * q + 4 * E, :].bitcast(I32), rows[q].bitcast(I32))
 
         def load_wq(e):
             nc.sync.dma_start(raw[e][:], wq[e].rearrange("(p j) c -> p j c", j=4))
@@ -120,8 +124,7 @@ def tile_moe_qkb_kernel(
         for j in range(3):
             nc.vector.memset(grad_scales[j][:, 0:T].bitcast(I32), 0)
         make_identity(nc, ident[:])
-        load_grad_scales(VP, 2, 4, nc.gpsimd)
-        load_plane(nc.gpsimd, wk_plane, 0, wk_scales, 0, 2)
+        load_wk_plane()
         load_grad_words(QP)
         nc.sync.dma_start(offs_t[:], offs)
         load_grad_words(KP)
@@ -133,10 +136,10 @@ def tile_moe_qkb_kernel(
         load_grad_scales(KP, 0, 4)
         load_grad_scales(VP, 0, 2)
         load_wq(2)
-        load_plane(nc.sync, wk_plane, 0, wk_scales, 2, 4)
-        load_plane(nc.sync, wv_plane, WV_ROW, wv_scales, 0, 2)
+        load_grad_scales(VP, 2, 4)
+        load_wv_plane(0, 2)
         load_wq(3)
-        load_plane(nc.sync, wv_plane, WV_ROW, wv_scales, 2, 4)
+        load_wv_plane(2, 4)
         load_wk(0)
         load_wv(0)
         load_wv(1)
@@ -192,7 +195,7 @@ def tile_moe_qkb_kernel(
                 return late_codes[ct][:, cols].bitcast(FP8X4), late_plane[ct][:, cols]
             if j == KP:
                 return wk_pairs[e // 2][:, e % 2, 2 * c0:2 * c1].bitcast(FP4X4), wk_plane[:, e, c0:c1]
-            return wv_codes[e][:, c0:c1].bitcast(FP8X4), wv_plane[WV_ROW:P, e, c0:c1]
+            return wv_codes[e][:, c0:c1].bitcast(FP8X4), wv_plane[4 * e:P, c0:c1]
 
         def slots(j, u0, u1):
             half = u0 // H

@@ -47,7 +47,7 @@ def tile_moe_qkb_kernel(
             return reuse.tile(shape, dtype, name=name, align_bytes=64, offset=offset)
 
         RAW = [8 * KIB * e for e in range(E)]
-        GATE0 = RAW[1] + 2 * KIB
+        GATE0 = RAW[3]
         REST3 = 32 * KIB
         END2 = 34 * KIB
 
@@ -81,8 +81,7 @@ def tile_moe_qkb_kernel(
         late_plane = [sb([P, 2 * P], U8, "late_plane0")]
         late_plane.extend([at(GATE0 + H + ct * 2 * P, [P, 2 * P], U8, "late_plane%d" % ct) for ct in range(1, CT - 1)])
         gate_rows = sb([P, P], F32, "gate_rows")
-        gate_col = at(RAW[1], [P, 2 * E], F32, "gate_col")
-        gate_first = at(GATE0, [P, 3 * P], F32, "gate_first")
+        gate_col = sb([P, 2 * E], F32, "gate_col")
         gate_tail = sb([P, H], F32, "gate_tail")
         ident = sb([P, P], F32, "ident")
         head = sb([P, 4, P], F32, "head")
@@ -127,10 +126,10 @@ def tile_moe_qkb_kernel(
         load_wk_plane()
         load_grad_words(QP)
         nc.sync.dma_start(offs_t[:], offs)
+        nc.sync.dma_start(gate_rows[:], gate.rearrange("a (s p) -> (a s) p", p=P)[0:P, :])
         load_grad_words(KP)
         load_wq(0)
         load_grad_words(VP)
-        nc.sync.dma_start(gate_rows[:], gate.rearrange("a (s p) -> (a s) p", p=P)[0:P, :])
         load_grad_scales(QP, 0, 4)
         load_wq(1)
         load_grad_scales(KP, 0, 4)
@@ -143,12 +142,11 @@ def tile_moe_qkb_kernel(
         load_wk(0)
         load_wv(0)
         load_wv(1)
+        nc.sync.dma_start(pos_t[0][:], pos1)
+        nc.sync.dma_start(pos_t[1][:], pos2)
         load_wk(1)
         load_wv(2)
         load_wv(3)
-        nc.sync.dma_start(gate_tail[:], gate[:, H:S])
-        nc.sync.dma_start(pos_t[0][:], pos1)
-        nc.sync.dma_start(pos_t[1][:], pos2)
 
         def gather_words(j):
             nc.vector.tensor_copy(slot_words[j][:], grad_words[j][:].indirect(offs_t[:]))
@@ -244,12 +242,15 @@ def tile_moe_qkb_kernel(
 
         for j in (QP, KP, VP):
             gather_words(j)
-        cast(0)
-        cast(1)
         gate_bank = bank(4)
         nc.tensor.transpose(gate_bank[:, 0:P], gate_rows[:], ident[:])
         nc.scalar.copy(gate_col[:], gate_bank[:, 0:2 * E])
-        nc.scalar.copy(gate_first[:, 0:2], gate_bank[:, 0:2])
+        spread = bank(5)
+        for i in range(4):
+            nc.tensor.transpose(spread[:, i * P:(i + 1) * P], gate_col[:, 4 + i:5 + i].to_broadcast([P, P]), ident[:])
+        nc.scalar.copy(gate_tail[:], spread[:])
+        cast(0)
+        cast(1)
         for e in LATE:
             cast_late(e)
         gather_scales(QP, 0)
@@ -262,7 +263,7 @@ def tile_moe_qkb_kernel(
             for s in range(4):
                 mx(sums[s][:], slots(j, s * P, (s + 1) * P), weights(j, s // 2, 0, K), j == QP, j == VP)
         for s in range(4):
-            gated_copy(head[:, s, :], sums[s][:, 0:P], gate_first if s < 2 else gate_col, s)
+            gated_copy(head[:, s, :], sums[s][:, 0:P], gate_col, s)
         turn(0, 0, [head[:, s, :] for s in range(4)], 4)
         for s in range(4):
             gated_copy(rest[s][:], sums[s][:, P:K], gate_col, s)

@@ -50,6 +50,7 @@ def tile_moe_qkb_kernel(
         GATE0 = RAW[3]
         REST3 = 32 * KIB
         END2 = 34 * KIB
+        ROUND0 = 40 * KIB
 
         offs_t = keep.tile([P, S // 16], U16, name="offs_t")
         pos_t = [keep.tile([P, T // 16], U16, name="pos%d" % i) for i in range(2)]
@@ -59,7 +60,8 @@ def tile_moe_qkb_kernel(
         grad_words = [sb([P, 3 * T], U32, "grad_words_" + n) for n in names]
         grad_scales = [sb([P, 2 * T], U8, "grad_scales_" + n) for n in names]
         raw = [at(RAW[e], [P, 4, K], F32, "raw%d" % e) for e in range(E)]
-        rounded = [sb([P, K, 4], BF16, "rounded%d" % e) for e in EARLY]
+        gate_spread = at(ROUND0, [P, 4], F32, "gate_spread")
+        rounded = [at(ROUND0, [P, K, 4], BF16, "rounded0"), sb([P, K, 4], BF16, "rounded1")]
         rounded_late = sb([P, 2, 2, P, 4], BF16, "rounded_late")
         rounded_mid = sb([P, 2, P, 4], BF16, "rounded_mid")
         rounded_end = {2: at(END2, [P, P, 4], BF16, "rounded_end2"), 3: sb([P, P, 4], BF16, "rounded_end3")}
@@ -95,10 +97,10 @@ def tile_moe_qkb_kernel(
             words = grad_words_in[j][0].rearrange("p t d -> p (t d)").bitcast(I32)
             nc.sync.dma_start(grad_words[j][:, 0:T].bitcast(I32), words)
 
-        def load_grad_scales(j, q0, q1):
+        def load_grad_scales(j, q0, q1, queue=nc.sync):
             for q in range(q0, q1):
                 rows = grad_scales_in[j][0][4 * q:4 * q + 4, :].bitcast(I32)
-                nc.sync.dma_start(grad_scales[j][32 * q:32 * q + 4, 0:T].bitcast(I32), rows)
+                queue.dma_start(grad_scales[j][32 * q:32 * q + 4, 0:T].bitcast(I32), rows)
 
         def load_wk_plane():
             rows = wk_scales.rearrange("e s (q r) c -> r q (e s) c", r=4)
@@ -123,6 +125,7 @@ def tile_moe_qkb_kernel(
         for j in range(3):
             nc.vector.memset(grad_scales[j][:, 0:T].bitcast(I32), 0)
         make_identity(nc, ident[:])
+        load_grad_scales(VP, 2, 4, nc.gpsimd)
         load_wk_plane()
         load_grad_words(QP)
         nc.sync.dma_start(offs_t[:], offs)
@@ -135,10 +138,8 @@ def tile_moe_qkb_kernel(
         load_grad_scales(KP, 0, 4)
         load_grad_scales(VP, 0, 2)
         load_wq(2)
-        load_grad_scales(VP, 2, 4)
-        load_wv_plane(0, 2)
+        load_wv_plane(0, 4)
         load_wq(3)
-        load_wv_plane(2, 4)
         load_wk(0)
         load_wv(0)
         load_wv(1)
@@ -244,10 +245,11 @@ def tile_moe_qkb_kernel(
             gather_words(j)
         gate_bank = bank(4)
         nc.tensor.transpose(gate_bank[:, 0:P], gate_rows[:], ident[:])
+        nc.scalar.copy(gate_spread[:], gate_bank[:, 4:8])
         nc.scalar.copy(gate_col[:], gate_bank[:, 0:2 * E])
         spread = bank(5)
         for i in range(4):
-            nc.tensor.transpose(spread[:, i * P:(i + 1) * P], gate_col[:, 4 + i:5 + i].to_broadcast([P, P]), ident[:])
+            nc.tensor.transpose(spread[:, i * P:(i + 1) * P], gate_spread[:, i:i + 1].to_broadcast([P, P]), ident[:])
         nc.scalar.copy(gate_tail[:], spread[:])
         cast(0)
         cast(1)

@@ -47,7 +47,6 @@ def tile_moe_qkb_kernel(
             return reuse.tile(shape, dtype, name=name, align_bytes=64, offset=offset)
 
         RAW = [8 * KIB * e for e in range(E)]
-        GATE0 = RAW[3]
         REST3 = 32 * KIB
         END2 = 34 * KIB
         ROUND0 = 40 * KIB
@@ -69,7 +68,7 @@ def tile_moe_qkb_kernel(
         slot_scales = [
             [sb([P, H], U8, "slot_scales_q0"), at(RAW[2], [P, H], U8, "slot_scales_q1")],
             [at(RAW[1] + 4 * KIB, [P, H], U8, "slot_scales_k0"), at(RAW[2] + H, [P, H], U8, "slot_scales_k1")],
-            [at(RAW[1] + KIB, [P, H], U8, "slot_scales_v0"), at(GATE0, [P, H], U8, "slot_scales_v1")],
+            [at(RAW[1] + KIB, [P, H], U8, "slot_scales_v0"), at(RAW[2] + 2 * H, [P, H], U8, "slot_scales_v1")],
         ]
         wk_plane = sb([P, E, K], U8, "wk_plane")
         wv_plane = sb([P, K], U8, "wv_plane")
@@ -79,9 +78,8 @@ def tile_moe_qkb_kernel(
         wq_plane = [sb([P, K], U8, "wq_plane%d" % e) for e in EARLY]
         late_codes = [sb([P, 2 * P], U32, "late_codes%d" % ct) for ct in range(CT - 1)]
         end_codes = {e: sb([P, P], U32, "end_codes%d" % e) for e in LATE}
-        end_plane = {2: at(GATE0 + H + 3 * 2 * P, [P, P], U8, "end_plane2"), 3: at(END2, [P, P], U8, "end_plane3")}
-        late_plane = [sb([P, 2 * P], U8, "late_plane0")]
-        late_plane.extend([at(GATE0 + H + ct * 2 * P, [P, 2 * P], U8, "late_plane%d" % ct) for ct in range(1, CT - 1)])
+        late_plane = [at(RAW[3] + ct * 2 * P, [P, 2 * P], U8, "late_plane%d" % ct) for ct in range(CT - 1)]
+        end_plane = {2: at(RAW[3], [P, P], U8, "end_plane2"), 3: at(END2, [P, P], U8, "end_plane3")}
         gate_rows = sb([P, P], F32, "gate_rows")
         gate_col = sb([P, 2 * E], F32, "gate_col")
         gate_tail = sb([P, H], F32, "gate_tail")
@@ -272,24 +270,23 @@ def tile_moe_qkb_kernel(
 
         gather_scales(KP, 1)
         gather_scales(QP, 1)
-        quantize_late(0)
         gather_scales(VP, 1)
-        quantize_late(1)
-        quantize_late(2)
+        for ct in range(CT - 1):
+            quantize_late(ct)
         tail = bank(5)
         late_sums = {1: bank(6), 2: bank(7)}
         tail_passes(tail, KP, True, False)
-        tail_passes(tail, QP, False, False)
-        late_passes(late_sums[1], 1, KP, True, False)
-        late_passes(late_sums[2], 2, KP, True, False)
-        tail_passes(tail, VP, False, True)
+        for ct in (1, 2):
+            late_passes(late_sums[ct], ct, KP, True, False)
+        tail_passes(tail, VP, False, False)
+        tail_passes(tail, QP, False, True)
         nc.vector.tensor_tensor(dx[0][:, H:S], tail[:], gate_tail[:], MULT)
         quantize_end(2)
         fetch(0, 0, T)
         quantize_end(3)
         for ct in (1, 2):
-            late_passes(late_sums[ct], ct, VP, False, False)
-            late_passes(late_sums[ct], ct, QP, False, True)
+            late_passes(late_sums[ct], ct, QP, False, False)
+            late_passes(late_sums[ct], ct, VP, False, True)
         late_copies(late_sums[1], 1)
         turn_early(1, 5)
         turn(1, 1, [late[1][:, i, :] for i in range(4)], 4)

@@ -73,7 +73,8 @@ def tile_moe_qkb_kernel(
         wk_plane = sb([P, E, K], U8, "wk_plane")
         wv_plane = sb([P, K], U8, "wv_plane")
         wk_pairs = [sb([P, 2, 2 * K], U8, "wk_pair%d" % i) for i in range(2)]
-        wv_codes = [sb([P, K], U32, "wv_codes%d" % e) for e in range(E)]
+        wv_codes = [sb([P, K], U32, "wv_codes%d" % e) for e in EARLY]
+        wv_late = [sb([P, 2, K // 2], U32, "wv_late%d" % h) for h in range(2)]
         wq_codes = [sb([P, K], U32, "wq_codes%d" % e) for e in EARLY]
         wq_plane = [sb([P, K], U8, "wq_plane%d" % e) for e in EARLY]
         late_codes = [sb([P, 2 * P], U32, "late_codes%d" % ct) for ct in range(CT - 1)]
@@ -120,6 +121,10 @@ def tile_moe_qkb_kernel(
         def load_wv(e):
             nc.sync.dma_start(wv_codes[e][:].bitcast(I32), wv_words[e, 0].rearrange("p c d -> p (c d)").bitcast(I32))
 
+        def load_wv_late(h):
+            words = wv_words.rearrange("e s p c d -> p (e s) (c d)")[:, 2:E, 2 * h * K:2 * (h + 1) * K]
+            nc.sync.dma_start(wv_late[h][:].bitcast(I32), words.bitcast(I32))
+
         for j in range(3):
             nc.vector.memset(grad_scales[j][:, 0:T].bitcast(I32), 0)
         make_identity(nc, ident[:])
@@ -141,11 +146,11 @@ def tile_moe_qkb_kernel(
         load_wk(0)
         load_wv(0)
         load_wv(1)
-        nc.sync.dma_start(pos_t[0][:], pos1)
-        nc.sync.dma_start(pos_t[1][:], pos2)
         load_wk(1)
-        load_wv(2)
-        load_wv(3)
+        load_wv_late(0)
+        nc.sync.dma_start(pos_t[0][:], pos1)
+        load_wv_late(1)
+        nc.sync.dma_start(pos_t[1][:], pos2)
 
         def gather_words(j):
             nc.vector.tensor_copy(slot_words[j][:], grad_words[j][:].indirect(offs_t[:]))
@@ -192,7 +197,9 @@ def tile_moe_qkb_kernel(
                 return late_codes[ct][:, cols].bitcast(FP8X4), late_plane[ct][:, cols]
             if j == KP:
                 return wk_pairs[e // 2][:, e % 2, 2 * c0:2 * c1].bitcast(FP4X4), wk_plane[:, e, c0:c1]
-            return wv_codes[e][:, c0:c1].bitcast(FP8X4), wv_plane[4 * e:P, c0:c1]
+            h, v0 = divmod(c0, K // 2)
+            codes = wv_codes[e][:, c0:c1] if e in EARLY else wv_late[h][:, e - 2, v0:v0 + c1 - c0]
+            return codes.bitcast(FP8X4), wv_plane[4 * e:P, c0:c1]
 
         def slots(j, u0, u1):
             half = u0 // H

@@ -22,7 +22,6 @@ ADD = mybir.AluOpType.add
 P = 128
 CT = K // P
 QP, KP, VP = 0, 1, 2
-EARLY, LATE = (0, 1), (2, 3)
 H = S // 2
 KIB = 1024
 
@@ -46,51 +45,48 @@ def tile_moe_qkb_kernel(
         def at(offset, shape, dtype, name):
             return reuse.tile(shape, dtype, name=name, align_bytes=64, offset=offset)
 
-        RAW = [8 * KIB * e for e in range(E)]
-        REST3 = 32 * KIB
-        END2 = 34 * KIB
-        ROUND0 = 40 * KIB
+        RAW1 = 0
+        ROUND0 = 8 * KIB
+        EARLY3 = 12 * KIB
+        GATE = 14 * KIB
+        COLS = 16 * KIB
 
         offs_t = keep.tile([P, S // 16], U16, name="offs_t")
         pos_t = [keep.tile([P, T // 16], U16, name="pos%d" % i) for i in range(2)]
         names = ("q", "k", "v")
         grad_words_in = (dq_words, dk_words, dv_words)
         grad_scales_in = (dq_scales, dk_scales, dv_scales)
-        grad_words = [sb([P, 3 * T], U32, "grad_words_" + n) for n in names]
+        grad_words = [sb([P, (3 if n == "q" else 2) * T], U32, "grad_words_" + n) for n in names]
         grad_scales = [sb([P, 2 * T], U8, "grad_scales_" + n) for n in names]
-        raw = [at(RAW[e], [P, 4, K], F32, "raw%d" % e) for e in range(E)]
+        raw = [at(RAW1, [P, 4, K], F32, "raw1") if e == 1 else sb([P, 4, K], F32, "raw%d" % e) for e in range(E)]
         gate_spread = at(ROUND0, [P, 4], F32, "gate_spread")
         rounded = [at(ROUND0, [P, K, 4], BF16, "rounded0"), sb([P, K, 4], BF16, "rounded1")]
-        rounded_late = sb([P, 2, 2, P, 4], BF16, "rounded_late")
-        rounded_mid = sb([P, 2, P, 4], BF16, "rounded_mid")
-        rounded_end = {2: at(END2, [P, P, 4], BF16, "rounded_end2"), 3: sb([P, P, 4], BF16, "rounded_end3")}
-        slot_words = [sb([P, S], U32, "slot_words_" + n) for n in names]
-        slot_scales = [
-            [sb([P, H], U8, "slot_scales_q0"), at(RAW[2], [P, H], U8, "slot_scales_q1")],
-            [at(RAW[1] + 4 * KIB, [P, H], U8, "slot_scales_k0"), at(RAW[2] + H, [P, H], U8, "slot_scales_k1")],
-            [at(RAW[1] + KIB, [P, H], U8, "slot_scales_v0"), at(RAW[2] + 2 * H, [P, H], U8, "slot_scales_v1")],
-        ]
+        rounded_late = [sb([P, 2, 2, P, 4], BF16, "rounded_late%d" % h) for h in range(2)]
+        q_words = sb([P, S], U32, "slot_words_q")
+        slot_words = [[q_words[:, 0:H], q_words[:, H:S]]] + [
+            [sb([P, H], U32, "slot_words0_" + names[j])[:],
+             at(RAW1 + 2 * KIB * j, [P, H], U32, "slot_words1_" + names[j])[:]] for j in (KP, VP)]
+        slot_scales = [[sb([P, H], U8, "slot_scales0_" + names[j]),
+                        at(COLS if j == KP else RAW1 + 6 * KIB + H * j, [P, H], U8, "slot_scales1_" + names[j])]
+                       for j in range(3)]
         wk_plane = sb([P, E, K], U8, "wk_plane")
         wv_plane = sb([P, K], U8, "wv_plane")
         wk_pairs = [sb([P, 2, 2 * K], U8, "wk_pair%d" % i) for i in range(2)]
-        wv_codes = [sb([P, K], U32, "wv_codes%d" % e) for e in EARLY]
+        wv_early = sb([P, 2, K], U32, "wv_early")
         wv_late = [sb([P, 2, K // 2], U32, "wv_late%d" % h) for h in range(2)]
-        wq_codes = [sb([P, K], U32, "wq_codes%d" % e) for e in EARLY]
-        wq_plane = [sb([P, K], U8, "wq_plane%d" % e) for e in EARLY]
-        late_codes = [sb([P, 2 * P], U32, "late_codes%d" % ct) for ct in range(CT - 1)]
-        end_codes = {e: sb([P, P], U32, "end_codes%d" % e) for e in LATE}
-        late_plane = [at(RAW[3] + ct * 2 * P, [P, 2 * P], U8, "late_plane%d" % ct) for ct in range(CT - 1)]
-        end_plane = {2: at(RAW[3], [P, P], U8, "end_plane2"), 3: at(END2, [P, P], U8, "end_plane3")}
+        wq_codes = [sb([P, K], U32, "wq_codes%d" % e) for e in range(2)]
+        wq_plane = [sb([P, K], U8, "wq_plane%d" % e) for e in range(2)]
+        late_codes = [sb([P, 2 * P], U32, "late_codes%d" % ct) for ct in range(CT)]
+        late_plane = [at(EARLY3 + ct * 2 * P, [P, 2 * P], U8, "late_plane%d" % ct) for ct in range(CT)]
         gate_rows = sb([P, P], F32, "gate_rows")
-        gate_col = sb([P, 2 * E], F32, "gate_col")
-        gate_tail = sb([P, H], F32, "gate_tail")
+        gate_col = [at(COLS, [P, 4], F32, "gate_col0"), sb([P, 4], F32, "gate_col1")]
+        gate_tail = at(GATE, [P, H], F32, "gate_tail")
         ident = sb([P, P], F32, "ident")
-        head = sb([P, 4, P], F32, "head")
-        rest = [sb([P, K - P], F32, "rest%d" % s) for s in range(3)] + [at(REST3, [P, K - P], F32, "rest3")]
-        late = {ct: sb([P, 4, P], F32, "late%d" % ct) for ct in range(1, CT)}
+        early = [sb([P, K], F32, "early%d" % s) for s in range(3)] + [at(EARLY3, [P, K], F32, "early3")]
+        late0 = sb([P, 4, P], F32, "late0")
         dx = [sb([P, S], F32, "dx%d" % ct) for ct in range(CT)]
         first = [sb([P, T], F32, "first%d" % ct) for ct in range(CT)]
-        res = [at(REST3, [P, T], F32, "res1") if ct == 1 else sb([P, T], F32, "res%d" % ct) for ct in range(CT)]
+        res = [at(GATE, [P, T], F32, "res1") if ct == 1 else sb([P, T], F32, "res%d" % ct) for ct in range(CT)]
 
         def load_grad_words(j):
             words = grad_words_in[j][0].rearrange("p t d -> p (t d)").bitcast(I32)
@@ -106,9 +102,9 @@ def tile_moe_qkb_kernel(
             for r in range(4):
                 nc.gpsimd.dma_start(wk_plane[r:P:32, :, :].bitcast(I32), rows[r].bitcast(I32))
 
-        def load_wv_plane(q0, q1):
+        def load_wv_plane():
             rows = wv_scales.rearrange("e s (q r) c -> q (e s) r c", r=4)
-            for q in range(q0, q1):
+            for q in range(4):
                 nc.sync.dma_start(wv_plane[32 * q:32 * q + 4 * E, :].bitcast(I32), rows[q].bitcast(I32))
 
         def load_wq(e):
@@ -118,61 +114,58 @@ def tile_moe_qkb_kernel(
             words = wk_words.rearrange("e s p b -> p (e s) b")[:, 2 * pair:2 * pair + 2, :]
             nc.sync.dma_start(wk_pairs[pair][:].bitcast(I32), words.bitcast(I32))
 
-        def load_wv(e):
-            nc.sync.dma_start(wv_codes[e][:].bitcast(I32), wv_words[e, 0].rearrange("p c d -> p (c d)").bitcast(I32))
+        def load_wv(dst, e0, b0, b1):
+            words = wv_words.rearrange("e s p c d -> p (e s) (c d)")[:, e0:e0 + 2, b0:b1]
+            nc.sync.dma_start(dst[:].bitcast(I32), words.bitcast(I32))
 
-        def load_wv_late(h):
-            words = wv_words.rearrange("e s p c d -> p (e s) (c d)")[:, 2:E, 2 * h * K:2 * (h + 1) * K]
-            nc.sync.dma_start(wv_late[h][:].bitcast(I32), words.bitcast(I32))
-
-        for j in range(3):
+        for j in (KP, VP, QP):
             nc.vector.memset(grad_scales[j][:, 0:T].bitcast(I32), 0)
         make_identity(nc, ident[:])
-        load_grad_scales(VP, 2, 4, nc.gpsimd)
         load_wk_plane()
         load_grad_words(QP)
         nc.sync.dma_start(offs_t[:], offs)
         nc.sync.dma_start(gate_rows[:], gate.rearrange("a (s p) -> (a s) p", p=P)[0:P, :])
         load_grad_words(KP)
-        load_wq(0)
         load_grad_words(VP)
-        load_grad_scales(QP, 0, 4)
-        load_wq(1)
+        load_wk(0)
+        load_wq(0)
         load_grad_scales(KP, 0, 4)
         load_grad_scales(VP, 0, 2)
+        load_wq(1)
+        load_grad_scales(VP, 2, 4)
+        load_grad_scales(QP, 0, 4)
         load_wq(2)
-        load_wv_plane(0, 4)
+        load_wv(wv_early, 0, 0, 4 * K)
+        load_wv_plane()
         load_wq(3)
-        load_wk(0)
-        load_wv(0)
-        load_wv(1)
         load_wk(1)
-        load_wv_late(0)
+        load_wv(wv_late[0], 2, 0, 2 * K)
+        load_wv(wv_late[1], 2, 2 * K, 4 * K)
         nc.sync.dma_start(pos_t[0][:], pos1)
-        load_wv_late(1)
         nc.sync.dma_start(pos_t[1][:], pos2)
 
-        def gather_words(j):
-            nc.vector.tensor_copy(slot_words[j][:], grad_words[j][:].indirect(offs_t[:]))
+        def gather(dst, window, half):
+            offsets = offs_t[:, half * H // 16:(half + 1) * H // 16]
+            nc.vector.tensor_copy(dst, window[:].indirect(offsets))
+
+        def gather_words(j, half):
+            gather(slot_words[j][half], grad_words[j], half)
 
         def gather_scales(j, half):
-            offsets = offs_t[:, half * H // 16:(half + 1) * H // 16]
-            nc.vector.tensor_copy(slot_scales[j][half][:], grad_scales[j][:].indirect(offsets))
+            gather(slot_scales[j][half][:], grad_scales[j], half)
 
         def cast(e):
             nc.scalar.copy(rounded[e][:].rearrange("p (c i) j -> p c j i", i=4),
                            raw[e][:].rearrange("p j (c i) -> p c j i", i=4))
 
-        def cast_late(e):
-            nc.scalar.copy(rounded_late[:, :, e - 2, :, :].rearrange("p t (c i) j -> p t c j i", i=4),
-                           raw[e][:, :, 0:2 * P].rearrange("p j (t c i) -> p t c j i", t=2, i=4))
-            for ct, dst in ((2, rounded_mid[:, e - 2, :, :]), (3, rounded_end[e][:])):
-                src = raw[e][:, :, ct * P:(ct + 1) * P]
-                if e == E - 1:
-                    nc.gpsimd.tensor_scalar(dst, src.rearrange("p j c -> p c j"), 1.0, 0.0, MULT, ADD)
-                else:
-                    nc.scalar.copy(dst.rearrange("p (c i) j -> p c j i", i=4),
-                                   src.rearrange("p j (c i) -> p c j i", i=4))
+        def cast_late(e, h):
+            dst = rounded_late[h][:, :, e - 2, :, :]
+            src = raw[e][:, :, 2 * h * P:2 * (h + 1) * P]
+            if e == E - 1:
+                nc.gpsimd.tensor_scalar(dst, src.rearrange("p j (t c) -> p t c j", t=2), 1.0, 0.0, MULT, ADD)
+            else:
+                nc.scalar.copy(dst.rearrange("p t (c i) j -> p t c j i", i=4),
+                               src.rearrange("p j (t c i) -> p t c j i", t=2, i=4))
 
         def quantize(codes, plane, values):
             nc.vector.quantize_mx(out=codes[:].bitcast(FP8X4), scales=plane[:], in_=values)
@@ -181,36 +174,32 @@ def tile_moe_qkb_kernel(
             quantize(wq_codes[e], wq_plane[e], rounded[e][:].rearrange("p c j -> p (c j)"))
 
         def quantize_late(ct):
-            values = rounded_mid[:] if ct == 2 else rounded_late[:, ct, :, :, :]
+            values = rounded_late[ct // 2][:, ct % 2, :, :, :]
             quantize(late_codes[ct], late_plane[ct], values.rearrange("p e c j -> p (e c j)"))
 
-        def quantize_end(e):
-            quantize(end_codes[e], end_plane[e], rounded_end[e][:].rearrange("p c j -> p (c j)"))
-
         def weights(j, e, c0, c1):
-            if j == QP and e in EARLY:
+            if j == QP and e < 2:
                 return wq_codes[e][:, c0:c1].bitcast(FP8X4), wq_plane[e][:, c0:c1]
-            if j == QP and c0 == K - P:
-                return end_codes[e][:].bitcast(FP8X4), end_plane[e][:]
             if j == QP:
                 ct, cols = c0 // P, slice((e - 2) * P, (e - 1) * P)
                 return late_codes[ct][:, cols].bitcast(FP8X4), late_plane[ct][:, cols]
             if j == KP:
                 return wk_pairs[e // 2][:, e % 2, 2 * c0:2 * c1].bitcast(FP4X4), wk_plane[:, e, c0:c1]
             h, v0 = divmod(c0, K // 2)
-            codes = wv_codes[e][:, c0:c1] if e in EARLY else wv_late[h][:, e - 2, v0:v0 + c1 - c0]
+            codes = wv_early[:, e, c0:c1] if e < 2 else wv_late[h][:, e - 2, v0:v0 + c1 - c0]
             return codes.bitcast(FP8X4), wv_plane[4 * e:P, c0:c1]
 
         def slots(j, u0, u1):
             half = u0 // H
-            return slot_words[j][:, u0:u1].bitcast(FP8X4), slot_scales[j][half][:, u0 - half * H:u1 - half * H]
+            cols = slice(u0 - half * H, u1 - half * H)
+            return slot_words[j][half][:, cols].bitcast(FP8X4), slot_scales[j][half][:, cols]
 
         def mx(acc, stationary, moving, start, stop):
             nc.tensor.matmul_mx(out=acc, lhsT=stationary[0], lhsT_scale=stationary[1], rhs=moving[0],
                                 rhs_scale=moving[1], start=start, stop=stop)
 
-        def gated_copy(dst, src, gates, s):
-            nc.scalar.activation(dst, src, COPY, scale=gates[:, s:s + 1])
+        def gated_copy(dst, src, s):
+            nc.scalar.activation(dst, src, COPY, scale=gate_col[s // 4][:, s % 4:s % 4 + 1])
 
         def turn(ct, half, blocks, n):
             turned = bank(n)
@@ -218,102 +207,82 @@ def tile_moe_qkb_kernel(
                 nc.tensor.transpose(turned[:, i * P:(i + 1) * P], block, ident[:])
             nc.scalar.copy(dx[ct][:, half * H:(half + 1) * H], turned[:])
 
-        def turn_early(ct, n):
-            turn(ct, 0, [rest[s][:, (ct - 1) * P:ct * P] for s in range(4)], n)
+        def late_passes(acc, ct, j):
+            cols = (ct * P, (ct + 1) * P)
+            if ct == 0:
+                for i in range(4):
+                    u0 = H + i * P
+                    mx(acc[:, i * P:(i + 1) * P], slots(j, u0, u0 + P), weights(j, u0 // C, *cols),
+                       j == VP and i == 0, j == QP and i == 3)
+            else:
+                for e in (2, 3):
+                    mx(acc[:, (e - 2) * C:(e - 1) * C], weights(j, e, *cols), slots(j, e * C, (e + 1) * C),
+                       j == VP and e == 2, j == QP and e == 3)
 
-        def late_passes(acc, ct, j, start, stop):
-            for i in range(4):
-                s = 4 + i
-                mx(acc[:, i * P:(i + 1) * P], slots(j, s * P, (s + 1) * P), weights(j, s // 2, ct * P, (ct + 1) * P),
-                   start and i == 0, stop and i == 3)
-
-        def late_copies(acc, ct):
-            for i in range(4):
-                gated_copy(late[ct][:, i, :], acc[:, i * P:(i + 1) * P], gate_col, 4 + i)
-
-        def tail_passes(acc, j, start, stop):
-            width = P if j == KP else C
-            cuts = list(range(H, S, width))
-            for u0 in cuts:
-                mx(acc[:, u0 - H:u0 - H + width], weights(j, u0 // C, 0, P), slots(j, u0, u0 + width),
-                   start and u0 == cuts[0], stop and u0 == cuts[-1])
-
-        def fetch(ct, t0, t1):
-            nc.vector.tensor_copy(first[ct][:, t0:t1], dx[ct][:].indirect(pos_t[0][:, t0 // 16:t1 // 16]))
+        def fetch(ct):
+            nc.scalar.activation(first[ct][:], dx[ct][:].indirect(pos_t[0][:]), COPY)
 
         def fetch_add(ct, t0, t1):
             nc.vector.tensor_tensor(res[ct][:, t0:t1], dx[ct][:].indirect(pos_t[1][:, t0 // 16:t1 // 16]),
                                     first[ct][:, t0:t1], ADD)
             nc.sync.dma_start(out[ct * P:(ct + 1) * P, t0:t1], res[ct][:, t0:t1])
 
-        for j in (QP, KP, VP):
-            gather_words(j)
         gate_bank = bank(4)
         nc.tensor.transpose(gate_bank[:, 0:P], gate_rows[:], ident[:])
         nc.scalar.copy(gate_spread[:], gate_bank[:, 4:8])
-        nc.scalar.copy(gate_col[:], gate_bank[:, 0:2 * E])
+        for half in range(2):
+            nc.scalar.copy(gate_col[half][:], gate_bank[:, 4 * half:4 * half + 4])
         spread = bank(5)
         for i in range(4):
             nc.tensor.transpose(spread[:, i * P:(i + 1) * P], gate_spread[:, i:i + 1].to_broadcast([P, P]), ident[:])
         nc.scalar.copy(gate_tail[:], spread[:])
+
+        nc.vector.tensor_copy(q_words[:], grad_words[QP][:].indirect(offs_t[:]))
+        for j in (KP, VP):
+            gather_words(j, 0)
         cast(0)
         cast(1)
-        for e in LATE:
-            cast_late(e)
-        gather_scales(QP, 0)
-        quantize_early(0)
-        quantize_early(1)
+        for e in (2, 3):
+            for h in range(2):
+                cast_late(e, h)
         gather_scales(KP, 0)
         gather_scales(VP, 0)
+        quantize_early(0)
+        gather_scales(QP, 0)
+        quantize_early(1)
         sums = [bank(s) for s in range(4)]
-        for j in (QP, KP, VP):
-            for s in range(4):
-                mx(sums[s][:], slots(j, s * P, (s + 1) * P), weights(j, s // 2, 0, K), j == QP, j == VP)
+        for s0, projections in ((0, (KP,)), (2, (KP,)), (0, (VP, QP)), (2, (VP, QP))):
+            for j in projections:
+                for s in (s0, s0 + 1):
+                    mx(sums[s][:], slots(j, s * P, (s + 1) * P), weights(j, s // 2, 0, K), j == KP, j == QP)
         for s in range(4):
-            gated_copy(head[:, s, :], sums[s][:, 0:P], gate_col, s)
-        turn(0, 0, [head[:, s, :] for s in range(4)], 4)
-        for s in range(4):
-            gated_copy(rest[s][:], sums[s][:, P:K], gate_col, s)
+            gated_copy(early[s][:], sums[s][:], s)
+        order = (1, 2, 3, 0)
+        for n, ct in enumerate(order):
+            turn(ct, 0, [early[s][:, ct * P:(ct + 1) * P] for s in range(4)], n)
 
-        gather_scales(KP, 1)
-        gather_scales(QP, 1)
+        gather_words(VP, 1)
         gather_scales(VP, 1)
-        for ct in range(CT - 1):
+        gather_scales(QP, 1)
+        gather_words(KP, 1)
+        gather_scales(KP, 1)
+        late_sums = [bank(n) for n in (6, 7, 4, 5)]
+        for ct in range(CT):
             quantize_late(ct)
-        tail = bank(5)
-        late_sums = {1: bank(6), 2: bank(7)}
-        tail_passes(tail, KP, True, False)
-        for ct in (1, 2):
-            late_passes(late_sums[ct], ct, KP, True, False)
-        tail_passes(tail, VP, False, False)
-        tail_passes(tail, QP, False, True)
-        nc.vector.tensor_tensor(dx[0][:, H:S], tail[:], gate_tail[:], MULT)
-        quantize_end(2)
-        fetch(0, 0, T)
-        quantize_end(3)
-        for ct in (1, 2):
-            late_passes(late_sums[ct], ct, QP, False, False)
-            late_passes(late_sums[ct], ct, VP, False, True)
-        late_copies(late_sums[1], 1)
-        turn_early(1, 5)
-        turn(1, 1, [late[1][:, i, :] for i in range(4)], 4)
-        turn_early(2, 6)
-        late_copies(late_sums[2], 2)
-        turn(2, 1, [late[2][:, i, :] for i in range(4)], 1)
-        late_sums[3] = bank(0)
-        for j in (KP, VP, QP):
-            late_passes(late_sums[3], 3, j, j == KP, j == QP)
-        late_copies(late_sums[3], 3)
-        turn_early(3, 1)
-        turn(3, 1, [late[3][:, i, :] for i in range(4)], 3)
+        for ct in range(CT):
+            late_passes(late_sums[ct], ct, VP)
+        for ct in range(CT):
+            late_passes(late_sums[ct], ct, KP)
+            late_passes(late_sums[ct], ct, QP)
+        for i in range(4):
+            gated_copy(late0[:, i, :], late_sums[0][:, i * P:(i + 1) * P], 4 + i)
+        for ct in range(1, CT):
+            nc.vector.tensor_tensor(dx[ct][:, H:S], late_sums[ct][:], gate_tail[:], MULT)
+        turn(0, 1, [late0[:, i, :] for i in range(4)], 0)
 
-        fetch_add(0, 0, T)
-        fetch(1, 0, T)
-        fetch(2, 0, T)
-        fetch_add(1, 0, T)
-        fetch_add(2, 0, T)
-        parts = ((0, 3 * T // 4), (3 * T // 4, T))
-        for t0, t1 in parts:
-            fetch(3, t0, t1)
-        for t0, t1 in parts:
-            fetch_add(3, t0, t1)
+        for ct in order:
+            fetch(ct)
+        for ct in order[:-1]:
+            fetch_add(ct, 0, T)
+        for t0, t1 in ((0, 3 * T // 4), (3 * T // 4, T)):
+            fetch_add(0, t0, t1)

@@ -48,8 +48,7 @@ def tile_moe_qkb_kernel(
         RAW1 = 0
         ROUND0 = 8 * KIB
         EARLY3 = 12 * KIB
-        GATE = 14 * KIB
-        COLS = 16 * KIB
+        GATE = 15 * KIB
 
         offs_t = keep.tile([P, S // 16], U16, name="offs_t")
         pos_t = [keep.tile([P, T // 16], U16, name="pos%d" % i) for i in range(2)]
@@ -67,7 +66,7 @@ def tile_moe_qkb_kernel(
             [sb([P, H], U32, "slot_words0_" + names[j])[:],
              at(RAW1 + 2 * KIB * j, [P, H], U32, "slot_words1_" + names[j])[:]] for j in (KP, VP)]
         slot_scales = [[sb([P, H], U8, "slot_scales0_" + names[j]),
-                        at(COLS if j == KP else RAW1 + 6 * KIB + H * j, [P, H], U8, "slot_scales1_" + names[j])]
+                        at(RAW1 + 6 * KIB + H * j, [P, H], U8, "slot_scales1_" + names[j])]
                        for j in range(3)]
         wk_plane = sb([P, E, K], U8, "wk_plane")
         wv_plane = sb([P, K], U8, "wv_plane")
@@ -79,14 +78,14 @@ def tile_moe_qkb_kernel(
         late_codes = [sb([P, 2 * P], U32, "late_codes%d" % ct) for ct in range(CT)]
         late_plane = [at(EARLY3 + ct * 2 * P, [P, 2 * P], U8, "late_plane%d" % ct) for ct in range(CT)]
         gate_rows = sb([P, P], F32, "gate_rows")
-        gate_col = [at(COLS, [P, 4], F32, "gate_col0"), sb([P, 4], F32, "gate_col1")]
+        gate_col = sb([P, 4], F32, "gate_col")
         gate_tail = at(GATE, [P, H], F32, "gate_tail")
         ident = sb([P, P], F32, "ident")
         early = [sb([P, K], F32, "early%d" % s) for s in range(3)] + [at(EARLY3, [P, K], F32, "early3")]
-        late0 = sb([P, 4, P], F32, "late0")
         dx = [sb([P, S], F32, "dx%d" % ct) for ct in range(CT)]
         first = [sb([P, T], F32, "first%d" % ct) for ct in range(CT)]
-        res = [at(GATE, [P, T], F32, "res1") if ct == 1 else sb([P, T], F32, "res%d" % ct) for ct in range(CT)]
+        res = [at(GATE + (2 * ct - 1) * KIB, [P, T], F32, "res%d" % ct) if ct < 2 else sb([P, T], F32, "res%d" % ct)
+               for ct in range(CT)]
 
         def load_grad_words(j):
             words = grad_words_in[j][0].rearrange("p t d -> p (t d)").bitcast(I32)
@@ -118,8 +117,8 @@ def tile_moe_qkb_kernel(
             words = wv_words.rearrange("e s p c d -> p (e s) (c d)")[:, e0:e0 + 2, b0:b1]
             nc.sync.dma_start(dst[:].bitcast(I32), words.bitcast(I32))
 
-        for j in (KP, VP, QP):
-            nc.vector.memset(grad_scales[j][:, 0:T].bitcast(I32), 0)
+        for j in (KP, QP, VP):
+            nc.gpsimd.memset(grad_scales[j][:, 0:T].bitcast(I32), 0)
         make_identity(nc, ident[:])
         load_wk_plane()
         load_grad_words(QP)
@@ -130,10 +129,10 @@ def tile_moe_qkb_kernel(
         load_wk(0)
         load_wq(0)
         load_grad_scales(KP, 0, 4)
-        load_grad_scales(VP, 0, 2)
+        load_grad_scales(QP, 0, 2)
         load_wq(1)
-        load_grad_scales(VP, 2, 4)
-        load_grad_scales(QP, 0, 4)
+        load_grad_scales(QP, 2, 4)
+        load_grad_scales(VP, 0, 4)
         load_wq(2)
         load_wv(wv_early, 0, 0, 4 * K)
         load_wv_plane()
@@ -199,7 +198,7 @@ def tile_moe_qkb_kernel(
                                 rhs_scale=moving[1], start=start, stop=stop)
 
         def gated_copy(dst, src, s):
-            nc.scalar.activation(dst, src, COPY, scale=gate_col[s // 4][:, s % 4:s % 4 + 1])
+            nc.scalar.activation(dst, src, COPY, scale=gate_col[:, s:s + 1])
 
         def turn(ct, half, blocks, n):
             turned = bank(n)
@@ -209,18 +208,12 @@ def tile_moe_qkb_kernel(
 
         def late_passes(acc, ct, j):
             cols = (ct * P, (ct + 1) * P)
-            if ct == 0:
-                for i in range(4):
-                    u0 = H + i * P
-                    mx(acc[:, i * P:(i + 1) * P], slots(j, u0, u0 + P), weights(j, u0 // C, *cols),
-                       j == VP and i == 0, j == QP and i == 3)
-            else:
-                for e in (2, 3):
-                    mx(acc[:, (e - 2) * C:(e - 1) * C], weights(j, e, *cols), slots(j, e * C, (e + 1) * C),
-                       j == VP and e == 2, j == QP and e == 3)
+            for e in (2, 3):
+                mx(acc[:, (e - 2) * C:(e - 1) * C], weights(j, e, *cols), slots(j, e * C, (e + 1) * C),
+                   j == VP and e == 2, j == KP and e == 3)
 
-        def fetch(ct):
-            nc.scalar.activation(first[ct][:], dx[ct][:].indirect(pos_t[0][:]), COPY)
+        def fetch(ct, t0, t1):
+            nc.scalar.activation(first[ct][:, t0:t1], dx[ct][:].indirect(pos_t[0][:, t0 // 16:t1 // 16]), COPY)
 
         def fetch_add(ct, t0, t1):
             nc.vector.tensor_tensor(res[ct][:, t0:t1], dx[ct][:].indirect(pos_t[1][:, t0 // 16:t1 // 16]),
@@ -230,8 +223,7 @@ def tile_moe_qkb_kernel(
         gate_bank = bank(4)
         nc.tensor.transpose(gate_bank[:, 0:P], gate_rows[:], ident[:])
         nc.scalar.copy(gate_spread[:], gate_bank[:, 4:8])
-        for half in range(2):
-            nc.scalar.copy(gate_col[half][:], gate_bank[:, 4 * half:4 * half + 4])
+        nc.scalar.copy(gate_col[:], gate_bank[:, 0:4])
         spread = bank(5)
         for i in range(4):
             nc.tensor.transpose(spread[:, i * P:(i + 1) * P], gate_spread[:, i:i + 1].to_broadcast([P, P]), ident[:])
@@ -246,43 +238,39 @@ def tile_moe_qkb_kernel(
             for h in range(2):
                 cast_late(e, h)
         gather_scales(KP, 0)
-        gather_scales(VP, 0)
         quantize_early(0)
         gather_scales(QP, 0)
+        gather_scales(VP, 0)
         quantize_early(1)
         sums = [bank(s) for s in range(4)]
-        for s0, projections in ((0, (KP,)), (2, (KP,)), (0, (VP, QP)), (2, (VP, QP))):
+        for s0, projections in ((0, (KP,)), (2, (KP,)), (0, (QP, VP)), (2, (VP, QP))):
             for j in projections:
                 for s in (s0, s0 + 1):
-                    mx(sums[s][:], slots(j, s * P, (s + 1) * P), weights(j, s // 2, 0, K), j == KP, j == QP)
+                    mx(sums[s][:], slots(j, s * P, (s + 1) * P), weights(j, s // 2, 0, K), j == KP,
+                       j == (VP if s0 == 0 else QP))
         for s in range(4):
             gated_copy(early[s][:], sums[s][:], s)
-        order = (1, 2, 3, 0)
-        for n, ct in enumerate(order):
-            turn(ct, 0, [early[s][:, ct * P:(ct + 1) * P] for s in range(4)], n)
+        for ct in range(CT):
+            turn(ct, 0, [early[s][:, ct * P:(ct + 1) * P] for s in range(4)], 4 + ct)
 
-        gather_words(VP, 1)
-        gather_scales(VP, 1)
+        for j in (VP, KP):
+            gather_words(j, 1)
+            gather_scales(j, 1)
         gather_scales(QP, 1)
-        gather_words(KP, 1)
-        gather_scales(KP, 1)
-        late_sums = [bank(n) for n in (6, 7, 4, 5)]
+        late_sums = [bank(n) for n in (1, 2, 3, 4)]
         for ct in range(CT):
             quantize_late(ct)
         for ct in range(CT):
             late_passes(late_sums[ct], ct, VP)
         for ct in range(CT):
-            late_passes(late_sums[ct], ct, KP)
             late_passes(late_sums[ct], ct, QP)
-        for i in range(4):
-            gated_copy(late0[:, i, :], late_sums[0][:, i * P:(i + 1) * P], 4 + i)
-        for ct in range(1, CT):
+            late_passes(late_sums[ct], ct, KP)
+        for ct in range(CT):
             nc.vector.tensor_tensor(dx[ct][:, H:S], late_sums[ct][:], gate_tail[:], MULT)
-        turn(0, 1, [late0[:, i, :] for i in range(4)], 0)
 
-        for ct in order:
-            fetch(ct)
-        for ct in order[:-1]:
+        for ct in range(CT):
+            fetch(ct, 0, T)
+        for ct in range(CT - 1):
             fetch_add(ct, 0, T)
         for t0, t1 in ((0, 3 * T // 4), (3 * T // 4, T)):
-            fetch_add(0, t0, t1)
+            fetch_add(CT - 1, t0, t1)

@@ -160,7 +160,7 @@ def tile_moe_qkb_kernel(
         def cast_late(e, h):
             dst = rounded_late[h][:, :, e - 2, :, :]
             src = raw[e][:, :, 2 * h * P:2 * (h + 1) * P]
-            if e == E - 1:
+            if e == E - 1 and h == 1:
                 nc.gpsimd.tensor_scalar(dst, src.rearrange("p j (t c) -> p t c j", t=2), 1.0, 0.0, MULT, ADD)
             else:
                 nc.scalar.copy(dst.rearrange("p t (c i) j -> p t c j i", i=4),

@@ -49,6 +49,7 @@ def tile_moe_qkb_kernel(
         ROUND0 = 8 * KIB
         EARLY3 = 12 * KIB
         GATE = 15 * KIB
+        FIRST = 18 * KIB
 
         offs_t = keep.tile([P, S // 16], U16, name="offs_t")
         pos_t = [keep.tile([P, T // 16], U16, name="pos%d" % i) for i in range(2)]
@@ -83,9 +84,10 @@ def tile_moe_qkb_kernel(
         ident = sb([P, P], F32, "ident")
         early = [sb([P, K], F32, "early%d" % s) for s in range(3)] + [at(EARLY3, [P, K], F32, "early3")]
         dx = [sb([P, S], F32, "dx%d" % ct) for ct in range(CT)]
-        first = [sb([P, T], F32, "first%d" % ct) for ct in range(CT)]
-        res = [at(GATE + (2 * ct - 1) * KIB, [P, T], F32, "res%d" % ct) if ct < 2 else sb([P, T], F32, "res%d" % ct)
-               for ct in range(CT)]
+        first = [at(FIRST + 2 * ct * KIB, [P, T], F32, "first%d" % ct) if ct < 2 else sb([P, T], F32, "first%d" % ct)
+                 for ct in range(CT)]
+        res = [at(GATE + (2 * ct - 1) * KIB, [P, T], F32, "res%d" % ct) if ct < 2
+               else at(FIRST + 2 * (ct - 2) * KIB, [P, T], F32, "res%d" % ct) for ct in range(CT)]
 
         def load_grad_words(j):
             words = grad_words_in[j][0].rearrange("p t d -> p (t d)").bitcast(I32)
@@ -139,8 +141,8 @@ def tile_moe_qkb_kernel(
         load_wq(3)
         load_wk(1)
         load_wv(wv_late[0], 2, 0, 2 * K)
-        load_wv(wv_late[1], 2, 2 * K, 4 * K)
         nc.sync.dma_start(pos_t[0][:], pos1)
+        load_wv(wv_late[1], 2, 2 * K, 4 * K)
         nc.sync.dma_start(pos_t[1][:], pos2)
 
         def gather(dst, window, half):
@@ -206,11 +208,14 @@ def tile_moe_qkb_kernel(
                 nc.tensor.transpose(turned[:, i * P:(i + 1) * P], block, ident[:])
             nc.scalar.copy(dx[ct][:, half * H:(half + 1) * H], turned[:])
 
+        def late_order(ct):
+            return (VP, QP, KP) if ct < 2 else (KP, QP, VP)
+
         def late_passes(acc, ct, j):
             cols = (ct * P, (ct + 1) * P)
             for e in (2, 3):
                 mx(acc[:, (e - 2) * C:(e - 1) * C], weights(j, e, *cols), slots(j, e * C, (e + 1) * C),
-                   j == VP and e == 2, j == KP and e == 3)
+                   j == late_order(ct)[0] and e == 2, j == late_order(ct)[2] and e == 3)
 
         def fetch(ct, t0, t1):
             nc.scalar.activation(first[ct][:, t0:t1], dx[ct][:].indirect(pos_t[0][:, t0 // 16:t1 // 16]), COPY)
@@ -261,16 +266,18 @@ def tile_moe_qkb_kernel(
         for ct in range(CT):
             quantize_late(ct)
         for ct in range(CT):
-            late_passes(late_sums[ct], ct, VP)
+            late_passes(late_sums[ct], ct, late_order(ct)[0])
         for ct in range(CT):
-            late_passes(late_sums[ct], ct, QP)
-            late_passes(late_sums[ct], ct, KP)
+            for j in late_order(ct)[1:]:
+                late_passes(late_sums[ct], ct, j)
         for ct in range(CT):
             nc.vector.tensor_tensor(dx[ct][:, H:S], late_sums[ct][:], gate_tail[:], MULT)
 
-        for ct in range(CT):
+        for ct in range(CT - 1):
             fetch(ct, 0, T)
+        for t0, t1 in ((0, T // 2), (T // 2, T)):
+            fetch(CT - 1, t0, t1)
         for ct in range(CT - 1):
             fetch_add(ct, 0, T)
-        for t0, t1 in ((0, 3 * T // 4), (3 * T // 4, T)):
+        for t0, t1 in ((0, T // 2), (T // 2, 3 * T // 4), (3 * T // 4, T)):
             fetch_add(CT - 1, t0, t1)

@@ -56,16 +56,15 @@ def tile_moe_qkb_kernel(
         names = ("q", "k", "v")
         grad_words_in = (dq_words, dk_words, dv_words)
         grad_scales_in = (dq_scales, dk_scales, dv_scales)
-        grad_words = [sb([P, (3 if n == "q" else 2) * T], U32, "grad_words_" + n) for n in names]
+        grad_words = [sb([P, (2 if n == "v" else 3) * T], U32, "grad_words_" + n) for n in names]
         grad_scales = [sb([P, 2 * T], U8, "grad_scales_" + n) for n in names]
         raw = [at(RAW1, [P, 4, K], F32, "raw1") if e == 1 else sb([P, 4, K], F32, "raw%d" % e) for e in range(E)]
         gate_spread = at(ROUND0, [P, 4], F32, "gate_spread")
         rounded = [at(ROUND0, [P, K, 4], BF16, "rounded0"), sb([P, K, 4], BF16, "rounded1")]
         rounded_late = [sb([P, 2, 2, P, 4], BF16, "rounded_late%d" % h) for h in range(2)]
-        q_words = sb([P, S], U32, "slot_words_q")
-        slot_words = [[q_words[:, 0:H], q_words[:, H:S]]] + [
-            [sb([P, H], U32, "slot_words0_" + names[j])[:],
-             at(RAW1 + 2 * KIB * j, [P, H], U32, "slot_words1_" + names[j])[:]] for j in (KP, VP)]
+        whole_words = [sb([P, S], U32, "slot_words_" + names[j]) for j in (QP, KP)]
+        slot_words = [[whole_words[j][:, 0:H], whole_words[j][:, H:S]] for j in (QP, KP)] + [
+            [sb([P, H], U32, "slot_words0_v")[:], at(RAW1, [P, H], U32, "slot_words1_v")[:]]]
         slot_scales = [[sb([P, H], U8, "slot_scales0_" + names[j]),
                         at(RAW1 + 6 * KIB + H * j, [P, H], U8, "slot_scales1_" + names[j])]
                        for j in range(3)]
@@ -234,9 +233,9 @@ def tile_moe_qkb_kernel(
             nc.tensor.transpose(spread[:, i * P:(i + 1) * P], gate_spread[:, i:i + 1].to_broadcast([P, P]), ident[:])
         nc.scalar.copy(gate_tail[:], spread[:])
 
-        nc.vector.tensor_copy(q_words[:], grad_words[QP][:].indirect(offs_t[:]))
-        for j in (KP, VP):
-            gather_words(j, 0)
+        for j in (QP, KP):
+            nc.vector.tensor_copy(whole_words[j][:], grad_words[j][:].indirect(offs_t[:]))
+        gather_words(VP, 0)
         cast(0)
         cast(1)
         for e in (2, 3):
@@ -258,10 +257,9 @@ def tile_moe_qkb_kernel(
         for ct in range(CT):
             turn(ct, 0, [early[s][:, ct * P:(ct + 1) * P] for s in range(4)], 4 + ct)
 
-        for j in (VP, KP):
-            gather_words(j, 1)
+        gather_words(VP, 1)
+        for j in (VP, KP, QP):
             gather_scales(j, 1)
-        gather_scales(QP, 1)
         late_sums = [bank(n) for n in (1, 2, 3, 4)]
         for ct in range(CT):
             quantize_late(ct)

@@ -50,6 +50,8 @@ def tile_moe_qkb_kernel(
         EARLY3 = 12 * KIB
         GATE = 15 * KIB
         FIRST = 18 * KIB
+        COLS = 22 * KIB
+        ROUND1 = 24 * KIB
 
         offs_t = keep.tile([P, S // 16], U16, name="offs_t")
         pos_t = [keep.tile([P, T // 16], U16, name="pos%d" % i) for i in range(2)]
@@ -60,8 +62,9 @@ def tile_moe_qkb_kernel(
         grad_scales = [sb([P, 2 * T], U8, "grad_scales_" + n) for n in names]
         raw = [at(RAW1, [P, 4, K], F32, "raw1") if e == 1 else sb([P, 4, K], F32, "raw%d" % e) for e in range(E)]
         gate_spread = at(ROUND0, [P, 4], F32, "gate_spread")
-        rounded = [at(ROUND0, [P, K, 4], BF16, "rounded0"), sb([P, K, 4], BF16, "rounded1")]
-        rounded_late = [sb([P, 2, 2, P, 4], BF16, "rounded_late%d" % h) for h in range(2)]
+        rounded = [at(ROUND0, [P, K, 4], BF16, "rounded0"), at(ROUND1, [P, K, 4], BF16, "rounded1")]
+        rounded_late = [at(ROUND1, [P, K // 2, 4], BF16, "rounded_late0"), sb([P, K // 2, 4], BF16, "rounded_late1"),
+                        sb([P, K // 2, 4], BF16, "rounded_late2"), at(COLS, [P, K // 2, 4], BF16, "rounded_late3")]
         whole_words = [sb([P, S], U32, "slot_words_" + names[j]) for j in (QP, KP)]
         slot_words = [[whole_words[j][:, 0:H], whole_words[j][:, H:S]] for j in (QP, KP)] + [
             [sb([P, H], U32, "slot_words0_v")[:], at(RAW1, [P, H], U32, "slot_words1_v")[:]]]
@@ -78,7 +81,7 @@ def tile_moe_qkb_kernel(
         late_codes = [sb([P, 2 * P], U32, "late_codes%d" % ct) for ct in range(CT)]
         late_plane = [at(EARLY3 + ct * 2 * P, [P, 2 * P], U8, "late_plane%d" % ct) for ct in range(CT)]
         gate_rows = sb([P, P], F32, "gate_rows")
-        gate_col = sb([P, 4], F32, "gate_col")
+        gate_col = at(COLS, [P, 4], F32, "gate_col")
         gate_tail = at(GATE, [P, H], F32, "gate_tail")
         ident = sb([P, P], F32, "ident")
         early = [sb([P, K], F32, "early%d" % s) for s in range(3)] + [at(EARLY3, [P, K], F32, "early3")]
@@ -159,13 +162,12 @@ def tile_moe_qkb_kernel(
                            raw[e][:].rearrange("p j (c i) -> p c j i", i=4))
 
         def cast_late(e, h):
-            dst = rounded_late[h][:, :, e - 2, :, :]
-            src = raw[e][:, :, 2 * h * P:2 * (h + 1) * P]
-            if e == E - 1 and h == 1:
-                nc.gpsimd.tensor_scalar(dst, src.rearrange("p j (t c) -> p t c j", t=2), 1.0, 0.0, MULT, ADD)
+            dst = rounded_late[2 * (e - 2) + h][:]
+            src = raw[e][:, :, h * K // 2:(h + 1) * K // 2]
+            if h == 0:
+                nc.gpsimd.tensor_scalar(dst, src.rearrange("p j c -> p c j"), 1.0, 0.0, MULT, ADD)
             else:
-                nc.scalar.copy(dst.rearrange("p t (c i) j -> p t c j i", i=4),
-                               src.rearrange("p j (t c i) -> p t c j i", t=2, i=4))
+                nc.scalar.copy(dst.rearrange("p (c i) j -> p c j i", i=4), src.rearrange("p j (c i) -> p c j i", i=4))
 
         def quantize(codes, plane, values):
             nc.vector.quantize_mx(out=codes[:].bitcast(FP8X4), scales=plane[:], in_=values)
@@ -173,16 +175,16 @@ def tile_moe_qkb_kernel(
         def quantize_early(e):
             quantize(wq_codes[e], wq_plane[e], rounded[e][:].rearrange("p c j -> p (c j)"))
 
-        def quantize_late(ct):
-            values = rounded_late[ct // 2][:, ct % 2, :, :, :]
-            quantize(late_codes[ct], late_plane[ct], values.rearrange("p e c j -> p (e c j)"))
+        def quantize_late(i):
+            quantize(late_codes[i], late_plane[i], rounded_late[i][:].rearrange("p c j -> p (c j)"))
 
         def weights(j, e, c0, c1):
             if j == QP and e < 2:
                 return wq_codes[e][:, c0:c1].bitcast(FP8X4), wq_plane[e][:, c0:c1]
             if j == QP:
-                ct, cols = c0 // P, slice((e - 2) * P, (e - 1) * P)
-                return late_codes[ct][:, cols].bitcast(FP8X4), late_plane[ct][:, cols]
+                h, q0 = divmod(c0, K // 2)
+                i, cols = 2 * (e - 2) + h, slice(q0, q0 + c1 - c0)
+                return late_codes[i][:, cols].bitcast(FP8X4), late_plane[i][:, cols]
             if j == KP:
                 return wk_pairs[e // 2][:, e % 2, 2 * c0:2 * c1].bitcast(FP4X4), wk_plane[:, e, c0:c1]
             h, v0 = divmod(c0, K // 2)
@@ -207,14 +209,10 @@ def tile_moe_qkb_kernel(
                 nc.tensor.transpose(turned[:, i * P:(i + 1) * P], block, ident[:])
             nc.scalar.copy(dx[ct][:, half * H:(half + 1) * H], turned[:])
 
-        def late_order(ct):
-            return (VP, QP, KP) if ct < 2 else (KP, QP, VP)
-
-        def late_passes(acc, ct, j):
-            cols = (ct * P, (ct + 1) * P)
-            for e in (2, 3):
-                mx(acc[:, (e - 2) * C:(e - 1) * C], weights(j, e, *cols), slots(j, e * C, (e + 1) * C),
-                   j == late_order(ct)[0] and e == 2, j == late_order(ct)[2] and e == 3)
+        def late_passes(ct, j, experts=(2, 3)):
+            for e in experts:
+                mx(late_sums[ct][:, (e - 2) * C:(e - 1) * C], weights(j, e, ct * P, (ct + 1) * P),
+                   slots(j, e * C, (e + 1) * C), j == KP and e == 2, j == QP and e == 3)
 
         def fetch(ct, t0, t1):
             nc.scalar.activation(first[ct][:, t0:t1], dx[ct][:].indirect(pos_t[0][:, t0 // 16:t1 // 16]), COPY)
@@ -257,17 +255,25 @@ def tile_moe_qkb_kernel(
         for ct in range(CT):
             turn(ct, 0, [early[s][:, ct * P:(ct + 1) * P] for s in range(4)], 4 + ct)
 
+        gather_scales(KP, 1)
         gather_words(VP, 1)
-        for j in (VP, KP, QP):
+        for j in (VP, QP):
             gather_scales(j, 1)
         late_sums = [bank(n) for n in (1, 2, 3, 4)]
         for ct in range(CT):
             quantize_late(ct)
-        for ct in range(CT):
-            late_passes(late_sums[ct], ct, late_order(ct)[0])
-        for ct in range(CT):
-            for j in late_order(ct)[1:]:
-                late_passes(late_sums[ct], ct, j)
+        for ct in range(CT - 1):
+            late_passes(ct, KP)
+        for ct in (0, 1):
+            late_passes(ct, QP, (2,))
+            late_passes(ct, VP)
+        for ct in (0, 1):
+            late_passes(ct, QP, (3,))
+        late_passes(3, KP)
+        for ct in (2, 3):
+            late_passes(ct, QP, (2,))
+            late_passes(ct, VP)
+            late_passes(ct, QP, (3,))
         for ct in range(CT):
             nc.vector.tensor_tensor(dx[ct][:, H:S], late_sums[ct][:], gate_tail[:], MULT)
 

@@ -64,7 +64,7 @@ def tile_moe_qkb_kernel(
         gate_spread = at(ROUND0, [P, 4], F32, "gate_spread")
         rounded = [at(ROUND0, [P, K, 4], BF16, "rounded0"), at(ROUND1, [P, K, 4], BF16, "rounded1")]
         rounded_late = [at(ROUND1, [P, K // 2, 4], BF16, "rounded_late0"), sb([P, K // 2, 4], BF16, "rounded_late1"),
-                        sb([P, K // 2, 4], BF16, "rounded_late2"), at(COLS, [P, K // 2, 4], BF16, "rounded_late3")]
+                        at(COLS, [P, K // 2, 4], BF16, "rounded_late2"), sb([P, K // 2, 4], BF16, "rounded_late3")]
         whole_words = [sb([P, S], U32, "slot_words_" + names[j]) for j in (QP, KP)]
         slot_words = [[whole_words[j][:, 0:H], whole_words[j][:, H:S]] for j in (QP, KP)] + [
             [sb([P, H], U32, "slot_words0_v")[:], at(RAW1, [P, H], U32, "slot_words1_v")[:]]]
@@ -121,13 +121,14 @@ def tile_moe_qkb_kernel(
             words = wv_words.rearrange("e s p c d -> p (e s) (c d)")[:, e0:e0 + 2, b0:b1]
             nc.sync.dma_start(dst[:].bitcast(I32), words.bitcast(I32))
 
+        nc.gpsimd.memset(gate_rows[:], 0.0)
         for j in (KP, QP, VP):
             nc.gpsimd.memset(grad_scales[j][:, 0:T].bitcast(I32), 0)
         make_identity(nc, ident[:])
         load_wk_plane()
         load_grad_words(QP)
         nc.sync.dma_start(offs_t[:], offs)
-        nc.sync.dma_start(gate_rows[:], gate.rearrange("a (s p) -> (a s) p", p=P)[0:P, :])
+        nc.sync.dma_start(gate_rows[0:2 * E, :], gate[0].rearrange("(s p) -> s p", p=P))
         load_grad_words(KP)
         load_grad_words(VP)
         load_wk(0)
@@ -140,8 +141,8 @@ def tile_moe_qkb_kernel(
         load_wq(2)
         load_wv(wv_early, 0, 0, 4 * K)
         load_wv_plane()
-        load_wq(3)
         load_wk(1)
+        load_wq(3)
         load_wv(wv_late[0], 2, 0, 2 * K)
         nc.sync.dma_start(pos_t[0][:], pos1)
         load_wv(wv_late[1], 2, 2 * K, 4 * K)
@@ -164,7 +165,7 @@ def tile_moe_qkb_kernel(
         def cast_late(e, h):
             dst = rounded_late[2 * (e - 2) + h][:]
             src = raw[e][:, :, h * K // 2:(h + 1) * K // 2]
-            if h == 0:
+            if h == e - 2:
                 nc.gpsimd.tensor_scalar(dst, src.rearrange("p j c -> p c j"), 1.0, 0.0, MULT, ADD)
             else:
                 nc.scalar.copy(dst.rearrange("p (c i) j -> p c j i", i=4), src.rearrange("p j (c i) -> p c j i", i=4))
@@ -259,18 +260,12 @@ def tile_moe_qkb_kernel(
         gather_words(VP, 1)
         for j in (VP, QP):
             gather_scales(j, 1)
-        late_sums = [bank(n) for n in (1, 2, 3, 4)]
+        late_sums = [bank(ct) for ct in range(CT)]
         for ct in range(CT):
             quantize_late(ct)
-        for ct in range(CT - 1):
+        for ct in range(CT):
             late_passes(ct, KP)
-        for ct in (0, 1):
-            late_passes(ct, QP, (2,))
-            late_passes(ct, VP)
-        for ct in (0, 1):
-            late_passes(ct, QP, (3,))
-        late_passes(3, KP)
-        for ct in (2, 3):
+        for ct in range(CT):
             late_passes(ct, QP, (2,))
             late_passes(ct, VP)
             late_passes(ct, QP, (3,))
@@ -279,9 +274,10 @@ def tile_moe_qkb_kernel(
 
         for ct in range(CT - 1):
             fetch(ct, 0, T)
-        for t0, t1 in ((0, T // 2), (T // 2, T)):
+        parts = ((0, T // 2), (T // 2, 3 * T // 4), (3 * T // 4, T))
+        for t0, t1 in parts:
             fetch(CT - 1, t0, t1)
         for ct in range(CT - 1):
             fetch_add(ct, 0, T)
-        for t0, t1 in ((0, T // 2), (T // 2, 3 * T // 4), (3 * T // 4, T)):
+        for t0, t1 in parts:
             fetch_add(CT - 1, t0, t1)

@@ -58,16 +58,14 @@ def tile_moe_qkb_kernel(
         names = ("q", "k", "v")
         grad_words_in = (dq_words, dk_words, dv_words)
         grad_scales_in = (dq_scales, dk_scales, dv_scales)
-        grad_words = [sb([P, (2 if n == "v" else 3) * T], U32, "grad_words_" + n) for n in names]
+        grad_words = [sb([P, 3 * T], U32, "grad_words_" + n) for n in names]
         grad_scales = [sb([P, 2 * T], U8, "grad_scales_" + n) for n in names]
         raw = [at(RAW1, [P, 4, K], F32, "raw1") if e == 1 else sb([P, 4, K], F32, "raw%d" % e) for e in range(E)]
         gate_spread = at(ROUND0, [P, 4], F32, "gate_spread")
         rounded = [at(ROUND0, [P, K, 4], BF16, "rounded0"), at(ROUND1, [P, K, 4], BF16, "rounded1")]
         rounded_late = [at(ROUND1, [P, K // 2, 4], BF16, "rounded_late0"), sb([P, K // 2, 4], BF16, "rounded_late1"),
                         at(COLS, [P, K // 2, 4], BF16, "rounded_late2"), sb([P, K // 2, 4], BF16, "rounded_late3")]
-        whole_words = [sb([P, S], U32, "slot_words_" + names[j]) for j in (QP, KP)]
-        slot_words = [[whole_words[j][:, 0:H], whole_words[j][:, H:S]] for j in (QP, KP)] + [
-            [sb([P, H], U32, "slot_words0_v")[:], at(RAW1, [P, H], U32, "slot_words1_v")[:]]]
+        slot_words = [sb([P, S], U32, "slot_words_" + n) for n in names]
         slot_scales = [[sb([P, H], U8, "slot_scales0_" + names[j]),
                         at(RAW1 + 6 * KIB + H * j, [P, H], U8, "slot_scales1_" + names[j])]
                        for j in range(3)]
@@ -148,15 +146,13 @@ def tile_moe_qkb_kernel(
         load_wv(wv_late[1], 2, 2 * K, 4 * K)
         nc.sync.dma_start(pos_t[1][:], pos2)
 
-        def gather(dst, window, half):
-            offsets = offs_t[:, half * H // 16:(half + 1) * H // 16]
-            nc.vector.tensor_copy(dst, window[:].indirect(offsets))
+        def gather_words(j):
+            nc.vector.tensor_copy(slot_words[j][:], grad_words[j][:].indirect(offs_t[:]))
 
-        def gather_words(j, half):
-            gather(slot_words[j][half], grad_words[j], half)
-
-        def gather_scales(j, half):
-            gather(slot_scales[j][half][:], grad_scales[j], half)
+        def gather_scales(j, u0, u1):
+            half = u0 // H
+            nc.vector.tensor_copy(slot_scales[j][half][:, u0 - half * H:u1 - half * H],
+                                  grad_scales[j][:].indirect(offs_t[:, u0 // 16:u1 // 16]))
 
         def cast(e):
             nc.scalar.copy(rounded[e][:].rearrange("p (c i) j -> p c j i", i=4),
@@ -194,8 +190,7 @@ def tile_moe_qkb_kernel(
 
         def slots(j, u0, u1):
             half = u0 // H
-            cols = slice(u0 - half * H, u1 - half * H)
-            return slot_words[j][half][:, cols].bitcast(FP8X4), slot_scales[j][half][:, cols]
+            return slot_words[j][:, u0:u1].bitcast(FP8X4), slot_scales[j][half][:, u0 - half * H:u1 - half * H]
 
         def mx(acc, stationary, moving, start, stop):
             nc.tensor.matmul_mx(out=acc, lhsT=stationary[0], lhsT_scale=stationary[1], rhs=moving[0],
@@ -232,18 +227,18 @@ def tile_moe_qkb_kernel(
             nc.tensor.transpose(spread[:, i * P:(i + 1) * P], gate_spread[:, i:i + 1].to_broadcast([P, P]), ident[:])
         nc.scalar.copy(gate_tail[:], spread[:])
 
-        for j in (QP, KP):
-            nc.vector.tensor_copy(whole_words[j][:], grad_words[j][:].indirect(offs_t[:]))
-        gather_words(VP, 0)
+        for j in (QP, KP, VP):
+            gather_words(j)
         cast(0)
         cast(1)
         for e in (2, 3):
             for h in range(2):
                 cast_late(e, h)
-        gather_scales(KP, 0)
+        gather_scales(KP, 0, H)
         quantize_early(0)
-        gather_scales(QP, 0)
-        gather_scales(VP, 0)
+        gather_scales(QP, 0, H)
+        for e in range(2):
+            gather_scales(VP, e * C, (e + 1) * C)
         quantize_early(1)
         sums = [bank(s) for s in range(4)]
         for s0, projections in ((0, (KP,)), (2, (KP,)), (0, (QP, VP)), (2, (VP, QP))):
@@ -256,10 +251,8 @@ def tile_moe_qkb_kernel(
         for ct in range(CT):
             turn(ct, 0, [early[s][:, ct * P:(ct + 1) * P] for s in range(4)], 4 + ct)
 
-        gather_scales(KP, 1)
-        gather_words(VP, 1)
-        for j in (VP, QP):
-            gather_scales(j, 1)
+        for j in (KP, VP, QP):
+            gather_scales(j, H, S)
         late_sums = [bank(ct) for ct in range(CT)]
         for ct in range(CT):
             quantize_late(ct)

@@ -65,7 +65,8 @@ def tile_moe_qkb_kernel(
         rounded = [at(ROUND0, [P, K, 4], BF16, "rounded0"), at(ROUND1, [P, K, 4], BF16, "rounded1")]
         rounded_late = [at(ROUND1, [P, K // 2, 4], BF16, "rounded_late0"), sb([P, K // 2, 4], BF16, "rounded_late1"),
                         at(COLS, [P, K // 2, 4], BF16, "rounded_late2"), sb([P, K // 2, 4], BF16, "rounded_late3")]
-        slot_words = [sb([P, S], U32, "slot_words_" + n) for n in names]
+        slot_words = [sb([P, S - C if n == "v" else S], U32, "slot_words_" + n) for n in names]
+        last_words = at(RAW1, [P, C], U32, "last_words_v")
         slot_scales = [[sb([P, H], U8, "slot_scales0_" + names[j]),
                         at(RAW1 + 6 * KIB + H * j, [P, H], U8, "slot_scales1_" + names[j])]
                        for j in range(3)]
@@ -137,8 +138,8 @@ def tile_moe_qkb_kernel(
         load_grad_scales(QP, 2, 4)
         load_grad_scales(VP, 0, 4)
         load_wq(2)
-        load_wv(wv_early, 0, 0, 4 * K)
         load_wv_plane()
+        load_wv(wv_early, 0, 0, 4 * K)
         load_wk(1)
         load_wq(3)
         load_wv(wv_late[0], 2, 0, 2 * K)
@@ -147,7 +148,8 @@ def tile_moe_qkb_kernel(
         nc.sync.dma_start(pos_t[1][:], pos2)
 
         def gather_words(j):
-            nc.vector.tensor_copy(slot_words[j][:], grad_words[j][:].indirect(offs_t[:]))
+            count = S - C if j == VP else S
+            nc.vector.tensor_copy(slot_words[j][:], grad_words[j][:].indirect(offs_t[:, 0:count // 16]))
 
         def gather_scales(j, u0, u1):
             half = u0 // H
@@ -190,7 +192,8 @@ def tile_moe_qkb_kernel(
 
         def slots(j, u0, u1):
             half = u0 // H
-            return slot_words[j][:, u0:u1].bitcast(FP8X4), slot_scales[j][half][:, u0 - half * H:u1 - half * H]
+            words = last_words[:] if j == VP and u0 == S - C else slot_words[j][:, u0:u1]
+            return words.bitcast(FP8X4), slot_scales[j][half][:, u0 - half * H:u1 - half * H]
 
         def mx(acc, stationary, moving, start, stop):
             nc.tensor.matmul_mx(out=acc, lhsT=stationary[0], lhsT_scale=stationary[1], rhs=moving[0],
@@ -251,7 +254,9 @@ def tile_moe_qkb_kernel(
         for ct in range(CT):
             turn(ct, 0, [early[s][:, ct * P:(ct + 1) * P] for s in range(4)], 4 + ct)
 
-        for j in (KP, VP, QP):
+        gather_scales(KP, H, S)
+        nc.vector.tensor_copy(last_words[:], grad_words[VP][:].indirect(offs_t[:, (S - C) // 16:S // 16]))
+        for j in (VP, QP):
             gather_scales(j, H, S)
         late_sums = [bank(ct) for ct in range(CT)]
         for ct in range(CT):

@@ -23,6 +23,7 @@ P = 128
 CT = K // P
 QP, KP, VP = 0, 1, 2
 H = S // 2
+SPLIT = 320
 KIB = 1024
 
 
@@ -87,6 +88,7 @@ def tile_moe_qkb_kernel(
         dx = [sb([P, S], F32, "dx%d" % ct) for ct in range(CT)]
         first = [at(FIRST + 2 * ct * KIB, [P, T], F32, "first%d" % ct) if ct < 2 else sb([P, T], F32, "first%d" % ct)
                  for ct in range(CT)]
+        second = sb([P, T - SPLIT], F32, "second")
         res = [at(GATE + (2 * ct - 1) * KIB, [P, T], F32, "res%d" % ct) if ct < 2
                else at(FIRST + 2 * (ct - 2) * KIB, [P, T], F32, "res%d" % ct) for ct in range(CT)]
 
@@ -213,8 +215,8 @@ def tile_moe_qkb_kernel(
                 mx(late_sums[ct][:, (e - 2) * C:(e - 1) * C], weights(j, e, ct * P, (ct + 1) * P),
                    slots(j, e * C, (e + 1) * C), j == KP and e == 2, j == QP and e == 3)
 
-        def fetch(ct, t0, t1):
-            nc.scalar.activation(first[ct][:, t0:t1], dx[ct][:].indirect(pos_t[0][:, t0 // 16:t1 // 16]), COPY)
+        def fetch(dst, ct, choice, t0, t1):
+            nc.scalar.activation(dst, dx[ct][:].indirect(pos_t[choice][:, t0 // 16:t1 // 16]), COPY)
 
         def fetch_add(ct, t0, t1):
             nc.vector.tensor_tensor(res[ct][:, t0:t1], dx[ct][:].indirect(pos_t[1][:, t0 // 16:t1 // 16]),
@@ -270,12 +272,18 @@ def tile_moe_qkb_kernel(
         for ct in range(CT):
             nc.vector.tensor_tensor(dx[ct][:, H:S], late_sums[ct][:], gate_tail[:], MULT)
 
-        for ct in range(CT - 1):
-            fetch(ct, 0, T)
+        shared, last = CT - 2, CT - 1
         parts = ((0, T // 2), (T // 2, 3 * T // 4), (3 * T // 4, T))
+        for ct in range(shared):
+            fetch(first[ct][:], ct, 0, 0, T)
+        fetch(first[shared][:], shared, 0, 0, T)
+        fetch(second[:], shared, 1, SPLIT, T)
         for t0, t1 in parts:
-            fetch(CT - 1, t0, t1)
-        for ct in range(CT - 1):
+            fetch(first[last][:, t0:t1], last, 0, t0, t1)
+        for ct in range(shared):
             fetch_add(ct, 0, T)
+        fetch_add(shared, 0, SPLIT)
+        nc.vector.tensor_tensor(res[shared][:, SPLIT:T], first[shared][:, SPLIT:T], second[:], ADD)
+        nc.sync.dma_start(out[shared * P:last * P, SPLIT:T], res[shared][:, SPLIT:T])
         for t0, t1 in parts:
-            fetch_add(CT - 1, t0, t1)
+            fetch_add(last, t0, t1)

@@ -25,6 +25,7 @@ QP, KP, VP = 0, 1, 2
 H = S // 2
 SPLIT = 320
 KIB = 1024
+ROW0 = (4, 0, 8)
 
 
 def tile_moe_qkb_kernel(
@@ -99,7 +100,7 @@ def tile_moe_qkb_kernel(
         def load_grad_scales(j, q0, q1, queue=nc.sync):
             for q in range(q0, q1):
                 rows = grad_scales_in[j][0][4 * q:4 * q + 4, :].bitcast(I32)
-                queue.dma_start(grad_scales[j][32 * q:32 * q + 4, 0:T].bitcast(I32), rows)
+                queue.dma_start(grad_scales[j][32 * q + ROW0[j]:32 * q + ROW0[j] + 4, 0:T].bitcast(I32), rows)
 
         def load_wk_plane():
             rows = wk_scales.rearrange("e s (q r) c -> r q (e s) c", r=4)
@@ -195,7 +196,7 @@ def tile_moe_qkb_kernel(
         def slots(j, u0, u1):
             half = u0 // H
             words = last_words[:] if j == VP and u0 == S - C else slot_words[j][:, u0:u1]
-            return words.bitcast(FP8X4), slot_scales[j][half][:, u0 - half * H:u1 - half * H]
+            return words.bitcast(FP8X4), slot_scales[j][half][ROW0[j]:P, u0 - half * H:u1 - half * H]
 
         def mx(acc, stationary, moving, start, stop):
             nc.tensor.matmul_mx(out=acc, lhsT=stationary[0], lhsT_scale=stationary[1], rhs=moving[0],

from contextlib import ExitStack

import concourse.mybir as mybir
from concourse.masks import make_identity

K, T, E, C, N = 512, 512, 4, 256, 512
S = E * C
FLOPS = 2 * 3 * N * K * S

F32 = mybir.dt.float32
BF16 = mybir.dt.bfloat16
I32 = mybir.dt.int32
U32 = mybir.dt.uint32
U16 = mybir.dt.uint16
U8 = mybir.dt.uint8
FP8X4 = mybir.dt.float8_e4m3fn_x4
FP4X4 = mybir.dt.float4_e2m1fn_x4
COPY = mybir.ActivationFunctionType.Copy
MULT = mybir.AluOpType.mult
ADD = mybir.AluOpType.add

P = 128
CT = K // P
QP, KP, VP = 0, 1, 2
H = S // 2
SPLIT = 320
KIB = 1024
ROW0 = (4, 0, 8)


def tile_moe_qkb_kernel(
    tc, dq_words, dq_scales, dk_words, dk_scales, dv_words, dv_scales, wq,
    wk_words, wk_scales, wv_words, wv_scales, gate, offs, pos1, pos2, out,
):
    nc = tc.nc
    with ExitStack() as ctx:
        keep = ctx.enter_context(tc.tile_pool(name="keep", bufs=1))
        reuse = ctx.enter_context(tc.tile_pool(name="reuse", bufs=1))
        psum = ctx.enter_context(tc.psum_pool(name="psum", bufs=1))

        def bank(n):
            return psum.tile([P, K], F32, name="bank%d" % n)

        def sb(shape, dtype, name):
            return keep.tile(shape, dtype, name=name, align_bytes=64)

        def at(offset, shape, dtype, name):
            return reuse.tile(shape, dtype, name=name, align_bytes=64, offset=offset)

        RAW1 = 0
        ROUND0 = 8 * KIB
        EARLY3 = 12 * KIB
        GATE = 15 * KIB
        FIRST = 18 * KIB
        COLS = 22 * KIB
        ROUND1 = 24 * KIB

        offs_t = keep.tile([P, S // 16], U16, name="offs_t")
        pos_t = [keep.tile([P, T // 16], U16, name="pos%d" % i) for i in range(2)]
        names = ("q", "k", "v")
        grad_words_in = (dq_words, dk_words, dv_words)
        grad_scales_in = (dq_scales, dk_scales, dv_scales)
        grad_words = [sb([P, 3 * T], U32, "grad_words_" + n) for n in names]
        grad_scales = [sb([P, 2 * T], U8, "grad_scales_" + n) for n in names]
        raw = [at(RAW1, [P, 4, K], F32, "raw1") if e == 1 else sb([P, 4, K], F32, "raw%d" % e) for e in range(E)]
        gate_spread = at(ROUND0, [P, 4], F32, "gate_spread")
        rounded = [at(ROUND0, [P, K, 4], BF16, "rounded0"), at(ROUND1, [P, K, 4], BF16, "rounded1")]
        rounded_late = [at(ROUND1, [P, K // 2, 4], BF16, "rounded_late0"), sb([P, K // 2, 4], BF16, "rounded_late1"),
                        at(COLS, [P, K // 2, 4], BF16, "rounded_late2"), sb([P, K // 2, 4], BF16, "rounded_late3")]
        slot_words = [sb([P, S - C if n == "v" else S], U32, "slot_words_" + n) for n in names]
        last_words = at(RAW1, [P, C], U32, "last_words_v")
        slot_scales = [[sb([P, H], U8, "slot_scales0_" + names[j]),
                        at(RAW1 + 6 * KIB + H * j, [P, H], U8, "slot_scales1_" + names[j])]
                       for j in range(3)]
        wk_plane = sb([P, E, K], U8, "wk_plane")
        wv_plane = sb([P, K], U8, "wv_plane")
        wk_pairs = [sb([P, 2, 2 * K], U8, "wk_pair%d" % i) for i in range(2)]
        wv_early = sb([P, 2, K], U32, "wv_early")
        wv_late = [sb([P, 2, K // 2], U32, "wv_late%d" % h) for h in range(2)]
        wq_codes = [sb([P, K], U32, "wq_codes%d" % e) for e in range(2)]
        wq_plane = [sb([P, K], U8, "wq_plane%d" % e) for e in range(2)]
        late_codes = [sb([P, 2 * P], U32, "late_codes%d" % ct) for ct in range(CT)]
        late_plane = [at(EARLY3 + ct * 2 * P, [P, 2 * P], U8, "late_plane%d" % ct) for ct in range(CT)]
        gate_rows = sb([P, P], F32, "gate_rows")
        gate_col = at(COLS, [P, 4], F32, "gate_col")
        gate_tail = at(GATE, [P, H], F32, "gate_tail")
        ident = sb([P, P], F32, "ident")
        early = [sb([P, K], F32, "early%d" % s) for s in range(3)] + [at(EARLY3, [P, K], F32, "early3")]
        dx = [sb([P, S], F32, "dx%d" % ct) for ct in range(CT)]
        first = [at(FIRST + 2 * ct * KIB, [P, T], F32, "first%d" % ct) if ct < 2 else sb([P, T], F32, "first%d" % ct)
                 for ct in range(CT)]
        second = sb([P, T - SPLIT], F32, "second")
        res = [at(GATE + (2 * ct - 1) * KIB, [P, T], F32, "res%d" % ct) if ct < 2
               else at(FIRST + 2 * (ct - 2) * KIB, [P, T], F32, "res%d" % ct) for ct in range(CT)]

        def load_grad_words(j):
            words = grad_words_in[j][0].rearrange("p t d -> p (t d)").bitcast(I32)
            nc.sync.dma_start(grad_words[j][:, 0:T].bitcast(I32), words)

        def load_grad_scales(j, q0, q1, queue=nc.sync):
            for q in range(q0, q1):
                rows = grad_scales_in[j][0][4 * q:4 * q + 4, :].bitcast(I32)
                queue.dma_start(grad_scales[j][32 * q + ROW0[j]:32 * q + ROW0[j] + 4, 0:T].bitcast(I32), rows)

        def load_wk_plane():
            rows = wk_scales.rearrange("e s (q r) c -> r q (e s) c", r=4)
            for r in range(4):
                nc.gpsimd.dma_start(wk_plane[r:P:32, :, :].bitcast(I32), rows[r].bitcast(I32))

        def load_wv_plane():
            rows = wv_scales.rearrange("e s (q r) c -> q (e s) r c", r=4)
            for q in range(4):
                nc.sync.dma_start(wv_plane[32 * q:32 * q + 4 * E, :].bitcast(I32), rows[q].bitcast(I32))

        def load_wq(e):
            nc.sync.dma_start(raw[e][:], wq[e].rearrange("(p j) c -> p j c", j=4))

        def load_wk(pair):
            words = wk_words.rearrange("e s p b -> p (e s) b")[:, 2 * pair:2 * pair + 2, :]
            nc.sync.dma_start(wk_pairs[pair][:].bitcast(I32), words.bitcast(I32))

        def load_wv(dst, e0, b0, b1):
            words = wv_words.rearrange("e s p c d -> p (e s) (c d)")[:, e0:e0 + 2, b0:b1]
            nc.sync.dma_start(dst[:].bitcast(I32), words.bitcast(I32))

        nc.gpsimd.memset(gate_rows[:], 0.0)
        for j in (KP, QP, VP):
            nc.gpsimd.memset(grad_scales[j][:, 0:T].bitcast(I32), 0)
        make_identity(nc, ident[:])
        load_wk_plane()
        load_grad_words(QP)
        nc.sync.dma_start(offs_t[:], offs)
        nc.sync.dma_start(gate_rows[0:2 * E, :], gate[0].rearrange("(s p) -> s p", p=P))
        load_grad_words(KP)
        load_grad_words(VP)
        load_wk(0)
        load_wq(0)
        load_grad_scales(KP, 0, 4)
        load_grad_scales(QP, 0, 2)
        load_wq(1)
        load_grad_scales(QP, 2, 4)
        load_grad_scales(VP, 0, 4)
        load_wq(2)
        load_wv_plane()
        load_wv(wv_early, 0, 0, 4 * K)
        load_wk(1)
        load_wq(3)
        load_wv(wv_late[0], 2, 0, 2 * K)
        nc.sync.dma_start(pos_t[0][:], pos1)
        load_wv(wv_late[1], 2, 2 * K, 4 * K)
        nc.sync.dma_start(pos_t[1][:], pos2)

        def gather_words(j):
            count = S - C if j == VP else S
            nc.vector.tensor_copy(slot_words[j][:], grad_words[j][:].indirect(offs_t[:, 0:count // 16]))

        def gather_scales(j, u0, u1):
            half = u0 // H
            nc.vector.tensor_copy(slot_scales[j][half][:, u0 - half * H:u1 - half * H],
                                  grad_scales[j][:].indirect(offs_t[:, u0 // 16:u1 // 16]))

        def cast(e):
            nc.scalar.copy(rounded[e][:].rearrange("p (c i) j -> p c j i", i=4),
                           raw[e][:].rearrange("p j (c i) -> p c j i", i=4))

        def cast_late(e, h):
            dst = rounded_late[2 * (e - 2) + h][:]
            src = raw[e][:, :, h * K // 2:(h + 1) * K // 2]
            if h == e - 2:
                nc.gpsimd.tensor_scalar(dst, src.rearrange("p j c -> p c j"), 1.0, 0.0, MULT, ADD)
            else:
                nc.scalar.copy(dst.rearrange("p (c i) j -> p c j i", i=4), src.rearrange("p j (c i) -> p c j i", i=4))

        def quantize(codes, plane, values):
            nc.vector.quantize_mx(out=codes[:].bitcast(FP8X4), scales=plane[:], in_=values)

        def quantize_early(e):
            quantize(wq_codes[e], wq_plane[e], rounded[e][:].rearrange("p c j -> p (c j)"))

        def quantize_late(i):
            quantize(late_codes[i], late_plane[i], rounded_late[i][:].rearrange("p c j -> p (c j)"))

        def weights(j, e, c0, c1):
            if j == QP and e < 2:
                return wq_codes[e][:, c0:c1].bitcast(FP8X4), wq_plane[e][:, c0:c1]
            if j == QP:
                h, q0 = divmod(c0, K // 2)
                i, cols = 2 * (e - 2) + h, slice(q0, q0 + c1 - c0)
                return late_codes[i][:, cols].bitcast(FP8X4), late_plane[i][:, cols]
            if j == KP:
                return wk_pairs[e // 2][:, e % 2, 2 * c0:2 * c1].bitcast(FP4X4), wk_plane[:, e, c0:c1]
            h, v0 = divmod(c0, K // 2)
            codes = wv_early[:, e, c0:c1] if e < 2 else wv_late[h][:, e - 2, v0:v0 + c1 - c0]
            return codes.bitcast(FP8X4), wv_plane[4 * e:P, c0:c1]

        def slots(j, u0, u1):
            half = u0 // H
            words = last_words[:] if j == VP and u0 == S - C else slot_words[j][:, u0:u1]
            return words.bitcast(FP8X4), slot_scales[j][half][ROW0[j]:P, u0 - half * H:u1 - half * H]

        def mx(acc, stationary, moving, start, stop):
            nc.tensor.matmul_mx(out=acc, lhsT=stationary[0], lhsT_scale=stationary[1], rhs=moving[0],
                                rhs_scale=moving[1], start=start, stop=stop)

        def gated_copy(dst, src, s):
            nc.scalar.activation(dst, src, COPY, scale=gate_col[:, s:s + 1])

        def turn(ct, half, blocks, n):
            turned = bank(n)
            for i, block in enumerate(blocks):
                nc.tensor.transpose(turned[:, i * P:(i + 1) * P], block, ident[:])
            nc.scalar.copy(dx[ct][:, half * H:(half + 1) * H], turned[:])

        def late_passes(ct, j, experts=(2, 3)):
            for e in experts:
                mx(late_sums[ct][:, (e - 2) * C:(e - 1) * C], weights(j, e, ct * P, (ct + 1) * P),
                   slots(j, e * C, (e + 1) * C), j == KP and e == 2, j == QP and e == 3)

        def fetch(dst, ct, choice, t0, t1):
            nc.scalar.activation(dst, dx[ct][:].indirect(pos_t[choice][:, t0 // 16:t1 // 16]), COPY)

        def fetch_add(ct, t0, t1):
            nc.vector.tensor_tensor(res[ct][:, t0:t1], dx[ct][:].indirect(pos_t[1][:, t0 // 16:t1 // 16]),
                                    first[ct][:, t0:t1], ADD)
            nc.sync.dma_start(out[ct * P:(ct + 1) * P, t0:t1], res[ct][:, t0:t1])

        gate_bank = bank(4)
        nc.tensor.transpose(gate_bank[:, 0:P], gate_rows[:], ident[:])
        nc.scalar.copy(gate_spread[:], gate_bank[:, 4:8])
        nc.scalar.copy(gate_col[:], gate_bank[:, 0:4])
        spread = bank(5)
        for i in range(4):
            nc.tensor.transpose(spread[:, i * P:(i + 1) * P], gate_spread[:, i:i + 1].to_broadcast([P, P]), ident[:])
        nc.scalar.copy(gate_tail[:], spread[:])

        for j in (QP, KP, VP):
            gather_words(j)
        cast(0)
        cast(1)
        for e in (2, 3):
            for h in range(2):
                cast_late(e, h)
        gather_scales(KP, 0, H)
        quantize_early(0)
        gather_scales(QP, 0, H)
        for e in range(2):
            gather_scales(VP, e * C, (e + 1) * C)
        quantize_early(1)
        sums = [bank(s) for s in range(4)]
        for s0, projections in ((0, (KP,)), (2, (KP,)), (0, (QP, VP)), (2, (VP, QP))):
            for j in projections:
                for s in (s0, s0 + 1):
                    mx(sums[s][:], slots(j, s * P, (s + 1) * P), weights(j, s // 2, 0, K), j == KP,
                       j == (VP if s0 == 0 else QP))
        for s in range(4):
            gated_copy(early[s][:], sums[s][:], s)
        for ct in range(CT):
            turn(ct, 0, [early[s][:, ct * P:(ct + 1) * P] for s in range(4)], 4 + ct)

        gather_scales(KP, H, S)
        nc.vector.tensor_copy(last_words[:], grad_words[VP][:].indirect(offs_t[:, (S - C) // 16:S // 16]))
        for j in (VP, QP):
            gather_scales(j, H, S)
        late_sums = [bank(ct) for ct in range(CT)]
        for ct in range(CT):
            quantize_late(ct)
        for ct in range(CT):
            late_passes(ct, KP)
        for ct in range(CT):
            late_passes(ct, QP, (2,))
            late_passes(ct, VP)
            late_passes(ct, QP, (3,))
        for ct in range(CT):
            nc.vector.tensor_tensor(dx[ct][:, H:S], late_sums[ct][:], gate_tail[:], MULT)

        shared, last = CT - 2, CT - 1
        parts = ((0, T // 2), (T // 2, 3 * T // 4), (3 * T // 4, T))
        for ct in range(shared):
            fetch(first[ct][:], ct, 0, 0, T)
        fetch(first[shared][:], shared, 0, 0, T)
        fetch(second[:], shared, 1, SPLIT, T)
        for t0, t1 in parts:
            fetch(first[last][:, t0:t1], last, 0, t0, t1)
        for ct in range(shared):
            fetch_add(ct, 0, T)
        fetch_add(shared, 0, SPLIT)
        nc.vector.tensor_tensor(res[shared][:, SPLIT:T], first[shared][:, SPLIT:T], second[:], ADD)
        nc.sync.dma_start(out[shared * P:last * P, SPLIT:T], res[shared][:, SPLIT:T])
        for t0, t1 in parts:
            fetch_add(last, t0, t1)
